import numpy as np
import ml_dtypes


def mxq(x, axis, fmt="e4m3"):
    dtype, down = {"e4m3": (ml_dtypes.float8_e4m3fn, 7), "e5m2": (ml_dtypes.float8_e5m2, 14)}[fmt]
    v = np.moveaxis(np.asarray(x, np.float32).astype(ml_dtypes.bfloat16).astype(np.float64), axis, -1)
    blocks = v.reshape(v.shape[:-1] + (-1, 32))
    amax = np.abs(blocks).max(-1, keepdims=True)
    byte = np.maximum(np.where(amax > 0, np.frexp(amax)[1] - 1 + 127, 0) - down, 1)
    scale = np.exp2(byte - 127.0)
    codes = (blocks / scale).astype(np.float32).astype(dtype).astype(np.float64)
    return np.moveaxis((codes * scale).reshape(v.shape), -1, axis)


WIDE = False


def mx_kscale(k):
    if not WIDE:
        return np.ones(k)
    levels = np.array([24, -24, 12, -12, 0])
    if k % 512:
        return np.exp2(np.random.permutation(np.resize(levels, k // 32))).repeat(32)
    a = np.empty((k // 512, 16))
    for p in range(k // 512):
        a[p, :8] = np.random.permutation(np.resize(levels, 8))
        for g in range(8):
            far = levels[np.abs(levels - a[p, g]) >= 10]
            a[p, g + 8] = far[np.random.randint(len(far))]
    return np.exp2(a.ravel()).repeat(32)


def f64(x):
    return np.asarray(x).astype(np.float64)


def striped(idx):
    return np.tile(idx.reshape(-1, 16).T, (8, 1)).astype(np.uint16)


def unstriped(offs):
    return offs[:16].T.reshape(-1).astype(np.int64)


E2M1 = np.array([0.0, 0.5, 1.0, 1.5, 2.0, 3.0, 4.0, 6.0, -0.0, -0.5, -1.0, -1.5, -2.0, -3.0, -4.0, -6.0])


def pack_weight(w, fmt):
    k, n = w.shape
    w = f64(np.asarray(w, np.float32).astype(ml_dtypes.bfloat16)).reshape(k // 32, 32, n)
    amax = np.abs(w).max(1)
    if fmt == "e4m3":
        byte = np.frexp(amax)[1] - 1 + 127 - 7
    else:
        mant, ex = np.frexp(amax / 6.0)
        byte = np.where(mant > 0.5, ex, ex - 1) + 127
    byte = np.clip(np.where(amax > 0, byte, 1), 1, 254)
    scaled = (w * np.exp2(127.0 - byte)[:, None, :]).reshape(k, n).astype(np.float32)
    by_word = np.ascontiguousarray(scaled.reshape(k // 512, 128, 4, n).transpose(0, 1, 3, 2))
    if fmt == "e4m3":
        words = by_word.astype(ml_dtypes.float8_e4m3fn).view(np.uint8)
    else:
        c = by_word.astype(ml_dtypes.float4_e2m1fn).view(np.uint8) & 0xF
        words = (c[..., 0::2] | (c[..., 1::2] << 4)).reshape(k // 512, 128, 2 * n)
    return np.ascontiguousarray(words), np.ascontiguousarray(byte.astype(np.uint8).reshape(k // 512, 16, n))


def unpack_weight(words, scales, fmt):
    g, _, n = scales.shape
    words = np.ascontiguousarray(words).reshape(g, 128, n, -1)
    if fmt == "e4m3":
        vals = words.view(ml_dtypes.float8_e4m3fn).astype(np.float64)
    else:
        nib = np.empty((g, 128, n, 4), np.uint8)
        nib[..., 0::2] = words & 0xF
        nib[..., 1::2] = words >> 4
        vals = E2M1[nib]
    vals = vals * np.repeat(np.exp2(scales.astype(np.float64) - 127.0), 8, axis=1)[..., None]
    return vals.transpose(0, 1, 3, 2).reshape(g * 512, n)


def pack_table4(v):
    words, scales = pack_weight(v, "e2m1")
    g, t = words.shape[0] // 2, v.shape[1]
    return np.ascontiguousarray(words.reshape(g, 2, 128, t, 2).transpose(0, 2, 3, 1, 4).reshape(g, 128, t, 4)), scales


def unpack_table4(words, scales):
    g, _, t, _ = words.shape
    return unpack_weight(words.reshape(g, 128, t, 2, 2).transpose(0, 3, 1, 2, 4).reshape(2 * g, 128, 2 * t), scales, "e2m1")


K, R, N, T, J = 1024, 1024, 256, 4096, 2048


def setup_inputs():
    n = np.random.standard_normal
    s = mx_kscale(K)[:, None]
    u = mx_kscale(R)[:, None]
    p_tab = pack_table4(n((K, T)) * s)
    p_wg = pack_weight(n((K, R)) / np.sqrt(K) / s, "e4m3")
    p_wu = pack_weight(n((K, R)) / np.sqrt(K) / s * u.T, "e2m1")
    return {
        "tab_words": p_tab[0],
        "tab_scales": p_tab[1],
        "wg_words": p_wg[0],
        "wg_scales": p_wg[1],
        "wu_words": p_wu[0],
        "wu_scales": p_wu[1],
        "wd": (n((R, N)) / np.sqrt(R) / u).astype(np.float32),
        "rT": (n((N, T))).astype(np.float32),
        "offs": striped(np.random.permutation(T)[:J]),
    }


def reference(tab_words, tab_scales, wg_words, wg_scales, wu_words, wu_scales, wd, rT, offs):
    idx = unstriped(offs)
    tab_ = unpack_table4(tab_words, tab_scales)[:, idx]
    wg_ = unpack_weight(wg_words, wg_scales, "e4m3")
    wu_ = unpack_weight(wu_words, wu_scales, "e2m1")
    ga = wg_.T @ tab_
    ub = wu_.T @ tab_
    h = np.maximum(ga, 0.0) * ub
    h_ = mxq(h, 0, "e4m3")
    wd_ = mxq(f64(wd), 0, "e4m3")
    y = wd_.T @ h_
    return y + f64(rT)[:, idx]

@@ -1,0 +1,271 @@
+from contextlib import ExitStack
+
+import concourse.mybir as mybir
+
+K, R, N, T, J = 1024, 1024, 256, 4096, 2048
+FLOPS = 2 * J * (2 * K * R + R * N)
+
+F32 = mybir.dt.float32
+BF16 = mybir.dt.bfloat16
+I32 = mybir.dt.int32
+U32 = mybir.dt.uint32
+U16 = mybir.dt.uint16
+U8 = mybir.dt.uint8
+FP8X4 = mybir.dt.float8_e4m3fn_x4
+FP4X4 = mybir.dt.float4_e2m1fn_x4
+MULT = mybir.AluOpType.mult
+ADD = mybir.AluOpType.add
+RELU = mybir.ActivationFunctionType.Relu
+
+P = 128
+CH = 512
+CHUNKS = J // CH
+SUB = 128
+HALVES = R // 512
+STEPS = CHUNKS * HALVES
+
+
+def tile_list_gmlpt_relu_resL_kernel(
+    tc, tab_words, tab_scales, wg_words, wg_scales, wu_words, wu_scales, wd, rT, offs, out
+):
+    nc = tc.nc
+    with ExitStack() as ctx:
+        lists = ctx.enter_context(tc.tile_pool(name="lists", bufs=1))
+        keep = ctx.enter_context(tc.tile_pool(name="keep", bufs=1))
+        ring = ctx.enter_context(tc.tile_pool(name="ring", bufs=3))
+        ps_g = ctx.enter_context(tc.psum_pool(name="ps_g", bufs=3))
+        ps_u = ctx.enter_context(tc.psum_pool(name="ps_u", bufs=3))
+        ps_y = ctx.enter_context(tc.psum_pool(name="ps_y", bufs=2))
+
+        offsets = lists.tile([P, J // 16], U16, name="offsets")
+        nc.sync.dma_start(offsets[:], offs)
+
+        def piece(c):
+            return offsets[:, c * CH // 16 : (c + 1) * CH // 16]
+
+        WS = 2 * 2 * R // 4
+        scale_win = keep.tile([P, T // 4], I32, name="scale_win", align_bytes=64)
+        nc.vector.memset(scale_win[:, 0 : T // 8], 0)
+        nc.gpsimd.memset(scale_win[:, T // 8 :], 0)
+        wsc_raw = keep.tile([P, 2, 2, R // 4], I32, name="wsc_raw", tag="slot_d", align_bytes=64)
+        nc.vector.memset(wsc_raw[:], 0)
+        planes = keep.tile([P, WS + J // 4], I32, name="planes", align_bytes=64)
+        nc.vector.memset(planes[:], 0)
+
+        wg_raw, wu_raw = [], []
+        for a in range(HALVES):
+            wg_raw.append(keep.tile([P, 2, 512], I32, name="wg_raw%d" % a, align_bytes=64))
+            wu_raw.append(keep.tile([P, 2, 256], I32, name="wu_raw%d" % a, align_bytes=64))
+
+        def load_wg(a):
+            nc.sync.dma_start(
+                wg_raw[a][:],
+                wg_words[:, :, 512 * a : 512 * (a + 1), :].rearrange("k p r i -> p k (r i)").bitcast(I32),
+            )
+
+        def load_wu(a):
+            nc.sync.dma_start(
+                wu_raw[a][:],
+                wu_words[:, :, 1024 * a : 1024 * (a + 1)].rearrange("k p c -> p k c").bitcast(I32),
+            )
+
+        load_wu(0)
+        nc.sync.dma_start(scale_win[4:P:8, :], tab_scales[1].bitcast(I32))
+        for q in range(4):
+            nc.sync.dma_start(scale_win[32 * q : 32 * q + 4, :], tab_scales[0, 4 * q : 4 * q + 4, :].bitcast(I32))
+        for w, w_scales in enumerate((wg_scales, wu_scales)):
+            nc.sync.dma_start(wsc_raw[4:P:8, w, :, :], w_scales.rearrange("k q c -> q k c").bitcast(I32))
+        word_win = keep.tile([P, T], I32, name="word_win", align_bytes=64)
+        nc.sync.dma_start(word_win[:], tab_words[0].rearrange("p t b -> p (t b)").bitcast(I32))
+        load_wg(0)
+        load_wg(1)
+        load_wu(1)
+        wd_raw = keep.tile([P, HALVES, 4, N], F32, name="wd_raw", align_bytes=64)
+        wd_rows = wd.rearrange("(a b t q) n -> a t b q n", a=HALVES, t=4, q=8)
+        for a in range(HALVES):
+            for t in range(4):
+                nc.sync.dma_start(wd_raw[:, a, t, :], wd_rows[a, t])
+        r_win = keep.tile([P, N // P, T], F32, name="r_win", align_bytes=64)
+        for m in range(N // P):
+            nc.sync.dma_start(r_win[:, m, :], rT[m * P : (m + 1) * P, :])
+
+        picked = [keep.tile([P, CH], U8, name="picked0", align_bytes=64)]
+        staged = keep.tile([P, WS + CH // 4], I32, name="staged", align_bytes=64)
+
+        def picked_cols(c, lo, hi):
+            if c == 0:
+                return picked[0][:, lo:hi]
+            return picked[1][:, (c - 1) * CH + lo : (c - 1) * CH + hi]
+
+        def gather_scales(c):
+            nc.vector.tensor_copy(picked_cols(c, 0, CH), scale_win[:].bitcast(U8).indirect(piece(c)))
+
+        def tab_plane(c, k, lo, hi):
+            if k == 0:
+                return picked_cols(c, lo, hi)
+            return planes[:, WS:].bitcast(U8)[:, c * CH + lo : c * CH + hi]
+
+        def w_plane(w, k, a, t):
+            at = (((w * 2 + k) * HALVES + a) * 4 + t) * 32
+            return planes[:, at : at + 32].bitcast(U8)
+
+        tab = {}
+
+        def gather_words(c):
+            both = ring.tile([P, CH], U32, name="both", align_bytes=64, bufs=1)
+            nc.vector.tensor_copy(both[:], word_win[:].bitcast(U32).indirect(piece(c)))
+            parted = ring.tile([P, 2, 2 * CH], U8, name="parted", align_bytes=64, bufs=2)
+            nc.vector.tensor_copy(
+                parted[:].bitcast(U16), both[:].bitcast(U16).rearrange("p (j d) -> p d j", d=2)
+            )
+            tab[c] = parted
+
+        wg_s, wu_s = {}, {}
+
+        def sort_words(a):
+            for store, name, e, raw in ((wg_s, "wg_s", 8, wg_raw), (wu_s, "wu_s", 4, wu_raw)):
+                dst = keep.tile([P, 4, 2, 16 * e], I32, name="%s%d" % (name, a), align_bytes=64)
+                nc.vector.tensor_copy(
+                    dst[:].rearrange("p t k (b e) -> p t (k b) e", e=e),
+                    raw[a][:].rearrange("p k (b t e) -> p t (k b) e", t=4, e=e),
+                )
+                store[a] = dst
+
+        gather_scales(0)
+        nc.vector.tensor_copy(staged[:, WS:], picked[0][:].bitcast(I32))
+        nc.vector.tensor_copy(
+            staged[:, 0:WS].rearrange("p (g t b e) -> p g t b e", t=4, b=16, e=2),
+            wsc_raw[:].rearrange("p w k (a b t e) -> p (w k a) t b e", a=HALVES, t=4, e=2),
+        )
+        for q in range(4):
+            nc.scalar.dma_start(planes[32 * q : 32 * q + 4, 0 : WS + CH // 4], staged[32 * q + 4 : 32 * q + 32 : 8, :])
+        gather_words(0)
+        sort_words(0)
+        picked.append(keep.tile([P, J - CH], U8, name="picked1", tag="slot_d", align_bytes=64))
+        for c in range(1, CHUNKS):
+            gather_scales(c)
+        for q in range(4):
+            nc.scalar.dma_start(
+                planes[32 * q : 32 * q + 4, WS + CH // 4 :],
+                picked[1][32 * q + 4 : 32 * q + 32 : 8, :].bitcast(I32),
+            )
+
+
+        relu_g, hid, hq, ys, res = {}, {}, {}, {}, {}
+
+        def gate(n, t):
+            c, a = divmod(n, HALVES)
+            if t == 0:
+                relu_g[n] = ring.tile([P, CH // 4, 4, 4], F32, name="relu_g")
+            bank = ps_g.tile([P, CH], F32, name="bank_g")
+            for k in range(2):
+                nc.tensor.matmul_mx(
+                    out=bank[:],
+                    lhsT=wg_s[a][:, t, k, :].bitcast(FP8X4),
+                    lhsT_scale=w_plane(0, k, a, t),
+                    rhs=tab[c][:, k, :].bitcast(FP4X4),
+                    rhs_scale=tab_plane(c, k, 0, CH),
+                    start=(k == 0),
+                    stop=(k == 1),
+                )
+            nc.scalar.activation(relu_g[n][:, :, t, :], bank[:].rearrange("p (c i) -> p c i", i=4), RELU)
+
+        def up(n, s):
+            c, a = divmod(n, HALVES)
+            if s == 0:
+                hid[n] = ring.tile([P, CH, 4], BF16, name="hid", align_bytes=64)
+            bank = ps_u.tile([P, 4, SUB], F32, name="bank_u")
+            for t in range(4):
+                for k in range(2):
+                    nc.tensor.matmul_mx(
+                        out=bank[:, t, :],
+                        lhsT=wu_s[a][:, t, k, :].bitcast(FP4X4),
+                        lhsT_scale=w_plane(1, k, a, t),
+                        rhs=tab[c][:, k, 2 * SUB * s : 2 * SUB * (s + 1)].bitcast(FP4X4),
+                        rhs_scale=tab_plane(c, k, SUB * s, SUB * (s + 1)),
+                        start=(k == 0),
+                        stop=(k == 1),
+                    )
+            nc.vector.tensor_tensor(
+                hid[n][:, SUB * s : SUB * (s + 1), :].rearrange("p (c i) t -> p c t i", i=4),
+                bank[:].rearrange("p t (c i) -> p c t i", i=4),
+                relu_g[n][:, SUB // 4 * s : SUB // 4 * (s + 1), :, :],
+                MULT,
+            )
+
+        wd_codes = keep.tile([P, HALVES, N], U32, name="wd_codes", align_bytes=64)
+        wd_scales = keep.tile([P, HALVES, N], U8, name="wd_scales", align_bytes=64)
+
+        def quantise_wd():
+            wd_bf = keep.tile([P, HALVES, N, 4], BF16, name="wd_bf", align_bytes=64)
+            for a in range(HALVES):
+                nc.scalar.copy(
+                    wd_bf[:, a].rearrange("p (c i) t -> p c t i", i=4),
+                    wd_raw[:, a].rearrange("p t (c i) -> p c t i", i=4),
+                )
+            nc.vector.quantize_mx(
+                out=wd_codes[:].rearrange("p a n -> p (a n)").bitcast(FP8X4),
+                scales=wd_scales[:].rearrange("p a n -> p (a n)"),
+                in_=wd_bf[:].rearrange("p a n t -> p (a n t)"),
+            )
+
+        def quantise(n):
+            codes = ring.tile([P, CH], U32, name="h_codes", align_bytes=64)
+            scales = ring.tile([P, CH], U8, name="h_scales", align_bytes=64)
+            nc.vector.quantize_mx(
+                out=codes[:].bitcast(FP8X4), scales=scales[:], in_=hid[n][:].rearrange("p j t -> p (j t)")
+            )
+            hq[n] = (codes, scales)
+
+        def down(n):
+            c, a = divmod(n, HALVES)
+            codes, scales = hq[n]
+            for m in range(N // P):
+                if a == 0:
+                    ys[c, m] = ps_y.tile([P, CH], F32, name="bank_y")
+                nc.tensor.matmul_mx(
+                    out=ys[c, m][:],
+                    lhsT=wd_codes[:, a, m * P : (m + 1) * P].bitcast(FP8X4),
+                    lhsT_scale=wd_scales[:, a, m * P : (m + 1) * P],
+                    rhs=codes[:].bitcast(FP8X4),
+                    rhs_scale=scales[:],
+                    start=(a == 0),
+                    stop=(a == HALVES - 1),
+                )
+
+        def gather_res(c, m):
+            res[c, m] = ring.tile([P, CH], F32, name="res", bufs=2)
+            nc.vector.tensor_copy(res[c, m][:], r_win[:, m, :].indirect(piece(c)))
+
+        def finish(c, m):
+            o = ring.tile([P, CH], F32, name="o", bufs=4)
+            nc.vector.tensor_tensor(o[:], ys[c, m][:], res[c, m][:], ADD)
+            nc.sync.dma_start(out[m * P : (m + 1) * P, c * CH : (c + 1) * CH], o[:])
+
+        for t in range(4):
+            gate(0, t)
+        sort_words(1)
+        for n in range(STEPS):
+            c, a = divmod(n, HALVES)
+            for i in range(4):
+                if n + 1 < STEPS:
+                    gate(n + 1, i)
+                up(n, i)
+                if i == 0 and n == 1:
+                    quantise_wd()
+                if i == 0 and n > 0:
+                    quantise(n - 1)
+                if i == 2 and n > 0:
+                    down(n - 1)
+                if a == 0 and i == 1 and c + 1 < CHUNKS:
+                    gather_words(c + 1)
+                if a == 0 and i == 3 and n > 0:
+                    finish(c - 1, 0)
+                if a == 1 and i == 0 and n > 1:
+                    finish(c - 1, 1)
+                if a == 1 and i in (1, 2):
+                    gather_res(c, i - 1)
+        quantise(STEPS - 1)
+        down(STEPS - 1)
+        for m in range(N // P):
+            finish(CHUNKS - 1, m)

@@ -34,8 +34,7 @@ def tile_list_gmlpt_relu_resL_kernel(
         keep = ctx.enter_context(tc.tile_pool(name="keep", bufs=1))
         ring = ctx.enter_context(tc.tile_pool(name="ring", bufs=3))
         ps_g = ctx.enter_context(tc.psum_pool(name="ps_g", bufs=3))
-        ps_u = ctx.enter_context(tc.psum_pool(name="ps_u", bufs=3))
-        ps_y = ctx.enter_context(tc.psum_pool(name="ps_y", bufs=2))
+        ps_u = ctx.enter_context(tc.psum_pool(name="ps_u", bufs=5))
 
         offsets = lists.tile([P, J // 16], U16, name="offsets")
         nc.sync.dma_start(offsets[:], offs)
@@ -51,6 +50,9 @@ def tile_list_gmlpt_relu_resL_kernel(
         nc.vector.memset(wsc_raw[:], 0)
         planes = keep.tile([P, WS + J // 4], I32, name="planes", align_bytes=64)
         nc.vector.memset(planes[:], 0)
+        warm = keep.tile([P, 2, 8], F32, name="warm")
+        nc.gpsimd.memset(warm[:, 0, :], 0.0)
+        nc.scalar.activation(warm[:, 1, :], warm[:, 0, :], RELU)
 
         wg_raw, wu_raw = [], []
         for a in range(HALVES):
@@ -80,14 +82,6 @@ def tile_list_gmlpt_relu_resL_kernel(
         load_wg(0)
         load_wg(1)
         load_wu(1)
-        wd_raw = keep.tile([P, HALVES, 4, N], F32, name="wd_raw", align_bytes=64)
-        wd_rows = wd.rearrange("(a b t q) n -> a t b q n", a=HALVES, t=4, q=8)
-        for a in range(HALVES):
-            for t in range(4):
-                nc.sync.dma_start(wd_raw[:, a, t, :], wd_rows[a, t])
-        r_win = keep.tile([P, N // P, T], F32, name="r_win", align_bytes=64)
-        for m in range(N // P):
-            nc.sync.dma_start(r_win[:, m, :], rT[m * P : (m + 1) * P, :])
 
         picked = [keep.tile([P, CH], U8, name="picked0", align_bytes=64)]
         staged = keep.tile([P, WS + CH // 4], I32, name="staged", align_bytes=64)
@@ -145,13 +139,22 @@ def tile_list_gmlpt_relu_resL_kernel(
         for c in range(1, CHUNKS):
             gather_scales(c)
         for q in range(4):
-            nc.scalar.dma_start(
+            nc.sync.dma_start(
                 planes[32 * q : 32 * q + 4, WS + CH // 4 :],
                 picked[1][32 * q + 4 : 32 * q + 32 : 8, :].bitcast(I32),
             )
 
 
-        relu_g, hid, hq, ys, res = {}, {}, {}, {}, {}
+        wd_raw = keep.tile([P, HALVES, 4, N], F32, name="wd_raw", align_bytes=64)
+        wd_rows = wd.rearrange("(a b t q) n -> a t b q n", a=HALVES, t=4, q=8)
+        for a in range(HALVES):
+            for t in range(4):
+                nc.sync.dma_start(wd_raw[:, a, t, :], wd_rows[a, t])
+        r_win = keep.tile([P, N // P, T], F32, name="r_win", align_bytes=64)
+        for m in range(N // P):
+            nc.sync.dma_start(r_win[:, m, :], rT[m * P : (m + 1) * P, :])
+
+        relu_g, hid, hq, res = {}, {}, {}, {}
 
         def gate(n, t):
             c, a = divmod(n, HALVES)
@@ -209,38 +212,56 @@ def tile_list_gmlpt_relu_resL_kernel(
                 in_=wd_bf[:].rearrange("p a n t -> p (a n t)"),
             )
 
-        def quantise(n):
-            codes = ring.tile([P, CH], U32, name="h_codes", align_bytes=64)
-            scales = ring.tile([P, CH], U8, name="h_scales", align_bytes=64)
-            nc.vector.quantize_mx(
-                out=codes[:].bitcast(FP8X4), scales=scales[:], in_=hid[n][:].rearrange("p j t -> p (j t)")
-            )
-            hq[n] = (codes, scales)
-
-        def down(n):
-            c, a = divmod(n, HALVES)
+        def quantise(n, lo, hi):
+            if lo == 0:
+                codes = ring.tile([P, CH], U32, name="h_codes", align_bytes=64)
+                scales = ring.tile([P, CH], U8, name="h_scales", align_bytes=64)
+                hq[n] = (codes, scales)
             codes, scales = hq[n]
-            for m in range(N // P):
-                if a == 0:
-                    ys[c, m] = ps_y.tile([P, CH], F32, name="bank_y")
+            nc.vector.quantize_mx(
+                out=codes[:, lo:hi].bitcast(FP8X4),
+                scales=scales[:, lo:hi],
+                in_=hid[n][:, lo:hi, :].rearrange("p j t -> p (j t)"),
+            )
+
+        def down(c, m, lo, hi, acc):
+            for a in range(HALVES):
+                codes, scales = hq[HALVES * c + a]
                 nc.tensor.matmul_mx(
-                    out=ys[c, m][:],
+                    out=acc,
                     lhsT=wd_codes[:, a, m * P : (m + 1) * P].bitcast(FP8X4),
                     lhsT_scale=wd_scales[:, a, m * P : (m + 1) * P],
-                    rhs=codes[:].bitcast(FP8X4),
-                    rhs_scale=scales[:],
+                    rhs=codes[:, lo:hi].bitcast(FP8X4),
+                    rhs_scale=scales[:, lo:hi],
                     start=(a == 0),
                     stop=(a == HALVES - 1),
                 )
 
         def gather_res(c, m):
-            res[c, m] = ring.tile([P, CH], F32, name="res", bufs=2)
-            nc.vector.tensor_copy(res[c, m][:], r_win[:, m, :].indirect(piece(c)))
+            if m == 0:
+                res[c] = ring.tile([P, N // P, CH], F32, name="res", bufs=2)
+            nc.vector.tensor_copy(res[c][:, m, :], r_win[:, m, :].indirect(piece(c)))
 
         def finish(c, m):
-            o = ring.tile([P, CH], F32, name="o", bufs=4)
-            nc.vector.tensor_tensor(o[:], ys[c, m][:], res[c, m][:], ADD)
+            bank = ps_g.tile([P, CH], F32, name="bank_g")
+            down(c, m, 0, CH, bank[:])
+            y = ring.tile([P, CH], F32, name="y", bufs=2)
+            nc.scalar.copy(y[:], bank[:])
+            o = ring.tile([P, CH], F32, name="o", bufs=2)
+            for lo in (0, CH // 2):
+                nc.gpsimd.tensor_tensor(
+                    o[:, lo : lo + CH // 2], y[:, lo : lo + CH // 2], res[c][:, m, lo : lo + CH // 2], ADD
+                )
             nc.sync.dma_start(out[m * P : (m + 1) * P, c * CH : (c + 1) * CH], o[:])
+
+        def finish_last(c, lo, hi):
+            bank = ps_g.tile([P, CH], F32, name="bank_g")
+            acc = bank[:].rearrange("p (m j) -> p m j", m=N // P)
+            for m in range(N // P):
+                down(c, m, lo, hi, acc[:, m, :])
+            o = ring.tile([P, N // P, hi - lo], F32, name="o_last", bufs=2)
+            nc.vector.tensor_tensor(o[:], acc, res[c][:, :, lo:hi], ADD)
+            nc.sync.dma_start(out.rearrange("(m p) j -> p m j", p=P)[:, :, c * CH + lo : c * CH + hi], o[:])
 
         for t in range(4):
             gate(0, t)
@@ -254,18 +275,15 @@ def tile_list_gmlpt_relu_resL_kernel(
                 if i == 0 and n == 1:
                     quantise_wd()
                 if i == 0 and n > 0:
-                    quantise(n - 1)
-                if i == 2 and n > 0:
-                    down(n - 1)
-                if a == 0 and i == 1 and c + 1 < CHUNKS:
+                    quantise(n - 1, 0, CH)
+                if a == 0 and i == 0 and c + 1 < CHUNKS:
                     gather_words(c + 1)
-                if a == 0 and i == 3 and n > 0:
-                    finish(c - 1, 0)
-                if a == 1 and i == 0 and n > 1:
-                    finish(c - 1, 1)
+                if a == 0 and i in (2, 3) and n > 0:
+                    finish(c - 1, i - 2)
                 if a == 1 and i in (1, 2):
                     gather_res(c, i - 1)
-        quantise(STEPS - 1)
-        down(STEPS - 1)
-        for m in range(N // P):
-            finish(CHUNKS - 1, m)
+                if n == STEPS - 1 and i == 2:
+                    quantise(n, 0, CH // 2)
+        finish_last(CHUNKS - 1, 0, CH // 2)
+        quantise(STEPS - 1, CH // 2, CH)
+        finish_last(CHUNKS - 1, CH // 2, CH)

@@ -18,11 +18,29 @@ ADD = mybir.AluOpType.add
 RELU = mybir.ActivationFunctionType.Relu
 
 P = 128
-CH = 512
-CHUNKS = J // CH
-SUB = 128
-HALVES = R // 512
+PACK = 4
+PASS = P * PACK
+K_PASSES = K // PASS
+HALVES = R // PASS
+RUN = 8
+CHUNK = 512
+CHUNKS = J // CHUNK
+LAST = CHUNKS - 1
+SUB = CHUNK // PACK
 STEPS = CHUNKS * HALVES
+OUT_TILES = N // P
+LINE = 4
+W_SCALE_WORDS = K_PASSES * R // 4
+CHUNK_WORDS = CHUNK // 4
+GATE_BANKS, UP_BANKS = 3, 5
+ALIGN = 64
+
+PACED = [("words", LAST, 0)] + [("res", c, m) for c in range(CHUNKS) for m in range(OUT_TILES)]
+
+
+def paced_tag(job):
+    n, second = divmod(PACED.index(job), 2)
+    return "%s%d" % (("gate", "hid")[second], n)
 
 
 def tile_list_gmlpt_relu_resL_kernel(
@@ -32,179 +50,171 @@ def tile_list_gmlpt_relu_resL_kernel(
     with ExitStack() as ctx:
         lists = ctx.enter_context(tc.tile_pool(name="lists", bufs=1))
         keep = ctx.enter_context(tc.tile_pool(name="keep", bufs=1))
-        ring = ctx.enter_context(tc.tile_pool(name="ring", bufs=3))
-        ps_g = ctx.enter_context(tc.psum_pool(name="ps_g", bufs=3))
-        ps_u = ctx.enter_context(tc.psum_pool(name="ps_u", bufs=5))
+        ring = ctx.enter_context(tc.tile_pool(name="ring", bufs=2))
+        ps_gate = ctx.enter_context(tc.psum_pool(name="ps_gate", bufs=GATE_BANKS))
+        ps_up = ctx.enter_context(tc.psum_pool(name="ps_up", bufs=UP_BANKS))
+
+        def held(shape, dtype, name, tag=None):
+            return keep.tile(shape, dtype, name=name, tag=tag or name, align_bytes=ALIGN)
 
         offsets = lists.tile([P, J // 16], U16, name="offsets")
         nc.sync.dma_start(offsets[:], offs)
 
-        def piece(c):
-            return offsets[:, c * CH // 16 : (c + 1) * CH // 16]
+        def entries(c):
+            return offsets[:, c * CHUNK // 16 : (c + 1) * CHUNK // 16]
 
-        WS = 2 * 2 * R // 4
-        scale_win = keep.tile([P, T // 4], I32, name="scale_win", align_bytes=64)
+        scale_win = held([P, T // 4], I32, "scale_win")
         nc.vector.memset(scale_win[:, 0 : T // 8], 0)
         nc.gpsimd.memset(scale_win[:, T // 8 :], 0)
-        wsc_raw = keep.tile([P, 2, 2, R // 4], I32, name="wsc_raw", tag="slot_d", align_bytes=64)
-        nc.vector.memset(wsc_raw[:], 0)
-        planes = keep.tile([P, WS + J // 4], I32, name="planes", align_bytes=64)
+        w_scale_raw = held([P, K_PASSES, R // 4], I32, "w_scale_raw")
+        nc.vector.memset(w_scale_raw[:], 0)
+        planes = held([P, 2, W_SCALE_WORDS + J // 4], I32, "planes")
         nc.vector.memset(planes[:], 0)
         warm = keep.tile([P, 2, 8], F32, name="warm")
         nc.gpsimd.memset(warm[:, 0, :], 0.0)
         nc.scalar.activation(warm[:, 1, :], warm[:, 0, :], RELU)
 
-        wg_raw, wu_raw = [], []
-        for a in range(HALVES):
-            wg_raw.append(keep.tile([P, 2, 512], I32, name="wg_raw%d" % a, align_bytes=64))
-            wu_raw.append(keep.tile([P, 2, 256], I32, name="wu_raw%d" % a, align_bytes=64))
+        wg_raw = [held([P, K_PASSES, PASS], I32, "wg_raw%d" % a) for a in range(HALVES)]
+        wu_raw = [held([P, K_PASSES, PASS // 2], I32, "wu_raw%d" % a) for a in range(HALVES)]
+        wd_raw = held([P, HALVES, PACK, N], F32, "wd_raw")
+        wd_rows = wd.rearrange("(a b t q) n -> a t b q n", a=HALVES, t=PACK, q=RUN)
+        wd_pieces = [(a, t) for a in range(HALVES) for t in range(PACK)]
+        res_win = held([P, OUT_TILES, T], F32, "res_win")
+        word_win = held([P, T], I32, "word_win")
 
-        def load_wg(a):
+        def load_wd(pieces):
+            for a, t in pieces:
+                nc.sync.dma_start(wd_raw[:, a, t, :], wd_rows[a, t])
+
+        load_wd(wd_pieces[:1])
+        nc.sync.dma_start(scale_win[0:P:4, :], tab_scales.rearrange("a s t -> s a t").bitcast(I32))
+        for x, w_scales in enumerate((wg_scales, wu_scales)):
+            nc.sync.dma_start(w_scale_raw[4 * x : P : 8, :, :], w_scales.rearrange("k s c -> s k c").bitcast(I32))
+        nc.sync.dma_start(word_win[:], tab_words[0].rearrange("p t b -> p (t b)").bitcast(I32))
+        for a in range(HALVES):
             nc.sync.dma_start(
                 wg_raw[a][:],
-                wg_words[:, :, 512 * a : 512 * (a + 1), :].rearrange("k p r i -> p k (r i)").bitcast(I32),
+                wg_words[:, :, PASS * a : PASS * (a + 1), :].rearrange("k p r i -> p k (r i)").bitcast(I32),
             )
-
-        def load_wu(a):
             nc.sync.dma_start(
                 wu_raw[a][:],
-                wu_words[:, :, 1024 * a : 1024 * (a + 1)].rearrange("k p c -> p k c").bitcast(I32),
+                wu_words[:, :, 2 * PASS * a : 2 * PASS * (a + 1)].rearrange("k p c -> p k c").bitcast(I32),
             )
 
-        load_wu(0)
-        nc.sync.dma_start(scale_win[4:P:8, :], tab_scales[1].bitcast(I32))
-        for q in range(4):
-            nc.sync.dma_start(scale_win[32 * q : 32 * q + 4, :], tab_scales[0, 4 * q : 4 * q + 4, :].bitcast(I32))
-        for w, w_scales in enumerate((wg_scales, wu_scales)):
-            nc.sync.dma_start(wsc_raw[4:P:8, w, :, :], w_scales.rearrange("k q c -> q k c").bitcast(I32))
-        word_win = keep.tile([P, T], I32, name="word_win", align_bytes=64)
-        nc.sync.dma_start(word_win[:], tab_words[0].rearrange("p t b -> p (t b)").bitcast(I32))
-        load_wg(0)
-        load_wg(1)
-        load_wu(1)
+        def gather_scales(c, dst):
+            nc.vector.tensor_copy(dst, scale_win[:].bitcast(U8).indirect(entries(c)))
 
-        picked = [keep.tile([P, CH], U8, name="picked0", align_bytes=64)]
-        staged = keep.tile([P, WS + CH // 4], I32, name="staged", align_bytes=64)
+        def move_scales(queue, src, lo, hi):
+            for quad in range(4):
+                queue.dma_start(planes[32 * quad : 32 * quad + 4, :, lo:hi], src[32 * quad : 32 * quad + 32 : 4, :])
 
-        def picked_cols(c, lo, hi):
-            if c == 0:
-                return picked[0][:, lo:hi]
-            return picked[1][:, (c - 1) * CH + lo : (c - 1) * CH + hi]
+        def table_plane(c, kp, lo, hi):
+            return planes[:, kp, W_SCALE_WORDS:].bitcast(U8)[:, c * CHUNK + lo : c * CHUNK + hi]
 
-        def gather_scales(c):
-            nc.vector.tensor_copy(picked_cols(c, 0, CH), scale_win[:].bitcast(U8).indirect(piece(c)))
+        def weight_plane(x, kp, a, t):
+            at = ((kp * HALVES + a) * PACK + t) * (P // 4)
+            return planes[:, x, at : at + P // 4].bitcast(U8)
 
-        def tab_plane(c, k, lo, hi):
-            if k == 0:
-                return picked_cols(c, lo, hi)
-            return planes[:, WS:].bitcast(U8)[:, c * CH + lo : c * CH + hi]
+        table = {}
 
-        def w_plane(w, k, a, t):
-            at = (((w * 2 + k) * HALVES + a) * 4 + t) * 32
-            return planes[:, at : at + 32].bitcast(U8)
-
-        tab = {}
-
-        def gather_words(c):
-            both = ring.tile([P, CH], U32, name="both", align_bytes=64, bufs=1)
-            nc.vector.tensor_copy(both[:], word_win[:].bitcast(U32).indirect(piece(c)))
-            parted = ring.tile([P, 2, 2 * CH], U8, name="parted", align_bytes=64, bufs=2)
+        def gather_words(c, tag):
+            both = held([P, CHUNK], U32, "both%d" % c, tag)
+            nc.vector.tensor_copy(both[:], word_win[:].bitcast(U32).indirect(entries(c)))
+            table[c] = held([P, K_PASSES, 2 * CHUNK], U8, "parted%d" % c)
             nc.vector.tensor_copy(
-                parted[:].bitcast(U16), both[:].bitcast(U16).rearrange("p (j d) -> p d j", d=2)
+                table[c][:].bitcast(U16), both[:].bitcast(U16).rearrange("p (j d) -> p d j", d=K_PASSES)
             )
-            tab[c] = parted
 
-        wg_s, wu_s = {}, {}
+        wg_sorted, wu_sorted = {}, {}
 
         def sort_words(a):
-            for store, name, e, raw in ((wg_s, "wg_s", 8, wg_raw), (wu_s, "wu_s", 4, wu_raw)):
-                dst = keep.tile([P, 4, 2, 16 * e], I32, name="%s%d" % (name, a), align_bytes=64)
+            for name, raw, store, e in (("wg", wg_raw, wg_sorted, RUN), ("wu", wu_raw, wu_sorted, RUN // 2)):
+                store[a] = held([P, PACK, K_PASSES, P // RUN * e], I32, "%s_sorted%d" % (name, a))
                 nc.vector.tensor_copy(
-                    dst[:].rearrange("p t k (b e) -> p t (k b) e", e=e),
-                    raw[a][:].rearrange("p k (b t e) -> p t (k b) e", t=4, e=e),
+                    store[a][:].rearrange("p t k (b e) -> p t (k b) e", e=e),
+                    raw[a][:].rearrange("p k (b t e) -> p t (k b) e", t=PACK, e=e),
                 )
-                store[a] = dst
 
-        gather_scales(0)
-        nc.vector.tensor_copy(staged[:, WS:], picked[0][:].bitcast(I32))
+        picked_first = held([P, CHUNK], U8, "picked_first")
+        staged = held([P, W_SCALE_WORDS + CHUNK_WORDS], I32, "staged")
+        gather_scales(0, picked_first[:])
+        nc.vector.tensor_copy(staged[:, W_SCALE_WORDS:], picked_first[:].bitcast(I32))
         nc.vector.tensor_copy(
-            staged[:, 0:WS].rearrange("p (g t b e) -> p g t b e", t=4, b=16, e=2),
-            wsc_raw[:].rearrange("p w k (a b t e) -> p (w k a) t b e", a=HALVES, t=4, e=2),
+            staged[:, 0:W_SCALE_WORDS].rearrange("p (g t b e) -> p g t b e", t=PACK, b=P // RUN, e=RUN // 4),
+            w_scale_raw[:].rearrange("p k (a b t e) -> p (k a) t b e", a=HALVES, t=PACK, e=RUN // 4),
         )
-        for q in range(4):
-            nc.scalar.dma_start(planes[32 * q : 32 * q + 4, 0 : WS + CH // 4], staged[32 * q + 4 : 32 * q + 32 : 8, :])
-        gather_words(0)
-        sort_words(0)
-        picked.append(keep.tile([P, J - CH], U8, name="picked1", tag="slot_d", align_bytes=64))
-        for c in range(1, CHUNKS):
-            gather_scales(c)
-        for q in range(4):
-            nc.sync.dma_start(
-                planes[32 * q : 32 * q + 4, WS + CH // 4 :],
-                picked[1][32 * q + 4 : 32 * q + 32 : 8, :].bitcast(I32),
+        move_scales(nc.scalar, staged, 0, W_SCALE_WORDS + CHUNK_WORDS)
+        gather_words(0, "both")
+        for a in range(HALVES):
+            sort_words(a)
+        picked_mid = held([P, (LAST - 1) * CHUNK], U8, "picked_mid", "w_scale_raw")
+        for c in range(1, LAST):
+            gather_scales(c, picked_mid[:, (c - 1) * CHUNK : c * CHUNK])
+        move_scales(
+            nc.sync, picked_mid[:].bitcast(I32), W_SCALE_WORDS + CHUNK_WORDS, W_SCALE_WORDS + LAST * CHUNK_WORDS
+        )
+        load_wd(wd_pieces[1:])
+        for m in range(OUT_TILES):
+            nc.sync.dma_start(res_win[:, m, :], rT[m * P : (m + 1) * P, :])
+
+        def last_scales():
+            picked_last = held([P, CHUNK], U8, "picked_last", "wg_raw1")
+            gather_scales(LAST, picked_last[:])
+            move_scales(
+                nc.sync, picked_last[:].bitcast(I32), W_SCALE_WORDS + LAST * CHUNK_WORDS, W_SCALE_WORDS + J // 4
             )
 
-
-        wd_raw = keep.tile([P, HALVES, 4, N], F32, name="wd_raw", align_bytes=64)
-        wd_rows = wd.rearrange("(a b t q) n -> a t b q n", a=HALVES, t=4, q=8)
-        for a in range(HALVES):
-            for t in range(4):
-                nc.sync.dma_start(wd_raw[:, a, t, :], wd_rows[a, t])
-        r_win = keep.tile([P, N // P, T], F32, name="r_win", align_bytes=64)
-        for m in range(N // P):
-            nc.sync.dma_start(r_win[:, m, :], rT[m * P : (m + 1) * P, :])
-
-        relu_g, hid, hq, res = {}, {}, {}, {}
+        relu_g, hid, hid_mx, res = {}, {}, {}, {}
 
         def gate(n, t):
             c, a = divmod(n, HALVES)
             if t == 0:
-                relu_g[n] = ring.tile([P, CH // 4, 4, 4], F32, name="relu_g")
-            bank = ps_g.tile([P, CH], F32, name="bank_g")
-            for k in range(2):
+                relu_g[n] = held([P, CHUNK // LINE, PACK, LINE], F32, "gate%d" % n)
+            bank = ps_gate.tile([P, CHUNK], F32, name="bank_gate")
+            for kp in range(K_PASSES):
                 nc.tensor.matmul_mx(
                     out=bank[:],
-                    lhsT=wg_s[a][:, t, k, :].bitcast(FP8X4),
-                    lhsT_scale=w_plane(0, k, a, t),
-                    rhs=tab[c][:, k, :].bitcast(FP4X4),
-                    rhs_scale=tab_plane(c, k, 0, CH),
-                    start=(k == 0),
-                    stop=(k == 1),
+                    lhsT=wg_sorted[a][:, t, kp, :].bitcast(FP8X4),
+                    lhsT_scale=weight_plane(0, kp, a, t),
+                    rhs=table[c][:, kp, :].bitcast(FP4X4),
+                    rhs_scale=table_plane(c, kp, 0, CHUNK),
+                    start=(kp == 0),
+                    stop=(kp == K_PASSES - 1),
                 )
-            nc.scalar.activation(relu_g[n][:, :, t, :], bank[:].rearrange("p (c i) -> p c i", i=4), RELU)
+            nc.scalar.activation(relu_g[n][:, :, t, :], bank[:].rearrange("p (g i) -> p g i", i=LINE), RELU)
 
         def up(n, s):
             c, a = divmod(n, HALVES)
             if s == 0:
-                hid[n] = ring.tile([P, CH, 4], BF16, name="hid", align_bytes=64)
-            bank = ps_u.tile([P, 4, SUB], F32, name="bank_u")
-            for t in range(4):
-                for k in range(2):
+                hid[n] = held([P, CHUNK, PACK], BF16, "hid%d" % n)
+            bank = ps_up.tile([P, PACK, SUB], F32, name="bank_up")
+            for t in range(PACK):
+                for kp in range(K_PASSES):
                     nc.tensor.matmul_mx(
                         out=bank[:, t, :],
-                        lhsT=wu_s[a][:, t, k, :].bitcast(FP4X4),
-                        lhsT_scale=w_plane(1, k, a, t),
-                        rhs=tab[c][:, k, 2 * SUB * s : 2 * SUB * (s + 1)].bitcast(FP4X4),
-                        rhs_scale=tab_plane(c, k, SUB * s, SUB * (s + 1)),
-                        start=(k == 0),
-                        stop=(k == 1),
+                        lhsT=wu_sorted[a][:, t, kp, :].bitcast(FP4X4),
+                        lhsT_scale=weight_plane(1, kp, a, t),
+                        rhs=table[c][:, kp, 2 * SUB * s : 2 * SUB * (s + 1)].bitcast(FP4X4),
+                        rhs_scale=table_plane(c, kp, SUB * s, SUB * (s + 1)),
+                        start=(kp == 0),
+                        stop=(kp == K_PASSES - 1),
                     )
             nc.vector.tensor_tensor(
-                hid[n][:, SUB * s : SUB * (s + 1), :].rearrange("p (c i) t -> p c t i", i=4),
-                bank[:].rearrange("p t (c i) -> p c t i", i=4),
-                relu_g[n][:, SUB // 4 * s : SUB // 4 * (s + 1), :, :],
+                hid[n][:, SUB * s : SUB * (s + 1), :].rearrange("p (g i) t -> p g t i", i=LINE),
+                bank[:].rearrange("p t (g i) -> p g t i", i=LINE),
+                relu_g[n][:, SUB // LINE * s : SUB // LINE * (s + 1), :, :],
                 MULT,
             )
 
-        wd_codes = keep.tile([P, HALVES, N], U32, name="wd_codes", align_bytes=64)
-        wd_scales = keep.tile([P, HALVES, N], U8, name="wd_scales", align_bytes=64)
+        wd_codes = held([P, HALVES, N], U32, "wd_codes")
+        wd_scales = held([P, HALVES, N], U8, "wd_scales")
 
         def quantise_wd():
-            wd_bf = keep.tile([P, HALVES, N, 4], BF16, name="wd_bf", align_bytes=64)
+            wd_bf = held([P, HALVES, N, PACK], BF16, "wd_bf")
             for a in range(HALVES):
                 nc.scalar.copy(
-                    wd_bf[:, a].rearrange("p (c i) t -> p c t i", i=4),
-                    wd_raw[:, a].rearrange("p t (c i) -> p c t i", i=4),
+                    wd_bf[:, a].rearrange("p (g i) t -> p g t i", i=LINE),
+                    wd_raw[:, a].rearrange("p t (g i) -> p g t i", i=LINE),
                 )
             nc.vector.quantize_mx(
                 out=wd_codes[:].rearrange("p a n -> p (a n)").bitcast(FP8X4),
@@ -212,12 +222,12 @@ def tile_list_gmlpt_relu_resL_kernel(
                 in_=wd_bf[:].rearrange("p a n t -> p (a n t)"),
             )
 
-        def quantise(n, lo, hi):
+        def quantise_hid(n, lo, hi):
             if lo == 0:
-                codes = ring.tile([P, CH], U32, name="h_codes", align_bytes=64)
-                scales = ring.tile([P, CH], U8, name="h_scales", align_bytes=64)
-                hq[n] = (codes, scales)
-            codes, scales = hq[n]
+                codes = ring.tile([P, CHUNK], U32, name="hid_codes", align_bytes=ALIGN, bufs=3)
+                scales = ring.tile([P, CHUNK], U8, name="hid_scales", align_bytes=ALIGN, bufs=3)
+                hid_mx[n] = (codes, scales)
+            codes, scales = hid_mx[n]
             nc.vector.quantize_mx(
                 out=codes[:, lo:hi].bitcast(FP8X4),
                 scales=scales[:, lo:hi],
@@ -226,7 +236,7 @@ def tile_list_gmlpt_relu_resL_kernel(
 
         def down(c, m, lo, hi, acc):
             for a in range(HALVES):
-                codes, scales = hq[HALVES * c + a]
+                codes, scales = hid_mx[HALVES * c + a]
                 nc.tensor.matmul_mx(
                     out=acc,
                     lhsT=wd_codes[:, a, m * P : (m + 1) * P].bitcast(FP8X4),
@@ -238,52 +248,69 @@ def tile_list_gmlpt_relu_resL_kernel(
                 )
 
         def gather_res(c, m):
-            if m == 0:
-                res[c] = ring.tile([P, N // P, CH], F32, name="res", bufs=2)
-            nc.vector.tensor_copy(res[c][:, m, :], r_win[:, m, :].indirect(piece(c)))
+            if c < LAST:
+                res[c, m] = held([P, CHUNK], F32, "res%d%d" % (c, m), paced_tag(("res", c, m)))
+                dst = res[c, m][:]
+            else:
+                if m == 0:
+                    res[c] = held([P, OUT_TILES, CHUNK], F32, "res_last", paced_tag(("res", c, m)))
+                dst = res[c][:, m, :]
+            nc.vector.tensor_copy(dst, res_win[:, m, :].indirect(entries(c)))
 
         def finish(c, m):
-            bank = ps_g.tile([P, CH], F32, name="bank_g")
-            down(c, m, 0, CH, bank[:])
-            y = ring.tile([P, CH], F32, name="y", bufs=2)
+            bank = ps_gate.tile([P, CHUNK], F32, name="bank_gate")
+            down(c, m, 0, CHUNK, bank[:])
+            y = ring.tile([P, CHUNK], F32, name="y")
             nc.scalar.copy(y[:], bank[:])
-            o = ring.tile([P, CH], F32, name="o", bufs=2)
-            for lo in (0, CH // 2):
-                nc.gpsimd.tensor_tensor(
-                    o[:, lo : lo + CH // 2], y[:, lo : lo + CH // 2], res[c][:, m, lo : lo + CH // 2], ADD
-                )
-            nc.sync.dma_start(out[m * P : (m + 1) * P, c * CH : (c + 1) * CH], o[:])
+            total = ring.tile([P, CHUNK], F32, name="total")
+            for lo in (0, CHUNK // 2):
+                cols = slice(lo, lo + CHUNK // 2)
+                nc.gpsimd.tensor_tensor(total[:, cols], y[:, cols], res[c, m][:, cols], ADD)
+            nc.sync.dma_start(out[m * P : (m + 1) * P, c * CHUNK : (c + 1) * CHUNK], total[:])
 
-        def finish_last(c, lo, hi):
-            bank = ps_g.tile([P, CH], F32, name="bank_g")
-            acc = bank[:].rearrange("p (m j) -> p m j", m=N // P)
-            for m in range(N // P):
-                down(c, m, lo, hi, acc[:, m, :])
-            o = ring.tile([P, N // P, hi - lo], F32, name="o_last", bufs=2)
-            nc.vector.tensor_tensor(o[:], acc, res[c][:, :, lo:hi], ADD)
-            nc.sync.dma_start(out.rearrange("(m p) j -> p m j", p=P)[:, :, c * CH + lo : c * CH + hi], o[:])
+        def finish_last(lo, hi):
+            bank = ps_gate.tile([P, CHUNK], F32, name="bank_gate")
+            acc = bank[:, 0 : OUT_TILES * (hi - lo)].rearrange("p (m j) -> p m j", m=OUT_TILES)
+            for m in range(OUT_TILES):
+                down(LAST, m, lo, hi, acc[:, m, :])
+            total = held([P, OUT_TILES, hi - lo], F32, "total_last%d" % lo)
+            nc.vector.tensor_tensor(total[:], acc, res[LAST][:, :, lo:hi], ADD)
+            nc.sync.dma_start(
+                out.rearrange("(m p) j -> p m j", p=P)[:, :, LAST * CHUNK + lo : LAST * CHUNK + hi], total[:]
+            )
 
-        for t in range(4):
+        for t in range(PACK):
             gate(0, t)
-        sort_words(1)
         for n in range(STEPS):
             c, a = divmod(n, HALVES)
-            for i in range(4):
+            for s in range(PACK):
                 if n + 1 < STEPS:
-                    gate(n + 1, i)
-                up(n, i)
-                if i == 0 and n == 1:
+                    gate(n + 1, s)
+                up(n, s)
+                if (n, s) == (1, 0):
                     quantise_wd()
-                if i == 0 and n > 0:
-                    quantise(n - 1, 0, CH)
-                if a == 0 and i == 0 and c + 1 < CHUNKS:
-                    gather_words(c + 1)
-                if a == 0 and i in (2, 3) and n > 0:
-                    finish(c - 1, i - 2)
-                if a == 1 and i in (1, 2):
-                    gather_res(c, i - 1)
-                if n == STEPS - 1 and i == 2:
-                    quantise(n, 0, CH // 2)
-        finish_last(CHUNKS - 1, 0, CH // 2)
-        quantise(STEPS - 1, CH // 2, CH)
-        finish_last(CHUNKS - 1, CH // 2, CH)
+                if s == 0 and n > 0:
+                    quantise_hid(n - 1, 0, CHUNK)
+                if (n, s) == (0, 0):
+                    gather_words(1, "both")
+                if (n, s) == (0, 2):
+                    last_scales()
+                if (n, s) == (0, 3):
+                    gather_words(2, "wu_raw1")
+                turn = 2 * (n - 1) + s // 2
+                if s % 2 == 0 and 0 <= turn < len(PACED):
+                    kind, chunk, m = PACED[turn]
+                    if kind == "words":
+                        gather_words(chunk, paced_tag(PACED[turn]))
+                    else:
+                        gather_res(chunk, m)
+                if a == 0 and c > 0 and s >= PACK - OUT_TILES:
+                    finish(c - 1, s - (PACK - OUT_TILES))
+                if (n, s) == (STEPS - 1, 2):
+                    quantise_hid(n, 0, 2 * SUB)
+                if (n, s) == (STEPS - 1, 3):
+                    quantise_hid(n, 2 * SUB, 3 * SUB)
+        finish_last(0, 2 * SUB)
+        quantise_hid(STEPS - 1, 3 * SUB, CHUNK)
+        finish_last(2 * SUB, 3 * SUB)
+        finish_last(3 * SUB, CHUNK)

@@ -33,6 +33,7 @@ LINE = 4
 W_SCALE_WORDS = K_PASSES * R // 4
 CHUNK_WORDS = CHUNK // 4
 GATE_BANKS, UP_BANKS = 3, 5
+WIDE = tuple(range(HALVES, STEPS, HALVES))
 ALIGN = 64
 
 PACED = [("words", LAST, 0)] + [("res", c, m) for c in range(CHUNKS) for m in range(OUT_TILES)]
@@ -68,8 +69,11 @@ def tile_list_gmlpt_relu_resL_kernel(
         nc.gpsimd.memset(scale_win[:, T // 8 :], 0)
         w_scale_raw = held([P, K_PASSES, R // 4], I32, "w_scale_raw")
         nc.vector.memset(w_scale_raw[:], 0)
-        planes = held([P, 2, W_SCALE_WORDS + J // 4], I32, "planes")
-        nc.vector.memset(planes[:], 0)
+        planes_first = held([P, 2, W_SCALE_WORDS + CHUNK_WORDS], I32, "planes_first")
+        planes_mid = held([P, 2, (LAST - 1) * CHUNK_WORDS], I32, "planes_mid")
+        planes_last = held([P, 2, CHUNK_WORDS], I32, "planes_last")
+        for planes in (planes_first, planes_mid, planes_last):
+            nc.vector.memset(planes[:], 0)
         warm = keep.tile([P, 2, 8], F32, name="warm")
         nc.gpsimd.memset(warm[:, 0, :], 0.0)
         nc.scalar.activation(warm[:, 1, :], warm[:, 0, :], RELU)
@@ -104,16 +108,20 @@ def tile_list_gmlpt_relu_resL_kernel(
         def gather_scales(c, dst):
             nc.vector.tensor_copy(dst, scale_win[:].bitcast(U8).indirect(entries(c)))
 
-        def move_scales(queue, src, lo, hi):
+        def move_scales(queue, src, dst):
             for quad in range(4):
-                queue.dma_start(planes[32 * quad : 32 * quad + 4, :, lo:hi], src[32 * quad : 32 * quad + 32 : 4, :])
+                queue.dma_start(dst[32 * quad : 32 * quad + 4, :, :], src[32 * quad : 32 * quad + 32 : 4, :])
 
         def table_plane(c, kp, lo, hi):
-            return planes[:, kp, W_SCALE_WORDS:].bitcast(U8)[:, c * CHUNK + lo : c * CHUNK + hi]
+            if c == 0:
+                return planes_first[:, kp, W_SCALE_WORDS:].bitcast(U8)[:, lo:hi]
+            if c == LAST:
+                return planes_last[:, kp, :].bitcast(U8)[:, lo:hi]
+            return planes_mid[:, kp, :].bitcast(U8)[:, (c - 1) * CHUNK + lo : (c - 1) * CHUNK + hi]
 
         def weight_plane(x, kp, a, t):
             at = ((kp * HALVES + a) * PACK + t) * (P // 4)
-            return planes[:, x, at : at + P // 4].bitcast(U8)
+            return planes_first[:, x, at : at + P // 4].bitcast(U8)
 
         table = {}
 
@@ -143,16 +151,14 @@ def tile_list_gmlpt_relu_resL_kernel(
             staged[:, 0:W_SCALE_WORDS].rearrange("p (g t b e) -> p g t b e", t=PACK, b=P // RUN, e=RUN // 4),
             w_scale_raw[:].rearrange("p k (a b t e) -> p (k a) t b e", a=HALVES, t=PACK, e=RUN // 4),
         )
-        move_scales(nc.scalar, staged, 0, W_SCALE_WORDS + CHUNK_WORDS)
+        move_scales(nc.scalar, staged, planes_first)
         gather_words(0, "both")
         for a in range(HALVES):
             sort_words(a)
         picked_mid = held([P, (LAST - 1) * CHUNK], U8, "picked_mid", "w_scale_raw")
         for c in range(1, LAST):
             gather_scales(c, picked_mid[:, (c - 1) * CHUNK : c * CHUNK])
-        move_scales(
-            nc.sync, picked_mid[:].bitcast(I32), W_SCALE_WORDS + CHUNK_WORDS, W_SCALE_WORDS + LAST * CHUNK_WORDS
-        )
+        move_scales(nc.sync, picked_mid[:].bitcast(I32), planes_mid)
         load_wd(wd_pieces[1:])
         for m in range(OUT_TILES):
             nc.sync.dma_start(res_win[:, m, :], rT[m * P : (m + 1) * P, :])
@@ -160,9 +166,7 @@ def tile_list_gmlpt_relu_resL_kernel(
         def last_scales():
             picked_last = held([P, CHUNK], U8, "picked_last", "wg_raw1")
             gather_scales(LAST, picked_last[:])
-            move_scales(
-                nc.sync, picked_last[:].bitcast(I32), W_SCALE_WORDS + LAST * CHUNK_WORDS, W_SCALE_WORDS + J // 4
-            )
+            move_scales(nc.sync, picked_last[:].bitcast(I32), planes_last)
 
         relu_g, hid, hid_mx, res = {}, {}, {}, {}
 
@@ -203,6 +207,36 @@ def tile_list_gmlpt_relu_resL_kernel(
                 hid[n][:, SUB * s : SUB * (s + 1), :].rearrange("p (g i) t -> p g t i", i=LINE),
                 bank[:].rearrange("p t (g i) -> p g t i", i=LINE),
                 relu_g[n][:, SUB // LINE * s : SUB // LINE * (s + 1), :, :],
+                MULT,
+            )
+
+        up_copy = {}
+
+        def up_wide(n, t):
+            c, a = divmod(n, HALVES)
+            if t == 0:
+                up_copy[n] = ring.tile([P, CHUNK // LINE, PACK, LINE], F32, name="up_copy", bufs=1)
+            bank = ps_up.tile([P, CHUNK], F32, name="bank_up")
+            for kp in range(K_PASSES):
+                nc.tensor.matmul_mx(
+                    out=bank[:],
+                    lhsT=wu_sorted[a][:, t, kp, :].bitcast(FP4X4),
+                    lhsT_scale=weight_plane(1, kp, a, t),
+                    rhs=table[c][:, kp, :].bitcast(FP4X4),
+                    rhs_scale=table_plane(c, kp, 0, CHUNK),
+                    start=(kp == 0),
+                    stop=(kp == K_PASSES - 1),
+                )
+            nc.scalar.copy(up_copy[n][:, :, t, :], bank[:].rearrange("p (g i) -> p g i", i=LINE))
+
+        def product_wide(n, lo, hi):
+            if lo == 0:
+                hid[n] = held([P, CHUNK, PACK], BF16, "hid%d" % n)
+            groups = slice(lo // LINE, hi // LINE)
+            nc.vector.tensor_tensor(
+                hid[n][:, lo:hi, :].rearrange("p (g i) t -> p g t i", i=LINE),
+                up_copy[n][:, groups, :, :],
+                relu_g[n][:, groups, :, :],
                 MULT,
             )
 
@@ -286,7 +320,12 @@ def tile_list_gmlpt_relu_resL_kernel(
             for s in range(PACK):
                 if n + 1 < STEPS:
                     gate(n + 1, s)
-                up(n, s)
+                if n + 1 in WIDE:
+                    up_wide(n + 1, s)
+                if n not in WIDE:
+                    up(n, s)
+                elif s % 2 == 0:
+                    product_wide(n, SUB * s, SUB * (s + 2))
                 if (n, s) == (1, 0):
                     quantise_wd()
                 if s == 0 and n > 0:
@@ -304,8 +343,8 @@ def tile_list_gmlpt_relu_resL_kernel(
                         gather_words(chunk, paced_tag(PACED[turn]))
                     else:
                         gather_res(chunk, m)
-                if a == 0 and c > 0 and s >= PACK - OUT_TILES:
-                    finish(c - 1, s - (PACK - OUT_TILES))
+                if a == 1 and c > 0 and s < OUT_TILES:
+                    finish(c - 1, s)
                 if (n, s) == (STEPS - 1, 2):
                     quantise_hid(n, 0, 2 * SUB)
                 if (n, s) == (STEPS - 1, 3):

@@ -30,18 +30,14 @@ SUB = CHUNK // PACK
 STEPS = CHUNKS * HALVES
 OUT_TILES = N // P
 LINE = 4
-W_SCALE_WORDS = K_PASSES * R // 4
+W_WORDS = K_PASSES * PASS // 4
 CHUNK_WORDS = CHUNK // 4
-GATE_BANKS, UP_BANKS = 3, 5
-WIDE = tuple(range(HALVES, STEPS, HALVES))
+BANKS = 8
 ALIGN = 64
-
-PACED = [("words", LAST, 0)] + [("res", c, m) for c in range(CHUNKS) for m in range(OUT_TILES)]
-
-
-def paced_tag(job):
-    n, second = divmod(PACED.index(job), 2)
-    return "%s%d" % (("gate", "hid")[second], n)
+LIVE = 96
+DEPTH = 3
+DOWN_AFTER = {2: 0, 4: 1}
+RES_AFTER = {(2, 0): (0, 0), (3, 0): (1, 0), (2, 1): (3, 0), (3, 1): (4, 0)}
 
 
 def tile_list_gmlpt_relu_resL_kernel(
@@ -52,11 +48,16 @@ def tile_list_gmlpt_relu_resL_kernel(
         lists = ctx.enter_context(tc.tile_pool(name="lists", bufs=1))
         keep = ctx.enter_context(tc.tile_pool(name="keep", bufs=1))
         ring = ctx.enter_context(tc.tile_pool(name="ring", bufs=2))
-        ps_gate = ctx.enter_context(tc.psum_pool(name="ps_gate", bufs=GATE_BANKS))
-        ps_up = ctx.enter_context(tc.psum_pool(name="ps_up", bufs=UP_BANKS))
+        psum = ctx.enter_context(tc.psum_pool(name="psum", bufs=1))
 
         def held(shape, dtype, name, tag=None):
             return keep.tile(shape, dtype, name=name, tag=tag or name, align_bytes=ALIGN)
+
+        used = []
+
+        def next_bank():
+            used.append(0)
+            return psum.tile([P, CHUNK], F32, name="bank%d" % len(used), tag="bank%d" % (len(used) % BANKS))
 
         offsets = lists.tile([P, J // 16], U16, name="offsets")
         nc.sync.dma_start(offsets[:], offs)
@@ -65,191 +66,197 @@ def tile_list_gmlpt_relu_resL_kernel(
             return offsets[:, c * CHUNK // 16 : (c + 1) * CHUNK // 16]
 
         scale_win = held([P, T // 4], I32, "scale_win")
-        nc.vector.memset(scale_win[:, 0 : T // 8], 0)
-        nc.gpsimd.memset(scale_win[:, T // 8 :], 0)
+        nc.sync.dma_start(scale_win[LIVE:P, :], tab_scales.rearrange("a s t -> s a t").bitcast(I32))
         w_scale_raw = held([P, K_PASSES, R // 4], I32, "w_scale_raw")
-        nc.vector.memset(w_scale_raw[:], 0)
-        planes_first = held([P, 2, W_SCALE_WORDS + CHUNK_WORDS], I32, "planes_first")
-        planes_mid = held([P, 2, (LAST - 1) * CHUNK_WORDS], I32, "planes_mid")
-        planes_last = held([P, 2, CHUNK_WORDS], I32, "planes_last")
-        for planes in (planes_first, planes_mid, planes_last):
+        for x, w_scales in enumerate((wg_scales, wu_scales)):
+            nc.sync.dma_start(w_scale_raw[LIVE + x : P : 2, :, :], w_scales.rearrange("k s c -> s k c").bitcast(I32))
+        word_win = held([P, T], I32, "word_win")
+        nc.sync.dma_start(word_win[:], tab_words[0].rearrange("p t b -> p (t b)").bitcast(I32))
+        wg_raw = {}
+
+        def load_wg(a, tag):
+            wg_raw[a] = held([P, K_PASSES, PASS], I32, "wg_raw%d" % a, tag)
+            nc.sync.dma_start(
+                wg_raw[a][:],
+                wg_words[:, :, PASS * a : PASS * (a + 1), :].rearrange("k p r i -> p k (r i)").bitcast(I32),
+            )
+
+        load_wg(0, "wg_raw0")
+
+        nc.vector.memset(scale_win[0:LIVE, :], 0)
+        planes_a = held([P, 2, W_WORDS + CHUNK_WORDS], I32, "planes_a")
+        planes_b = held([P, 2, W_WORDS + (LAST - 1) * CHUNK_WORDS], I32, "planes_b")
+        planes_c = held([P, 2, CHUNK_WORDS], I32, "planes_c")
+        for planes in (planes_a, planes_b, planes_c):
             nc.vector.memset(planes[:], 0)
         warm = keep.tile([P, 2, 8], F32, name="warm")
         nc.gpsimd.memset(warm[:, 0, :], 0.0)
         nc.scalar.activation(warm[:, 1, :], warm[:, 0, :], RELU)
 
-        wg_raw = [held([P, K_PASSES, PASS], I32, "wg_raw%d" % a) for a in range(HALVES)]
-        wu_raw = [held([P, K_PASSES, PASS // 2], I32, "wu_raw%d" % a) for a in range(HALVES)]
-        wd_raw = held([P, HALVES, PACK, N], F32, "wd_raw")
-        wd_rows = wd.rearrange("(a b t q) n -> a t b q n", a=HALVES, t=PACK, q=RUN)
-        wd_pieces = [(a, t) for a in range(HALVES) for t in range(PACK)]
-        res_win = held([P, OUT_TILES, T], F32, "res_win")
-        word_win = held([P, T], I32, "word_win")
-
-        def load_wd(pieces):
-            for a, t in pieces:
-                nc.sync.dma_start(wd_raw[:, a, t, :], wd_rows[a, t])
-
-        load_wd(wd_pieces[:1])
-        nc.sync.dma_start(scale_win[0:P:4, :], tab_scales.rearrange("a s t -> s a t").bitcast(I32))
-        for x, w_scales in enumerate((wg_scales, wu_scales)):
-            nc.sync.dma_start(w_scale_raw[4 * x : P : 8, :, :], w_scales.rearrange("k s c -> s k c").bitcast(I32))
-        nc.sync.dma_start(word_win[:], tab_words[0].rearrange("p t b -> p (t b)").bitcast(I32))
-        for a in range(HALVES):
-            nc.sync.dma_start(
-                wg_raw[a][:],
-                wg_words[:, :, PASS * a : PASS * (a + 1), :].rearrange("k p r i -> p k (r i)").bitcast(I32),
-            )
-            nc.sync.dma_start(
-                wu_raw[a][:],
-                wu_words[:, :, 2 * PASS * a : 2 * PASS * (a + 1)].rearrange("k p c -> p k c").bitcast(I32),
-            )
-
         def gather_scales(c, dst):
             nc.vector.tensor_copy(dst, scale_win[:].bitcast(U8).indirect(entries(c)))
 
+        def sort_scales(a, staged):
+            nc.vector.tensor_copy(
+                staged[LIVE:P, 0:W_WORDS].rearrange("p (k t b e) -> p k t b e", k=K_PASSES, t=PACK, e=RUN // 4),
+                w_scale_raw[LIVE:P, :, PASS // 4 * a : PASS // 4 * (a + 1)].rearrange(
+                    "p k (b t e) -> p k t b e", t=PACK, e=RUN // 4
+                ),
+            )
+
         def move_scales(queue, src, dst):
             for quad in range(4):
-                queue.dma_start(dst[32 * quad : 32 * quad + 4, :, :], src[32 * quad : 32 * quad + 32 : 4, :])
+                queue.dma_start(dst[32 * quad : 32 * quad + 4, :, :], src[LIVE + 8 * quad : LIVE + 8 * quad + 8, :])
 
         def table_plane(c, kp, lo, hi):
             if c == 0:
-                return planes_first[:, kp, W_SCALE_WORDS:].bitcast(U8)[:, lo:hi]
+                return planes_a[:, kp, W_WORDS:].bitcast(U8)[:, lo:hi]
             if c == LAST:
-                return planes_last[:, kp, :].bitcast(U8)[:, lo:hi]
-            return planes_mid[:, kp, :].bitcast(U8)[:, (c - 1) * CHUNK + lo : (c - 1) * CHUNK + hi]
+                return planes_c[:, kp, :].bitcast(U8)[:, lo:hi]
+            return planes_b[:, kp, W_WORDS:].bitcast(U8)[:, (c - 1) * CHUNK + lo : (c - 1) * CHUNK + hi]
 
         def weight_plane(x, kp, a, t):
-            at = ((kp * HALVES + a) * PACK + t) * (P // 4)
-            return planes_first[:, x, at : at + P // 4].bitcast(U8)
+            at = (kp * PACK + t) * (P // 4)
+            return (planes_a, planes_b)[a][:, x, at : at + P // 4].bitcast(U8)
 
-        table = {}
+        both, table = {}, {}
 
-        def gather_words(c, tag):
-            both = held([P, CHUNK], U32, "both%d" % c, tag)
-            nc.vector.tensor_copy(both[:], word_win[:].bitcast(U32).indirect(entries(c)))
+        def gather_words(c):
+            both[c] = held([P, CHUNK], U32, "both%d" % c, ("both0", "wg_raw0", "picked_a", "staged_b")[c])
+            nc.vector.tensor_copy(both[c][:], word_win[:].bitcast(U32).indirect(entries(c)))
+
+        def part_words(c):
             table[c] = held([P, K_PASSES, 2 * CHUNK], U8, "parted%d" % c)
             nc.vector.tensor_copy(
-                table[c][:].bitcast(U16), both[:].bitcast(U16).rearrange("p (j d) -> p d j", d=K_PASSES)
+                table[c][:].bitcast(U16), both[c][:].bitcast(U16).rearrange("p (j d) -> p d j", d=K_PASSES)
             )
 
         wg_sorted, wu_sorted = {}, {}
 
-        def sort_words(a):
-            for name, raw, store, e in (("wg", wg_raw, wg_sorted, RUN), ("wu", wu_raw, wu_sorted, RUN // 2)):
-                store[a] = held([P, PACK, K_PASSES, P // RUN * e], I32, "%s_sorted%d" % (name, a))
-                nc.vector.tensor_copy(
-                    store[a][:].rearrange("p t k (b e) -> p t (k b) e", e=e),
-                    raw[a][:].rearrange("p k (b t e) -> p t (k b) e", t=PACK, e=e),
-                )
+        def sort_wg(a):
+            wg_sorted[a] = held([P, PACK, K_PASSES, P], I32, "wg_sorted%d" % a)
+            nc.vector.tensor_copy(
+                wg_sorted[a][:].rearrange("p t k (b e) -> p t (k b) e", e=RUN),
+                wg_raw[a][:].rearrange("p k (b t e) -> p t (k b) e", t=PACK, e=RUN),
+            )
 
-        picked_first = held([P, CHUNK], U8, "picked_first")
-        staged = held([P, W_SCALE_WORDS + CHUNK_WORDS], I32, "staged")
-        gather_scales(0, picked_first[:])
-        nc.vector.tensor_copy(staged[:, W_SCALE_WORDS:], picked_first[:].bitcast(I32))
-        nc.vector.tensor_copy(
-            staged[:, 0:W_SCALE_WORDS].rearrange("p (g t b e) -> p g t b e", t=PACK, b=P // RUN, e=RUN // 4),
-            w_scale_raw[:].rearrange("p k (a b t e) -> p (k a) t b e", a=HALVES, t=PACK, e=RUN // 4),
-        )
-        move_scales(nc.scalar, staged, planes_first)
-        gather_words(0, "both")
-        for a in range(HALVES):
-            sort_words(a)
-        picked_mid = held([P, (LAST - 1) * CHUNK], U8, "picked_mid", "w_scale_raw")
+        def sort_wu(a):
+            wu_sorted[a] = held([P, PACK, K_PASSES, P // 2], I32, "wu_sorted%d" % a)
+            nc.vector.tensor_copy(
+                wu_sorted[a][:].rearrange("p t k (b e) -> p t k b e", e=RUN // 2),
+                wu_raw[:, :, PASS // 2 * a : PASS // 2 * (a + 1)].rearrange(
+                    "p k (b t e) -> p t k b e", t=PACK, e=RUN // 2
+                ),
+            )
+
+        picked_a = held([P, CHUNK], U8, "picked_a")
+        staged_a = held([P, W_WORDS + CHUNK_WORDS], I32, "staged_a")
+        gather_scales(0, picked_a[:])
+        sort_scales(0, staged_a)
+        nc.vector.tensor_copy(staged_a[LIVE:P, W_WORDS:], picked_a[LIVE:P, :].bitcast(I32))
+        move_scales(nc.scalar, staged_a, planes_a)
+        wu_raw = held([P, K_PASSES, R // 2], I32, "wu_raw", "picked_a")
+        nc.sync.dma_start(wu_raw[:], wu_words.rearrange("k p c -> p k c").bitcast(I32))
+        load_wg(1, "staged_a")
+        gather_words(0)
+        sort_wg(0)
+        part_words(0)
+        sort_wu(0)
+        picked_b = held([P, (LAST - 1) * CHUNK], U8, "picked_b")
+        staged_b = held([P, W_WORDS + (LAST - 1) * CHUNK_WORDS], I32, "staged_b")
         for c in range(1, LAST):
-            gather_scales(c, picked_mid[:, (c - 1) * CHUNK : c * CHUNK])
-        move_scales(nc.sync, picked_mid[:].bitcast(I32), planes_mid)
-        load_wd(wd_pieces[1:])
-        for m in range(OUT_TILES):
-            nc.sync.dma_start(res_win[:, m, :], rT[m * P : (m + 1) * P, :])
+            gather_scales(c, picked_b[:, (c - 1) * CHUNK : c * CHUNK])
+        sort_scales(1, staged_b)
+        nc.vector.tensor_copy(staged_b[LIVE:P, W_WORDS:], picked_b[LIVE:P, :].bitcast(I32))
+        move_scales(nc.scalar, staged_b, planes_b)
 
-        def last_scales():
-            picked_last = held([P, CHUNK], U8, "picked_last", "wg_raw1")
-            gather_scales(LAST, picked_last[:])
-            move_scales(nc.sync, picked_last[:].bitcast(I32), planes_last)
+        wd_raw = held([P, HALVES, PACK, N], F32, "wd_raw", "picked_b")
+        wd_rows = wd.rearrange("(a b t q) n -> a t b q n", a=HALVES, t=PACK, q=RUN)
+        for a in range(HALVES):
+            for t in range(PACK):
+                nc.sync.dma_start(wd_raw[:, a, t, :], wd_rows[a, t])
+        res_win = {}
 
-        relu_g, hid, hid_mx, res = {}, {}, {}, {}
+        def load_res(m, tag):
+            res_win[m] = held([P, T], F32, "res_win%d" % m, tag)
+            nc.sync.dma_start(res_win[m][:], rT[m * P : (m + 1) * P, :])
+
+        gather_words(1)
+        sort_wg(1)
+        part_words(1)
+        load_res(0, "wg_raw0")
+        sort_wu(1)
+        gather_words(2)
+        picked_c = held([P, CHUNK], U8, "picked_c", "staged_a")
+        gather_scales(LAST, picked_c[:])
+        part_words(2)
+        load_res(1, "picked_a")
+        move_scales(nc.sync, picked_c[:].bitcast(I32), planes_c)
+        gather_words(3)
+        part_words(3)
+
+        relu_g, up_copy, hid, hid_mx, res = {}, {}, {}, {}, {}
+
+        def first_products(bank, x, n, t, lo, hi):
+            c, a = divmod(n, HALVES)
+            for kp in range(K_PASSES):
+                nc.tensor.matmul_mx(
+                    out=bank,
+                    lhsT=(wg_sorted[a][:, t, kp, :].bitcast(FP8X4), wu_sorted[a][:, t, kp, :].bitcast(FP4X4))[x],
+                    lhsT_scale=weight_plane(x, kp, a, t),
+                    rhs=table[c][:, kp, 2 * lo : 2 * hi].bitcast(FP4X4),
+                    rhs_scale=table_plane(c, kp, lo, hi),
+                    start=(kp == 0),
+                    stop=(kp == K_PASSES - 1),
+                )
 
         def gate(n, t):
-            c, a = divmod(n, HALVES)
             if t == 0:
-                relu_g[n] = held([P, CHUNK // LINE, PACK, LINE], F32, "gate%d" % n)
-            bank = ps_gate.tile([P, CHUNK], F32, name="bank_gate")
-            for kp in range(K_PASSES):
-                nc.tensor.matmul_mx(
-                    out=bank[:],
-                    lhsT=wg_sorted[a][:, t, kp, :].bitcast(FP8X4),
-                    lhsT_scale=weight_plane(0, kp, a, t),
-                    rhs=table[c][:, kp, :].bitcast(FP4X4),
-                    rhs_scale=table_plane(c, kp, 0, CHUNK),
-                    start=(kp == 0),
-                    stop=(kp == K_PASSES - 1),
-                )
+                relu_g[n] = ring.tile([P, CHUNK // LINE, PACK, LINE], F32, name="relu_g", bufs=DEPTH)
+            bank = next_bank()
+            first_products(bank[:], 0, n, t, 0, CHUNK)
             nc.scalar.activation(relu_g[n][:, :, t, :], bank[:].rearrange("p (g i) -> p g i", i=LINE), RELU)
 
-        def up(n, s):
-            c, a = divmod(n, HALVES)
-            if s == 0:
-                hid[n] = held([P, CHUNK, PACK], BF16, "hid%d" % n)
-            bank = ps_up.tile([P, PACK, SUB], F32, name="bank_up")
-            for t in range(PACK):
-                for kp in range(K_PASSES):
-                    nc.tensor.matmul_mx(
-                        out=bank[:, t, :],
-                        lhsT=wu_sorted[a][:, t, kp, :].bitcast(FP4X4),
-                        lhsT_scale=weight_plane(1, kp, a, t),
-                        rhs=table[c][:, kp, 2 * SUB * s : 2 * SUB * (s + 1)].bitcast(FP4X4),
-                        rhs_scale=table_plane(c, kp, SUB * s, SUB * (s + 1)),
-                        start=(kp == 0),
-                        stop=(kp == K_PASSES - 1),
-                    )
-            nc.vector.tensor_tensor(
-                hid[n][:, SUB * s : SUB * (s + 1), :].rearrange("p (g i) t -> p g t i", i=LINE),
-                bank[:].rearrange("p t (g i) -> p g t i", i=LINE),
-                relu_g[n][:, SUB // LINE * s : SUB // LINE * (s + 1), :, :],
-                MULT,
-            )
-
-        up_copy = {}
-
         def up_wide(n, t):
-            c, a = divmod(n, HALVES)
             if t == 0:
-                up_copy[n] = ring.tile([P, CHUNK // LINE, PACK, LINE], F32, name="up_copy", bufs=1)
-            bank = ps_up.tile([P, CHUNK], F32, name="bank_up")
-            for kp in range(K_PASSES):
-                nc.tensor.matmul_mx(
-                    out=bank[:],
-                    lhsT=wu_sorted[a][:, t, kp, :].bitcast(FP4X4),
-                    lhsT_scale=weight_plane(1, kp, a, t),
-                    rhs=table[c][:, kp, :].bitcast(FP4X4),
-                    rhs_scale=table_plane(c, kp, 0, CHUNK),
-                    start=(kp == 0),
-                    stop=(kp == K_PASSES - 1),
-                )
+                up_copy[n] = ring.tile([P, CHUNK // LINE, PACK, LINE], F32, name="up_copy", bufs=DEPTH)
+            bank = next_bank()
+            first_products(bank[:], 1, n, t, 0, CHUNK)
             nc.scalar.copy(up_copy[n][:, :, t, :], bank[:].rearrange("p (g i) -> p g i", i=LINE))
 
-        def product_wide(n, lo, hi):
-            if lo == 0:
-                hid[n] = held([P, CHUNK, PACK], BF16, "hid%d" % n)
-            groups = slice(lo // LINE, hi // LINE)
+        def product(n, h, lo, hi, up_values):
+            if lo == h * CHUNK // 2:
+                hid[n, h] = held([P, CHUNK // 2, PACK], BF16, "hid%d%d" % (n, h))
+            at = h * CHUNK // 2
             nc.vector.tensor_tensor(
-                hid[n][:, lo:hi, :].rearrange("p (g i) t -> p g t i", i=LINE),
-                up_copy[n][:, groups, :, :],
-                relu_g[n][:, groups, :, :],
+                hid[n, h][:, lo - at : hi - at, :].rearrange("p (g i) t -> p g t i", i=LINE),
+                up_values,
+                relu_g[n][:, lo // LINE : hi // LINE, :, :],
                 MULT,
             )
+
+        def product_wide(n, h):
+            lo, hi = h * CHUNK // 2, (h + 1) * CHUNK // 2
+            product(n, h, lo, hi, up_copy[n][:, lo // LINE : hi // LINE, :, :])
+
+        def up_narrow(n, s):
+            bank = next_bank()
+            quarters = bank[:].rearrange("p (t j) -> p t j", t=PACK)
+            for t in range(PACK):
+                first_products(quarters[:, t, :], 1, n, t, SUB * s, SUB * (s + 1))
+            product(n, s // 2, SUB * s, SUB * (s + 1), quarters.rearrange("p t (g i) -> p g t i", i=LINE))
 
         wd_codes = held([P, HALVES, N], U32, "wd_codes")
         wd_scales = held([P, HALVES, N], U8, "wd_scales")
+        wd_bf = held([P, HALVES, N, PACK], BF16, "wd_bf")
+
+        def cast_wd(a):
+            nc.scalar.copy(
+                wd_bf[:, a].rearrange("p (g i) t -> p g t i", i=LINE),
+                wd_raw[:, a].rearrange("p t (g i) -> p g t i", i=LINE),
+            )
 
         def quantise_wd():
-            wd_bf = held([P, HALVES, N, PACK], BF16, "wd_bf")
-            for a in range(HALVES):
-                nc.scalar.copy(
-                    wd_bf[:, a].rearrange("p (g i) t -> p g t i", i=LINE),
-                    wd_raw[:, a].rearrange("p t (g i) -> p g t i", i=LINE),
-                )
             nc.vector.quantize_mx(
                 out=wd_codes[:].rearrange("p a n -> p (a n)").bitcast(FP8X4),
                 scales=wd_scales[:].rearrange("p a n -> p (a n)"),
@@ -258,14 +265,16 @@ def tile_list_gmlpt_relu_resL_kernel(
 
         def quantise_hid(n, lo, hi):
             if lo == 0:
-                codes = ring.tile([P, CHUNK], U32, name="hid_codes", align_bytes=ALIGN, bufs=3)
-                scales = ring.tile([P, CHUNK], U8, name="hid_scales", align_bytes=ALIGN, bufs=3)
+                codes = ring.tile([P, CHUNK], U32, name="hid_codes", align_bytes=ALIGN, bufs=4)
+                scales = ring.tile([P, CHUNK], U8, name="hid_scales", align_bytes=ALIGN, bufs=4)
                 hid_mx[n] = (codes, scales)
             codes, scales = hid_mx[n]
+            h = lo // (CHUNK // 2)
+            at = h * CHUNK // 2
             nc.vector.quantize_mx(
                 out=codes[:, lo:hi].bitcast(FP8X4),
                 scales=scales[:, lo:hi],
-                in_=hid[n][:, lo:hi, :].rearrange("p j t -> p (j t)"),
+                in_=hid[n, h][:, lo - at : hi - at, :].rearrange("p j t -> p (j t)"),
             )
 
         def down(c, m, lo, hi, acc):
@@ -282,74 +291,64 @@ def tile_list_gmlpt_relu_resL_kernel(
                 )
 
         def gather_res(c, m):
-            if c < LAST:
-                res[c, m] = held([P, CHUNK], F32, "res%d%d" % (c, m), paced_tag(("res", c, m)))
-                dst = res[c, m][:]
-            else:
-                if m == 0:
-                    res[c] = held([P, OUT_TILES, CHUNK], F32, "res_last", paced_tag(("res", c, m)))
-                dst = res[c][:, m, :]
-            nc.vector.tensor_copy(dst, res_win[:, m, :].indirect(entries(c)))
+            res[c, m] = held([P, CHUNK], F32, "res%d%d" % (c, m), "hid%d%d" % RES_AFTER[c, m])
+            nc.vector.tensor_copy(res[c, m][:], res_win[m][:].indirect(entries(c)))
 
-        def finish(c, m):
-            bank = ps_gate.tile([P, CHUNK], F32, name="bank_gate")
-            down(c, m, 0, CHUNK, bank[:])
-            y = ring.tile([P, CHUNK], F32, name="y")
-            nc.scalar.copy(y[:], bank[:])
-            total = ring.tile([P, CHUNK], F32, name="total")
-            for lo in (0, CHUNK // 2):
-                cols = slice(lo, lo + CHUNK // 2)
-                nc.gpsimd.tensor_tensor(total[:, cols], y[:, cols], res[c, m][:, cols], ADD)
-            nc.sync.dma_start(out[m * P : (m + 1) * P, c * CHUNK : (c + 1) * CHUNK], total[:])
+        def finish(c):
+            for m in range(OUT_TILES):
+                bank = next_bank()
+                down(c, m, 0, CHUNK, bank[:])
+                total = ring.tile([P, CHUNK], F32, name="total")
+                if (c, m) in RES_AFTER:
+                    nc.vector.tensor_tensor(total[:], bank[:], res[c, m][:], ADD)
+                else:
+                    y = ring.tile([P, CHUNK], F32, name="y")
+                    nc.scalar.copy(y[:], bank[:])
+                    nc.vector.tensor_tensor(total[:], res_win[m][:].indirect(entries(c)), y[:], ADD)
+                nc.sync.dma_start(out[m * P : (m + 1) * P, c * CHUNK : (c + 1) * CHUNK], total[:])
 
         def finish_last(lo, hi):
-            bank = ps_gate.tile([P, CHUNK], F32, name="bank_gate")
+            bank = next_bank()
             acc = bank[:, 0 : OUT_TILES * (hi - lo)].rearrange("p (m j) -> p m j", m=OUT_TILES)
             for m in range(OUT_TILES):
                 down(LAST, m, lo, hi, acc[:, m, :])
             total = held([P, OUT_TILES, hi - lo], F32, "total_last%d" % lo)
-            nc.vector.tensor_tensor(total[:], acc, res[LAST][:, :, lo:hi], ADD)
+            for m in range(OUT_TILES):
+                nc.vector.tensor_tensor(total[:, m, :], acc[:, m, :], res[LAST, m][:, lo:hi], ADD)
             nc.sync.dma_start(
                 out.rearrange("(m p) j -> p m j", p=P)[:, :, LAST * CHUNK + lo : LAST * CHUNK + hi], total[:]
             )
 
+        for n in range(STEPS - 1):
+            for t in range(PACK):
+                gate(n, t)
+            for t in range(PACK):
+                if (n, t) == (STEPS - 2, 2):
+                    finish(LAST - 1)
+                up_wide(n, t)
+            if n < HALVES:
+                cast_wd(n)
+            if n in DOWN_AFTER:
+                finish(DOWN_AFTER[n])
+            for h in range(2):
+                product_wide(n, h)
+            for h in range(2):
+                quantise_hid(n, h * CHUNK // 2, (h + 1) * CHUNK // 2)
+            if n == 1:
+                quantise_wd()
+            for job, (step, h) in RES_AFTER.items():
+                if step == n:
+                    gather_res(job[0], job[1])
+        n = STEPS - 1
         for t in range(PACK):
-            gate(0, t)
-        for n in range(STEPS):
-            c, a = divmod(n, HALVES)
-            for s in range(PACK):
-                if n + 1 < STEPS:
-                    gate(n + 1, s)
-                if n + 1 in WIDE:
-                    up_wide(n + 1, s)
-                if n not in WIDE:
-                    up(n, s)
-                elif s % 2 == 0:
-                    product_wide(n, SUB * s, SUB * (s + 2))
-                if (n, s) == (1, 0):
-                    quantise_wd()
-                if s == 0 and n > 0:
-                    quantise_hid(n - 1, 0, CHUNK)
-                if (n, s) == (0, 0):
-                    gather_words(1, "both")
-                if (n, s) == (0, 2):
-                    last_scales()
-                if (n, s) == (0, 3):
-                    gather_words(2, "wu_raw1")
-                turn = 2 * (n - 1) + s // 2
-                if s % 2 == 0 and 0 <= turn < len(PACED):
-                    kind, chunk, m = PACED[turn]
-                    if kind == "words":
-                        gather_words(chunk, paced_tag(PACED[turn]))
-                    else:
-                        gather_res(chunk, m)
-                if a == 1 and c > 0 and s < OUT_TILES:
-                    finish(c - 1, s)
-                if (n, s) == (STEPS - 1, 2):
-                    quantise_hid(n, 0, 2 * SUB)
-                if (n, s) == (STEPS - 1, 3):
-                    quantise_hid(n, 2 * SUB, 3 * SUB)
+            gate(n, t)
+        up_narrow(n, 0)
+        up_narrow(n, 1)
+        up_narrow(n, 2)
+        quantise_hid(n, 0, 2 * SUB)
+        up_narrow(n, 3)
+        quantise_hid(n, 2 * SUB, 3 * SUB)
         finish_last(0, 2 * SUB)
-        quantise_hid(STEPS - 1, 3 * SUB, CHUNK)
+        quantise_hid(n, 3 * SUB, CHUNK)
         finish_last(2 * SUB, 3 * SUB)
         finish_last(3 * SUB, CHUNK)

@@ -30,14 +30,16 @@ SUB = CHUNK // PACK
 STEPS = CHUNKS * HALVES
 OUT_TILES = N // P
 LINE = 4
+PAIR = 2
 W_WORDS = K_PASSES * PASS // 4
 CHUNK_WORDS = CHUNK // 4
 BANKS = 8
 ALIGN = 64
 LIVE = 96
 DEPTH = 3
-DOWN_AFTER = {2: 0, 4: 1}
-RES_AFTER = {(2, 0): (0, 0), (3, 0): (1, 0), (2, 1): (3, 0), (3, 1): (4, 0)}
+DOWN_AFTER = {2: 0, 4: 1, 6: 2}
+RES_AFTER = {(0, 0): (0, 0), (1, 0): (1, 0), (2, 0): (1, 1), (0, 1): (2, 0), (1, 1): (3, 0), (3, 0): (3, 1), (2, 1): (4, 0), (3, 1): (5, 0)}
+NARROW = (3, 5, 7)
 
 
 def tile_list_gmlpt_relu_resL_kernel(
@@ -212,39 +214,39 @@ def tile_list_gmlpt_relu_resL_kernel(
 
         def gate(n, t):
             if t == 0:
-                relu_g[n] = ring.tile([P, CHUNK // LINE, PACK, LINE], F32, name="relu_g", bufs=DEPTH)
+                relu_g[n] = ring.tile([P, PACK, CHUNK], F32, name="relu_g", bufs=DEPTH)
             bank = next_bank()
             first_products(bank[:], 0, n, t, 0, CHUNK)
-            nc.scalar.activation(relu_g[n][:, :, t, :], bank[:].rearrange("p (g i) -> p g i", i=LINE), RELU)
+            nc.scalar.activation(relu_g[n][:, t, :], bank[:], RELU)
 
         def up_wide(n, t):
             if t == 0:
-                up_copy[n] = ring.tile([P, CHUNK // LINE, PACK, LINE], F32, name="up_copy", bufs=DEPTH)
+                up_copy[n] = ring.tile([P, PACK, CHUNK], F32, name="up_copy", bufs=DEPTH)
             bank = next_bank()
             first_products(bank[:], 1, n, t, 0, CHUNK)
-            nc.scalar.copy(up_copy[n][:, :, t, :], bank[:].rearrange("p (g i) -> p g i", i=LINE))
+            nc.scalar.copy(up_copy[n][:, t, :], bank[:])
 
         def product(n, h, lo, hi, up_values):
             if lo == h * CHUNK // 2:
                 hid[n, h] = held([P, CHUNK // 2, PACK], BF16, "hid%d%d" % (n, h))
             at = h * CHUNK // 2
             nc.vector.tensor_tensor(
-                hid[n, h][:, lo - at : hi - at, :].rearrange("p (g i) t -> p g t i", i=LINE),
-                up_values,
-                relu_g[n][:, lo // LINE : hi // LINE, :, :],
+                hid[n, h][:, lo - at : hi - at, :].rearrange("p (g i) t -> p g t i", i=PAIR),
+                up_values.rearrange("p t (g i) -> p g t i", i=PAIR),
+                relu_g[n][:, :, lo:hi].rearrange("p t (g i) -> p g t i", i=PAIR),
                 MULT,
             )
 
         def product_wide(n, h):
             lo, hi = h * CHUNK // 2, (h + 1) * CHUNK // 2
-            product(n, h, lo, hi, up_copy[n][:, lo // LINE : hi // LINE, :, :])
+            product(n, h, lo, hi, up_copy[n][:, :, lo:hi])
 
         def up_narrow(n, s):
             bank = next_bank()
             quarters = bank[:].rearrange("p (t j) -> p t j", t=PACK)
             for t in range(PACK):
                 first_products(quarters[:, t, :], 1, n, t, SUB * s, SUB * (s + 1))
-            product(n, s // 2, SUB * s, SUB * (s + 1), quarters.rearrange("p t (g i) -> p g t i", i=LINE))
+            product(n, s // 2, SUB * s, SUB * (s + 1), quarters)
 
         wd_codes = held([P, HALVES, N], U32, "wd_codes")
         wd_scales = held([P, HALVES, N], U8, "wd_scales")
@@ -294,18 +296,20 @@ def tile_list_gmlpt_relu_resL_kernel(
             res[c, m] = held([P, CHUNK], F32, "res%d%d" % (c, m), "hid%d%d" % RES_AFTER[c, m])
             nc.vector.tensor_copy(res[c, m][:], res_win[m][:].indirect(entries(c)))
 
+        y = {}
+
         def finish(c):
             for m in range(OUT_TILES):
                 bank = next_bank()
                 down(c, m, 0, CHUNK, bank[:])
-                total = ring.tile([P, CHUNK], F32, name="total")
-                if (c, m) in RES_AFTER:
-                    nc.vector.tensor_tensor(total[:], bank[:], res[c, m][:], ADD)
-                else:
-                    y = ring.tile([P, CHUNK], F32, name="y")
-                    nc.scalar.copy(y[:], bank[:])
-                    nc.vector.tensor_tensor(total[:], res_win[m][:].indirect(entries(c)), y[:], ADD)
-                nc.sync.dma_start(out[m * P : (m + 1) * P, c * CHUNK : (c + 1) * CHUNK], total[:])
+                y[c, m] = ring.tile([P, CHUNK], F32, name="y")
+                nc.scalar.copy(y[c, m][:], bank[:])
+
+        def add_res(c, n):
+            total = held([P, OUT_TILES, CHUNK], F32, "total%d" % c, "hid%d1" % n)
+            for m in range(OUT_TILES):
+                nc.gpsimd.tensor_tensor(total[:, m, :], y[c, m][:], res[c, m][:], ADD)
+                nc.sync.dma_start(out[m * P : (m + 1) * P, c * CHUNK : (c + 1) * CHUNK], total[:, m, :])
 
         def finish_last(lo, hi):
             bank = next_bank()
@@ -323,15 +327,17 @@ def tile_list_gmlpt_relu_resL_kernel(
             for t in range(PACK):
                 gate(n, t)
             for t in range(PACK):
-                if (n, t) == (STEPS - 2, 2):
-                    finish(LAST - 1)
-                up_wide(n, t)
+                if n in NARROW:
+                    up_narrow(n, t)
+                else:
+                    up_wide(n, t)
             if n < HALVES:
                 cast_wd(n)
             if n in DOWN_AFTER:
                 finish(DOWN_AFTER[n])
             for h in range(2):
-                product_wide(n, h)
+                if n not in NARROW:
+                    product_wide(n, h)
             for h in range(2):
                 quantise_hid(n, h * CHUNK // 2, (h + 1) * CHUNK // 2)
             if n == 1:
@@ -339,6 +345,8 @@ def tile_list_gmlpt_relu_resL_kernel(
             for job, (step, h) in RES_AFTER.items():
                 if step == n:
                     gather_res(job[0], job[1])
+            if n in DOWN_AFTER:
+                add_res(DOWN_AFTER[n], n)
         n = STEPS - 1
         for t in range(PACK):
             gate(n, t)

@@ -38,8 +38,9 @@ ALIGN = 64
 LIVE = 96
 DEPTH = 3
 DOWN_AFTER = {2: 0, 4: 1, 6: 2}
-RES_AFTER = {(0, 0): (0, 0), (1, 0): (1, 0), (2, 0): (1, 1), (0, 1): (2, 0), (1, 1): (3, 0), (3, 0): (3, 1), (2, 1): (4, 0), (3, 1): (5, 0)}
-NARROW = (3, 5, 7)
+RES_AFTER = {(2, 0): (1, 1), (3, 0): (3, 1), (2, 1): (3, 0), (3, 1): (5, 0)}
+NARROW = (1, 3, 5, 7)
+POOLED = (1, 3, 5)
 
 
 def tile_list_gmlpt_relu_resL_kernel(
@@ -64,8 +65,8 @@ def tile_list_gmlpt_relu_resL_kernel(
         offsets = lists.tile([P, J // 16], U16, name="offsets")
         nc.sync.dma_start(offsets[:], offs)
 
-        def entries(c):
-            return offsets[:, c * CHUNK // 16 : (c + 1) * CHUNK // 16]
+        def entries(c, count=1):
+            return offsets[:, c * CHUNK // 16 : (c + count) * CHUNK // 16]
 
         scale_win = held([P, T // 4], I32, "scale_win")
         nc.sync.dma_start(scale_win[LIVE:P, :], tab_scales.rearrange("a s t -> s a t").bitcast(I32))
@@ -76,14 +77,15 @@ def tile_list_gmlpt_relu_resL_kernel(
         nc.sync.dma_start(word_win[:], tab_words[0].rearrange("p t b -> p (t b)").bitcast(I32))
         wg_raw = {}
 
-        def load_wg(a, tag):
-            wg_raw[a] = held([P, K_PASSES, PASS], I32, "wg_raw%d" % a, tag)
+        def load_wg(a, kp, tag):
+            wg_raw[a, kp] = held([P, PASS], I32, "wg_raw%d%d" % (a, kp), tag)
             nc.sync.dma_start(
-                wg_raw[a][:],
-                wg_words[:, :, PASS * a : PASS * (a + 1), :].rearrange("k p r i -> p k (r i)").bitcast(I32),
+                wg_raw[a, kp][:],
+                wg_words[kp, :, PASS * a : PASS * (a + 1), :].rearrange("p r i -> p (r i)").bitcast(I32),
             )
 
-        load_wg(0, "wg_raw0")
+        load_wg(0, 0, "wg_raw00")
+        load_wg(0, 1, "wg_raw0")
 
         nc.vector.memset(scale_win[0:LIVE, :], 0)
         planes_a = held([P, 2, W_WORDS + CHUNK_WORDS], I32, "planes_a")
@@ -95,8 +97,8 @@ def tile_list_gmlpt_relu_resL_kernel(
         nc.gpsimd.memset(warm[:, 0, :], 0.0)
         nc.scalar.activation(warm[:, 1, :], warm[:, 0, :], RELU)
 
-        def gather_scales(c, dst):
-            nc.vector.tensor_copy(dst, scale_win[:].bitcast(U8).indirect(entries(c)))
+        def gather_scales(c, dst, count=1):
+            nc.vector.tensor_copy(dst, scale_win[:].bitcast(U8).indirect(entries(c, count)))
 
         def sort_scales(a, staged):
             nc.vector.tensor_copy(
@@ -124,7 +126,7 @@ def tile_list_gmlpt_relu_resL_kernel(
         both, table = {}, {}
 
         def gather_words(c):
-            both[c] = held([P, CHUNK], U32, "both%d" % c, ("both0", "wg_raw0", "picked_a", "staged_b")[c])
+            both[c] = held([P, CHUNK], U32, "both%d" % c, ("both0", "wg_raw0", "picked_a", "hid10")[c])
             nc.vector.tensor_copy(both[c][:], word_win[:].bitcast(U32).indirect(entries(c)))
 
         def part_words(c):
@@ -133,22 +135,28 @@ def tile_list_gmlpt_relu_resL_kernel(
                 table[c][:].bitcast(U16), both[c][:].bitcast(U16).rearrange("p (j d) -> p d j", d=K_PASSES)
             )
 
-        wg_sorted, wu_sorted = {}, {}
+        wg_sorted = {}
 
         def sort_wg(a):
             wg_sorted[a] = held([P, PACK, K_PASSES, P], I32, "wg_sorted%d" % a)
-            nc.vector.tensor_copy(
-                wg_sorted[a][:].rearrange("p t k (b e) -> p t (k b) e", e=RUN),
-                wg_raw[a][:].rearrange("p k (b t e) -> p t (k b) e", t=PACK, e=RUN),
-            )
+            if a == 1:
+                nc.vector.tensor_copy(
+                    wg_sorted[a][:].rearrange("p t k (b e) -> p t (k b) e", e=RUN),
+                    wg_raw[a][:].rearrange("p k (b t e) -> p t (k b) e", t=PACK, e=RUN),
+                )
+                return
+            for kp in range(K_PASSES):
+                nc.vector.tensor_copy(
+                    wg_sorted[a][:, :, kp, :].rearrange("p t (b e) -> p t b e", e=RUN),
+                    wg_raw[a, kp][:].rearrange("p (b t e) -> p t b e", t=PACK, e=RUN),
+                )
 
-        def sort_wu(a):
-            wu_sorted[a] = held([P, PACK, K_PASSES, P // 2], I32, "wu_sorted%d" % a)
+        wu_all = held([P, PACK, K_PASSES, HALVES, P // 2], I32, "wu_sorted")
+
+        def sort_wu():
             nc.vector.tensor_copy(
-                wu_sorted[a][:].rearrange("p t k (b e) -> p t k b e", e=RUN // 2),
-                wu_raw[:, :, PASS // 2 * a : PASS // 2 * (a + 1)].rearrange(
-                    "p k (b t e) -> p t k b e", t=PACK, e=RUN // 2
-                ),
+                wu_all[:].rearrange("p t k a (b e) -> p t (k a b) e", e=RUN // 2),
+                wu_raw[:].rearrange("p k (g t e) -> p t (k g) e", t=PACK, e=RUN // 2),
             )
 
         picked_a = held([P, CHUNK], U8, "picked_a")
@@ -159,15 +167,25 @@ def tile_list_gmlpt_relu_resL_kernel(
         move_scales(nc.scalar, staged_a, planes_a)
         wu_raw = held([P, K_PASSES, R // 2], I32, "wu_raw", "picked_a")
         nc.sync.dma_start(wu_raw[:], wu_words.rearrange("k p c -> p k c").bitcast(I32))
-        load_wg(1, "staged_a")
+        wg_raw[1] = held([P, K_PASSES, PASS], I32, "wg_raw1", "staged_a")
+        nc.sync.dma_start(wg_raw[1][:], wg_words[:, :, PASS:, :].rearrange("k p r i -> p k (r i)").bitcast(I32))
         gather_words(0)
         sort_wg(0)
         part_words(0)
-        sort_wu(0)
+        sort_wu()
         picked_b = held([P, (LAST - 1) * CHUNK], U8, "picked_b")
         staged_b = held([P, W_WORDS + (LAST - 1) * CHUNK_WORDS], I32, "staged_b")
-        for c in range(1, LAST):
-            gather_scales(c, picked_b[:, (c - 1) * CHUNK : c * CHUNK])
+        gather_scales(1, picked_b[:], LAST - 1)
+        for w in range(6):
+            nc.tensor.matmul_mx(
+                out=next_bank()[:],
+                lhsT=picked_b[:, 0 : 2 * P].bitcast(FP4X4),
+                lhsT_scale=picked_b[:, 0:P],
+                rhs=picked_b[:].bitcast(FP4X4),
+                rhs_scale=picked_b[:, 0:CHUNK],
+                start=True,
+                stop=True,
+            )
         sort_scales(1, staged_b)
         nc.vector.tensor_copy(staged_b[LIVE:P, W_WORDS:], picked_b[LIVE:P, :].bitcast(I32))
         move_scales(nc.scalar, staged_b, planes_b)
@@ -186,16 +204,15 @@ def tile_list_gmlpt_relu_resL_kernel(
         gather_words(1)
         sort_wg(1)
         part_words(1)
-        load_res(0, "wg_raw0")
-        sort_wu(1)
+        load_res(0, "wg_raw00")
         gather_words(2)
-        picked_c = held([P, CHUNK], U8, "picked_c", "staged_a")
-        gather_scales(LAST, picked_c[:])
         part_words(2)
-        load_res(1, "picked_a")
-        move_scales(nc.sync, picked_c[:].bitcast(I32), planes_c)
-        gather_words(3)
-        part_words(3)
+        load_res(1, "wg_raw0")
+
+        def last_scales():
+            picked_c = held([P, CHUNK], U8, "picked_c", "hid00")
+            gather_scales(LAST, picked_c[:])
+            move_scales(nc.sync, picked_c[:].bitcast(I32), planes_c)
 
         relu_g, up_copy, hid, hid_mx, res = {}, {}, {}, {}, {}
 
@@ -204,7 +221,7 @@ def tile_list_gmlpt_relu_resL_kernel(
             for kp in range(K_PASSES):
                 nc.tensor.matmul_mx(
                     out=bank,
-                    lhsT=(wg_sorted[a][:, t, kp, :].bitcast(FP8X4), wu_sorted[a][:, t, kp, :].bitcast(FP4X4))[x],
+                    lhsT=(wg_sorted[a][:, t, kp, :].bitcast(FP8X4), wu_all[:, t, kp, a, :].bitcast(FP4X4))[x],
                     lhsT_scale=weight_plane(x, kp, a, t),
                     rhs=table[c][:, kp, 2 * lo : 2 * hi].bitcast(FP4X4),
                     rhs_scale=table_plane(c, kp, lo, hi),
@@ -227,7 +244,7 @@ def tile_list_gmlpt_relu_resL_kernel(
             nc.scalar.copy(up_copy[n][:, t, :], bank[:])
 
         def product(n, h, lo, hi, up_values):
-            if lo == h * CHUNK // 2:
+            if (n, h) not in hid:
                 hid[n, h] = held([P, CHUNK // 2, PACK], BF16, "hid%d%d" % (n, h))
             at = h * CHUNK // 2
             nc.vector.tensor_tensor(
@@ -246,7 +263,15 @@ def tile_list_gmlpt_relu_resL_kernel(
             quarters = bank[:].rearrange("p (t j) -> p t j", t=PACK)
             for t in range(PACK):
                 first_products(quarters[:, t, :], 1, n, t, SUB * s, SUB * (s + 1))
-            product(n, s // 2, SUB * s, SUB * (s + 1), quarters)
+            if n in POOLED and s == 0:
+                copied = held([P, SUB, PACK], F32, "up_quarter%d" % n)
+                nc.scalar.copy(copied[:], quarters.rearrange("p t j -> p j t"))
+                hid[n, 2] = held([P, SUB, PACK], BF16, "hid%d2" % n, "y%d1" % DOWN_AFTER[n - 1] if n > 1 else "hid01")
+                nc.gpsimd.tensor_tensor(
+                    hid[n, 2][:], copied[:], relu_g[n][:, :, 0:SUB].rearrange("p t j -> p j t"), MULT
+                )
+            else:
+                product(n, s // 2, SUB * s, SUB * (s + 1), quarters)
 
         wd_codes = held([P, HALVES, N], U32, "wd_codes")
         wd_scales = held([P, HALVES, N], U8, "wd_scales")
@@ -266,13 +291,15 @@ def tile_list_gmlpt_relu_resL_kernel(
             )
 
         def quantise_hid(n, lo, hi):
-            if lo == 0:
+            if n not in hid_mx:
                 codes = ring.tile([P, CHUNK], U32, name="hid_codes", align_bytes=ALIGN, bufs=4)
                 scales = ring.tile([P, CHUNK], U8, name="hid_scales", align_bytes=ALIGN, bufs=4)
                 hid_mx[n] = (codes, scales)
             codes, scales = hid_mx[n]
             h = lo // (CHUNK // 2)
             at = h * CHUNK // 2
+            if n in POOLED and lo == 0:
+                h = 2
             nc.vector.quantize_mx(
                 out=codes[:, lo:hi].bitcast(FP8X4),
                 scales=scales[:, lo:hi],
@@ -293,8 +320,9 @@ def tile_list_gmlpt_relu_resL_kernel(
                 )
 
         def gather_res(c, m):
-            res[c, m] = held([P, CHUNK], F32, "res%d%d" % (c, m), "hid%d%d" % RES_AFTER[c, m])
-            nc.vector.tensor_copy(res[c, m][:], res_win[m][:].indirect(entries(c)))
+            picked = held([P, CHUNK], F32, "res%d%d" % (c, m), "hid%d%d" % RES_AFTER[c, m])
+            nc.vector.tensor_copy(picked[:], res_win[m][:].indirect(entries(c)))
+            res[c, m] = picked[:]
 
         y = {}
 
@@ -302,13 +330,16 @@ def tile_list_gmlpt_relu_resL_kernel(
             for m in range(OUT_TILES):
                 bank = next_bank()
                 down(c, m, 0, CHUNK, bank[:])
-                y[c, m] = ring.tile([P, CHUNK], F32, name="y")
+                y[c, m] = held([P, CHUNK], F32, "y%d%d" % (c, m))
                 nc.scalar.copy(y[c, m][:], bank[:])
 
         def add_res(c, n):
-            total = held([P, OUT_TILES, CHUNK], F32, "total%d" % c, "hid%d1" % n)
+            total = held([P, OUT_TILES, CHUNK], F32, "total%d" % c, "hid%d%d" % (n, (c, 0) in RES_AFTER))
             for m in range(OUT_TILES):
-                nc.gpsimd.tensor_tensor(total[:, m, :], y[c, m][:], res[c, m][:], ADD)
+                if (c, m) in RES_AFTER:
+                    nc.gpsimd.tensor_tensor(total[:, m, :], y[c, m][:], res[c, m], ADD)
+                else:
+                    nc.vector.tensor_tensor(total[:, m, :], res_win[m][:].indirect(entries(c)), y[c, m][:], ADD)
                 nc.sync.dma_start(out[m * P : (m + 1) * P, c * CHUNK : (c + 1) * CHUNK], total[:, m, :])
 
         def finish_last(lo, hi):
@@ -338,10 +369,18 @@ def tile_list_gmlpt_relu_resL_kernel(
             for h in range(2):
                 if n not in NARROW:
                     product_wide(n, h)
-            for h in range(2):
-                quantise_hid(n, h * CHUNK // 2, (h + 1) * CHUNK // 2)
+            pieces = [(0, CHUNK // 2), (CHUNK // 2, CHUNK)]
+            if n in POOLED:
+                pieces = [(SUB, 2 * SUB), (0, SUB), (2 * SUB, CHUNK)]
+            for lo, hi in pieces:
+                quantise_hid(n, lo, hi)
             if n == 1:
                 quantise_wd()
+            if n == 0:
+                last_scales()
+            if n == 1:
+                gather_words(LAST)
+                part_words(LAST)
             for job, (step, h) in RES_AFTER.items():
                 if step == n:
                     gather_res(job[0], job[1])

@@ -26,6 +26,7 @@ RUN = 8
 CHUNK = 512
 CHUNKS = J // CHUNK
 LAST = CHUNKS - 1
+HALF = CHUNK // 2
 SUB = CHUNK // PACK
 STEPS = CHUNKS * HALVES
 OUT_TILES = N // P
@@ -37,10 +38,9 @@ BANKS = 8
 ALIGN = 64
 LIVE = 96
 DEPTH = 3
-DOWN_AFTER = {2: 0, 4: 1, 6: 2}
-RES_AFTER = {(2, 0): (1, 1), (3, 0): (3, 1), (2, 1): (3, 0), (3, 1): (5, 0)}
-NARROW = (1, 3, 5, 7)
-POOLED = (1, 3, 5)
+MX_DEPTH = 4
+FUSED = 2
+WARM_PASSES = 7
 
 
 def tile_list_gmlpt_relu_resL_kernel(
@@ -56,11 +56,12 @@ def tile_list_gmlpt_relu_resL_kernel(
         def held(shape, dtype, name, tag=None):
             return keep.tile(shape, dtype, name=name, tag=tag or name, align_bytes=ALIGN)
 
-        used = []
+        banks_taken = []
 
         def next_bank():
-            used.append(0)
-            return psum.tile([P, CHUNK], F32, name="bank%d" % len(used), tag="bank%d" % (len(used) % BANKS))
+            banks_taken.append(True)
+            count = len(banks_taken)
+            return psum.tile([P, CHUNK], F32, name="bank%d" % count, tag="bank%d" % (count % BANKS))
 
         offsets = lists.tile([P, J // 16], U16, name="offsets")
         nc.sync.dma_start(offsets[:], offs)
@@ -75,22 +76,14 @@ def tile_list_gmlpt_relu_resL_kernel(
             nc.sync.dma_start(w_scale_raw[LIVE + x : P : 2, :, :], w_scales.rearrange("k s c -> s k c").bitcast(I32))
         word_win = held([P, T], I32, "word_win")
         nc.sync.dma_start(word_win[:], tab_words[0].rearrange("p t b -> p (t b)").bitcast(I32))
-        wg_raw = {}
-
-        def load_wg(a, kp, tag):
-            wg_raw[a, kp] = held([P, PASS], I32, "wg_raw%d%d" % (a, kp), tag)
-            nc.sync.dma_start(
-                wg_raw[a, kp][:],
-                wg_words[kp, :, PASS * a : PASS * (a + 1), :].rearrange("p r i -> p (r i)").bitcast(I32),
-            )
-
-        load_wg(0, 0, "wg_raw00")
-        load_wg(0, 1, "wg_raw0")
+        wg_first = [held([P, PASS], I32, "wg_first%d" % kp) for kp in range(K_PASSES)]
+        for kp in range(K_PASSES):
+            nc.sync.dma_start(wg_first[kp][:], wg_words[kp, :, 0:PASS, :].rearrange("p r i -> p (r i)").bitcast(I32))
 
         nc.vector.memset(scale_win[0:LIVE, :], 0)
         planes_a = held([P, 2, W_WORDS + CHUNK_WORDS], I32, "planes_a")
-        planes_b = held([P, 2, W_WORDS + (LAST - 1) * CHUNK_WORDS], I32, "planes_b")
-        planes_c = held([P, 2, CHUNK_WORDS], I32, "planes_c")
+        planes_b = held([P, 2, W_WORDS + CHUNK_WORDS], I32, "planes_b")
+        planes_c = held([P, 2, 2 * CHUNK_WORDS], I32, "planes_c")
         for planes in (planes_a, planes_b, planes_c):
             nc.vector.memset(planes[:], 0)
         warm = keep.tile([P, 2, 8], F32, name="warm")
@@ -100,83 +93,76 @@ def tile_list_gmlpt_relu_resL_kernel(
         def gather_scales(c, dst, count=1):
             nc.vector.tensor_copy(dst, scale_win[:].bitcast(U8).indirect(entries(c, count)))
 
-        def sort_scales(a, staged):
+        def stage_scales(a, picked, staged):
             nc.vector.tensor_copy(
                 staged[LIVE:P, 0:W_WORDS].rearrange("p (k t b e) -> p k t b e", k=K_PASSES, t=PACK, e=RUN // 4),
                 w_scale_raw[LIVE:P, :, PASS // 4 * a : PASS // 4 * (a + 1)].rearrange(
                     "p k (b t e) -> p k t b e", t=PACK, e=RUN // 4
                 ),
             )
+            nc.vector.tensor_copy(staged[LIVE:P, W_WORDS:], picked[LIVE:P, 0:CHUNK].bitcast(I32))
 
         def move_scales(queue, src, dst):
             for quad in range(4):
                 queue.dma_start(dst[32 * quad : 32 * quad + 4, :, :], src[LIVE + 8 * quad : LIVE + 8 * quad + 8, :])
 
         def table_plane(c, kp, lo, hi):
-            if c == 0:
-                return planes_a[:, kp, W_WORDS:].bitcast(U8)[:, lo:hi]
-            if c == LAST:
-                return planes_c[:, kp, :].bitcast(U8)[:, lo:hi]
-            return planes_b[:, kp, W_WORDS:].bitcast(U8)[:, (c - 1) * CHUNK + lo : (c - 1) * CHUNK + hi]
+            if c < HALVES:
+                return (planes_a, planes_b)[c][:, kp, W_WORDS:].bitcast(U8)[:, lo:hi]
+            return planes_c[:, kp, :].bitcast(U8)[:, (c - HALVES) * CHUNK + lo : (c - HALVES) * CHUNK + hi]
 
         def weight_plane(x, kp, a, t):
             at = (kp * PACK + t) * (P // 4)
             return (planes_a, planes_b)[a][:, x, at : at + P // 4].bitcast(U8)
 
-        both, table = {}, {}
+        both, table, wg_sorted = {}, {}, {}
 
-        def gather_words(c):
-            both[c] = held([P, CHUNK], U32, "both%d" % c, ("both0", "wg_raw0", "picked_a", "hid10")[c])
+        def gather_words(c, tag):
+            both[c] = held([P, CHUNK], U32, "both%d" % c, tag)
             nc.vector.tensor_copy(both[c][:], word_win[:].bitcast(U32).indirect(entries(c)))
 
+        def by_pass(c):
+            return both[c][:].bitcast(U16).rearrange("p (j d) -> p d j", d=K_PASSES)
+
         def part_words(c):
-            table[c] = held([P, K_PASSES, 2 * CHUNK], U8, "parted%d" % c)
-            nc.vector.tensor_copy(
-                table[c][:].bitcast(U16), both[c][:].bitcast(U16).rearrange("p (j d) -> p d j", d=K_PASSES)
-            )
-
-        wg_sorted = {}
-
-        def sort_wg(a):
-            wg_sorted[a] = held([P, PACK, K_PASSES, P], I32, "wg_sorted%d" % a)
-            if a == 1:
-                nc.vector.tensor_copy(
-                    wg_sorted[a][:].rearrange("p t k (b e) -> p t (k b) e", e=RUN),
-                    wg_raw[a][:].rearrange("p k (b t e) -> p t (k b) e", t=PACK, e=RUN),
-                )
-                return
+            parted = held([P, K_PASSES, 2 * CHUNK], U8, "parted%d" % c)
+            nc.vector.tensor_copy(parted[:].bitcast(U16), by_pass(c))
             for kp in range(K_PASSES):
-                nc.vector.tensor_copy(
-                    wg_sorted[a][:, :, kp, :].rearrange("p t (b e) -> p t b e", e=RUN),
-                    wg_raw[a, kp][:].rearrange("p (b t e) -> p t b e", t=PACK, e=RUN),
-                )
+                table[c, kp] = parted[:, kp, :]
 
-        wu_all = held([P, PACK, K_PASSES, HALVES, P // 2], I32, "wu_sorted")
-
-        def sort_wu():
+        def first_operands(kp):
+            ordered = held([P, PACK, P], I32, "wg_sorted0%d" % kp)
             nc.vector.tensor_copy(
-                wu_all[:].rearrange("p t k a (b e) -> p t (k a b) e", e=RUN // 2),
-                wu_raw[:].rearrange("p k (g t e) -> p t (k g) e", t=PACK, e=RUN // 2),
+                ordered[:].rearrange("p t (b e) -> p t b e", e=RUN),
+                wg_first[kp][:].rearrange("p (b t e) -> p t b e", t=PACK, e=RUN),
             )
+            wg_sorted[0, kp] = ordered[:]
+            parted = held([P, 2 * CHUNK], U8, "parted0%d" % kp)
+            nc.vector.tensor_copy(parted[:].bitcast(U16), by_pass(0)[:, kp, :])
+            table[0, kp] = parted[:]
 
+        wu_sorted = held([P, PACK, K_PASSES, HALVES, P // 2], I32, "wu_sorted")
         picked_a = held([P, CHUNK], U8, "picked_a")
         staged_a = held([P, W_WORDS + CHUNK_WORDS], I32, "staged_a")
         gather_scales(0, picked_a[:])
-        sort_scales(0, staged_a)
-        nc.vector.tensor_copy(staged_a[LIVE:P, W_WORDS:], picked_a[LIVE:P, :].bitcast(I32))
+        stage_scales(0, picked_a, staged_a)
         move_scales(nc.scalar, staged_a, planes_a)
         wu_raw = held([P, K_PASSES, R // 2], I32, "wu_raw", "picked_a")
         nc.sync.dma_start(wu_raw[:], wu_words.rearrange("k p c -> p k c").bitcast(I32))
-        wg_raw[1] = held([P, K_PASSES, PASS], I32, "wg_raw1", "staged_a")
-        nc.sync.dma_start(wg_raw[1][:], wg_words[:, :, PASS:, :].rearrange("k p r i -> p k (r i)").bitcast(I32))
-        gather_words(0)
-        sort_wg(0)
-        part_words(0)
-        sort_wu()
-        picked_b = held([P, (LAST - 1) * CHUNK], U8, "picked_b")
-        staged_b = held([P, W_WORDS + (LAST - 1) * CHUNK_WORDS], I32, "staged_b")
-        gather_scales(1, picked_b[:], LAST - 1)
-        for w in range(6):
+        wg_second = held([P, K_PASSES, PASS], I32, "wg_second", "staged_a")
+        nc.sync.dma_start(wg_second[:], wg_words[:, :, PASS:, :].rearrange("k p r i -> p k (r i)").bitcast(I32))
+        gather_words(0, "both0")
+        for kp in range(K_PASSES):
+            first_operands(kp)
+        nc.vector.tensor_copy(
+            wu_sorted[:].rearrange("p t k a (b e) -> p t (k a b) e", e=RUN // 2),
+            wu_raw[:].rearrange("p k (g t e) -> p t (k g) e", t=PACK, e=RUN // 2),
+        )
+        picked_b = held([P, 2 * CHUNK], U8, "picked_b")
+        staged_b = held([P, W_WORDS + CHUNK_WORDS], I32, "staged_b")
+        nc.vector.memset(picked_b[:, CHUNK:].bitcast(I32), 0)
+        gather_scales(1, picked_b[:, 0:CHUNK])
+        for w in range(WARM_PASSES):
             nc.tensor.matmul_mx(
                 out=next_bank()[:],
                 lhsT=picked_b[:, 0 : 2 * P].bitcast(FP4X4),
@@ -186,8 +172,7 @@ def tile_list_gmlpt_relu_resL_kernel(
                 start=True,
                 stop=True,
             )
-        sort_scales(1, staged_b)
-        nc.vector.tensor_copy(staged_b[LIVE:P, W_WORDS:], picked_b[LIVE:P, :].bitcast(I32))
+        stage_scales(1, picked_b, staged_b)
         move_scales(nc.scalar, staged_b, planes_b)
 
         wd_raw = held([P, HALVES, PACK, N], F32, "wd_raw", "picked_b")
@@ -197,56 +182,67 @@ def tile_list_gmlpt_relu_resL_kernel(
                 nc.sync.dma_start(wd_raw[:, a, t, :], wd_rows[a, t])
         res_win = {}
 
-        def load_res(m, tag):
-            res_win[m] = held([P, T], F32, "res_win%d" % m, tag)
+        def load_res(m):
+            res_win[m] = held([P, T], F32, "res_win%d" % m, "wg_first%d" % m)
             nc.sync.dma_start(res_win[m][:], rT[m * P : (m + 1) * P, :])
 
-        gather_words(1)
-        sort_wg(1)
+        gather_words(1, "wg_first1")
+        ordered = held([P, PACK, K_PASSES, P], I32, "wg_sorted1")
+        nc.vector.tensor_copy(
+            ordered[:].rearrange("p t k (b e) -> p t (k b) e", e=RUN),
+            wg_second[:].rearrange("p k (b t e) -> p t (k b) e", t=PACK, e=RUN),
+        )
+        for kp in range(K_PASSES):
+            wg_sorted[1, kp] = ordered[:, :, kp, :]
         part_words(1)
-        load_res(0, "wg_raw00")
-        gather_words(2)
+        load_res(0)
+        gather_words(2, "picked_a")
+        picked_c = held([P, 2 * CHUNK], U8, "picked_c", "staged_a")
+        gather_scales(2, picked_c[:], 2)
         part_words(2)
-        load_res(1, "wg_raw0")
+        load_res(1)
+        move_scales(nc.sync, picked_c[:].bitcast(I32), planes_c)
 
-        def last_scales():
-            picked_c = held([P, CHUNK], U8, "picked_c", "hid00")
-            gather_scales(LAST, picked_c[:])
-            move_scales(nc.sync, picked_c[:].bitcast(I32), planes_c)
+        relu_g, up_copy, hid, hid_mx, res, y = {}, {}, {}, {}, {}, {}
 
-        relu_g, up_copy, hid, hid_mx, res = {}, {}, {}, {}, {}
+        def hid_tag(n, h):
+            return "hid%d%d" % (n, h)
 
-        def first_products(bank, x, n, t, lo, hi):
+        def first_products(acc, x, n, t, lo, hi, passes=range(K_PASSES)):
             c, a = divmod(n, HALVES)
-            for kp in range(K_PASSES):
+            for kp in passes:
                 nc.tensor.matmul_mx(
-                    out=bank,
-                    lhsT=(wg_sorted[a][:, t, kp, :].bitcast(FP8X4), wu_all[:, t, kp, a, :].bitcast(FP4X4))[x],
+                    out=acc,
+                    lhsT=(wg_sorted[a, kp][:, t, :].bitcast(FP8X4), wu_sorted[:, t, kp, a, :].bitcast(FP4X4))[x],
                     lhsT_scale=weight_plane(x, kp, a, t),
-                    rhs=table[c][:, kp, 2 * lo : 2 * hi].bitcast(FP4X4),
+                    rhs=table[c, kp][:, 2 * lo : 2 * hi].bitcast(FP4X4),
                     rhs_scale=table_plane(c, kp, lo, hi),
                     start=(kp == 0),
                     stop=(kp == K_PASSES - 1),
                 )
 
-        def gate(n, t):
-            if t == 0:
-                relu_g[n] = ring.tile([P, PACK, CHUNK], F32, name="relu_g", bufs=DEPTH)
-            bank = next_bank()
-            first_products(bank[:], 0, n, t, 0, CHUNK)
-            nc.scalar.activation(relu_g[n][:, t, :], bank[:], RELU)
+        def gate(n):
+            if n == 0:
+                opened = [next_bank() for t in range(PACK)]
+                for t in range(PACK):
+                    first_products(opened[t][:], 0, n, t, 0, CHUNK, [0])
+            relu_g[n] = ring.tile([P, PACK, CHUNK], F32, name="relu_g", bufs=DEPTH)
+            for t in range(PACK):
+                bank = opened[t] if n == 0 else next_bank()
+                first_products(bank[:], 0, n, t, 0, CHUNK, [1] if n == 0 else range(K_PASSES))
+                nc.scalar.activation(relu_g[n][:, t, :], bank[:], RELU)
 
-        def up_wide(n, t):
-            if t == 0:
-                up_copy[n] = ring.tile([P, PACK, CHUNK], F32, name="up_copy", bufs=DEPTH)
-            bank = next_bank()
-            first_products(bank[:], 1, n, t, 0, CHUNK)
-            nc.scalar.copy(up_copy[n][:, t, :], bank[:])
+        def up_wide(n):
+            up_copy[n] = ring.tile([P, PACK, CHUNK], F32, name="up_copy", bufs=DEPTH)
+            for t in range(PACK):
+                bank = next_bank()
+                first_products(bank[:], 1, n, t, 0, CHUNK)
+                nc.scalar.copy(up_copy[n][:, t, :], bank[:])
 
-        def product(n, h, lo, hi, up_values):
+        def product(n, lo, hi, up_values):
+            h, at = lo // HALF, lo // HALF * HALF
             if (n, h) not in hid:
-                hid[n, h] = held([P, CHUNK // 2, PACK], BF16, "hid%d%d" % (n, h))
-            at = h * CHUNK // 2
+                hid[n, h] = held([P, HALF, PACK], BF16, hid_tag(n, h))
             nc.vector.tensor_tensor(
                 hid[n, h][:, lo - at : hi - at, :].rearrange("p (g i) t -> p g t i", i=PAIR),
                 up_values.rearrange("p t (g i) -> p g t i", i=PAIR),
@@ -254,24 +250,25 @@ def tile_list_gmlpt_relu_resL_kernel(
                 MULT,
             )
 
-        def product_wide(n, h):
-            lo, hi = h * CHUNK // 2, (h + 1) * CHUNK // 2
-            product(n, h, lo, hi, up_copy[n][:, :, lo:hi])
+        def up_quarter(n, s):
+            bank = next_bank()
+            places = bank[:].rearrange("p (t j) -> p t j", t=PACK)
+            for t in range(PACK):
+                first_products(places[:, t, :], 1, n, t, SUB * s, SUB * (s + 1))
+            return places
 
         def up_narrow(n, s):
-            bank = next_bank()
-            quarters = bank[:].rearrange("p (t j) -> p t j", t=PACK)
-            for t in range(PACK):
-                first_products(quarters[:, t, :], 1, n, t, SUB * s, SUB * (s + 1))
-            if n in POOLED and s == 0:
-                copied = held([P, SUB, PACK], F32, "up_quarter%d" % n)
-                nc.scalar.copy(copied[:], quarters.rearrange("p t j -> p j t"))
-                hid[n, 2] = held([P, SUB, PACK], BF16, "hid%d2" % n, "y%d1" % DOWN_AFTER[n - 1] if n > 1 else "hid01")
-                nc.gpsimd.tensor_tensor(
-                    hid[n, 2][:], copied[:], relu_g[n][:, :, 0:SUB].rearrange("p t j -> p j t"), MULT
-                )
-            else:
-                product(n, s // 2, SUB * s, SUB * (s + 1), quarters)
+            product(n, SUB * s, SUB * (s + 1), up_quarter(n, s))
+
+        def up_pooled(n):
+            places = up_quarter(n, 0)
+            copied = held([P, SUB, PACK], F32, "up_quarter%d" % n)
+            nc.scalar.copy(copied[:], places.rearrange("p t j -> p j t"))
+            after = hid_tag(0, 1) if n == 1 else "y%d1" % (n // HALVES - 1)
+            hid[n, "pool"] = held([P, SUB, PACK], BF16, "hid_pool%d" % n, after)
+            nc.gpsimd.tensor_tensor(
+                hid[n, "pool"][:], copied[:], relu_g[n][:, :, 0:SUB].rearrange("p t j -> p j t"), MULT
+            )
 
         wd_codes = held([P, HALVES, N], U32, "wd_codes")
         wd_scales = held([P, HALVES, N], U8, "wd_scales")
@@ -283,27 +280,18 @@ def tile_list_gmlpt_relu_resL_kernel(
                 wd_raw[:, a].rearrange("p t (g i) -> p g t i", i=LINE),
             )
 
-        def quantise_wd():
-            nc.vector.quantize_mx(
-                out=wd_codes[:].rearrange("p a n -> p (a n)").bitcast(FP8X4),
-                scales=wd_scales[:].rearrange("p a n -> p (a n)"),
-                in_=wd_bf[:].rearrange("p a n t -> p (a n t)"),
-            )
-
         def quantise_hid(n, lo, hi):
             if n not in hid_mx:
-                codes = ring.tile([P, CHUNK], U32, name="hid_codes", align_bytes=ALIGN, bufs=4)
-                scales = ring.tile([P, CHUNK], U8, name="hid_scales", align_bytes=ALIGN, bufs=4)
+                codes = ring.tile([P, CHUNK], U32, name="hid_codes", align_bytes=ALIGN, bufs=MX_DEPTH)
+                scales = ring.tile([P, CHUNK], U8, name="hid_scales", align_bytes=ALIGN, bufs=MX_DEPTH)
                 hid_mx[n] = (codes, scales)
             codes, scales = hid_mx[n]
-            h = lo // (CHUNK // 2)
-            at = h * CHUNK // 2
-            if n in POOLED and lo == 0:
-                h = 2
+            h, at = lo // HALF, lo // HALF * HALF
+            values = hid[n, "pool"] if lo == 0 and (n, "pool") in hid else hid[n, h]
             nc.vector.quantize_mx(
                 out=codes[:, lo:hi].bitcast(FP8X4),
                 scales=scales[:, lo:hi],
-                in_=hid[n, h][:, lo - at : hi - at, :].rearrange("p j t -> p (j t)"),
+                in_=values[:, lo - at : hi - at, :].rearrange("p j t -> p (j t)"),
             )
 
         def down(c, m, lo, hi, acc):
@@ -319,14 +307,23 @@ def tile_list_gmlpt_relu_resL_kernel(
                     stop=(a == HALVES - 1),
                 )
 
-        def gather_res(c, m):
-            picked = held([P, CHUNK], F32, "res%d%d" % (c, m), "hid%d%d" % RES_AFTER[c, m])
-            nc.vector.tensor_copy(picked[:], res_win[m][:].indirect(entries(c)))
-            res[c, m] = picked[:]
+        def gather_res(c, m, dst):
+            res[c, m] = dst
+            nc.vector.tensor_copy(dst, res_win[m][:].indirect(entries(c)))
 
-        y = {}
+        def look_ahead(n):
+            if n == 1:
+                gather_words(LAST, hid_tag(n, 0))
+                part_words(LAST)
+                gather_res(FUSED, 0, held([P, CHUNK], F32, "res20", hid_tag(n, 1))[:])
+            if n == 3:
+                gather_res(FUSED, 1, held([P, CHUNK], F32, "res21", hid_tag(n, 0))[:])
+            if n == 5:
+                res[LAST] = held([P, OUT_TILES, CHUNK], F32, "res_last", hid_tag(n, 0))
+                for m in range(OUT_TILES):
+                    gather_res(LAST, m, res[LAST][:, m, :])
 
-        def finish(c):
+        def last_product(c):
             for m in range(OUT_TILES):
                 bank = next_bank()
                 down(c, m, 0, CHUNK, bank[:])
@@ -334,12 +331,12 @@ def tile_list_gmlpt_relu_resL_kernel(
                 nc.scalar.copy(y[c, m][:], bank[:])
 
         def add_res(c, n):
-            total = held([P, OUT_TILES, CHUNK], F32, "total%d" % c, "hid%d%d" % (n, (c, 0) in RES_AFTER))
+            total = held([P, OUT_TILES, CHUNK], F32, "total%d" % c, hid_tag(n, 0 if c < FUSED else 1))
             for m in range(OUT_TILES):
-                if (c, m) in RES_AFTER:
-                    nc.gpsimd.tensor_tensor(total[:, m, :], y[c, m][:], res[c, m], ADD)
-                else:
+                if c < FUSED:
                     nc.vector.tensor_tensor(total[:, m, :], res_win[m][:].indirect(entries(c)), y[c, m][:], ADD)
+                else:
+                    nc.gpsimd.tensor_tensor(total[:, m, :], y[c, m][:], res[c, m], ADD)
                 nc.sync.dma_start(out[m * P : (m + 1) * P, c * CHUNK : (c + 1) * CHUNK], total[:, m, :])
 
         def finish_last(lo, hi):
@@ -348,54 +345,55 @@ def tile_list_gmlpt_relu_resL_kernel(
             for m in range(OUT_TILES):
                 down(LAST, m, lo, hi, acc[:, m, :])
             total = held([P, OUT_TILES, hi - lo], F32, "total_last%d" % lo)
-            for m in range(OUT_TILES):
-                nc.vector.tensor_tensor(total[:, m, :], acc[:, m, :], res[LAST, m][:, lo:hi], ADD)
+            nc.vector.tensor_tensor(total[:], acc, res[LAST][:, :, lo:hi], ADD)
             nc.sync.dma_start(
                 out.rearrange("(m p) j -> p m j", p=P)[:, :, LAST * CHUNK + lo : LAST * CHUNK + hi], total[:]
             )
 
-        for n in range(STEPS - 1):
-            for t in range(PACK):
-                gate(n, t)
-            for t in range(PACK):
-                if n in NARROW:
-                    up_narrow(n, t)
-                else:
-                    up_wide(n, t)
-            if n < HALVES:
-                cast_wd(n)
-            if n in DOWN_AFTER:
-                finish(DOWN_AFTER[n])
-            for h in range(2):
-                if n not in NARROW:
-                    product_wide(n, h)
-            pieces = [(0, CHUNK // 2), (CHUNK // 2, CHUNK)]
-            if n in POOLED:
-                pieces = [(SUB, 2 * SUB), (0, SUB), (2 * SUB, CHUNK)]
-            for lo, hi in pieces:
+        def wide_step(n):
+            c = n // HALVES
+            gate(n)
+            up_wide(n)
+            if c == 0:
+                cast_wd(0)
+            else:
+                last_product(c - 1)
+            for lo in (0, HALF):
+                product(n, lo, lo + HALF, up_copy[n][:, :, lo : lo + HALF])
+            for lo in (0, HALF):
+                quantise_hid(n, lo, lo + HALF)
+            if c > 0:
+                add_res(c - 1, n)
+
+        def narrow_step(n):
+            gate(n)
+            up_pooled(n)
+            for s in range(1, PACK):
+                up_narrow(n, s)
+            if n == 1:
+                cast_wd(1)
+            for lo, hi in ((SUB, HALF), (0, SUB), (HALF, CHUNK)):
                 quantise_hid(n, lo, hi)
             if n == 1:
-                quantise_wd()
-            if n == 0:
-                last_scales()
-            if n == 1:
-                gather_words(LAST)
-                part_words(LAST)
-            for job, (step, h) in RES_AFTER.items():
-                if step == n:
-                    gather_res(job[0], job[1])
-            if n in DOWN_AFTER:
-                add_res(DOWN_AFTER[n], n)
+                nc.vector.quantize_mx(
+                    out=wd_codes[:].rearrange("p a n -> p (a n)").bitcast(FP8X4),
+                    scales=wd_scales[:].rearrange("p a n -> p (a n)"),
+                    in_=wd_bf[:].rearrange("p a n t -> p (a n t)"),
+                )
+            look_ahead(n)
+
+        for c in range(LAST):
+            wide_step(HALVES * c)
+            narrow_step(HALVES * c + 1)
+        wide_step(STEPS - 2)
         n = STEPS - 1
-        for t in range(PACK):
-            gate(n, t)
-        up_narrow(n, 0)
-        up_narrow(n, 1)
-        up_narrow(n, 2)
-        quantise_hid(n, 0, 2 * SUB)
-        up_narrow(n, 3)
-        quantise_hid(n, 2 * SUB, 3 * SUB)
-        finish_last(0, 2 * SUB)
-        quantise_hid(n, 3 * SUB, CHUNK)
-        finish_last(2 * SUB, 3 * SUB)
-        finish_last(3 * SUB, CHUNK)
+        gate(n)
+        for s in range(PACK - 1):
+            up_narrow(n, s)
+        quantise_hid(n, 0, HALF)
+        up_narrow(n, PACK - 1)
+        quantise_hid(n, HALF, HALF + SUB)
+        finish_last(0, HALF)
+        quantise_hid(n, HALF + SUB, CHUNK)
+        finish_last(HALF, HALF + SUB)
+        finish_last(HALF + SUB, CHUNK)

@@ -35,12 +35,11 @@ PAIR = 2
 W_WORDS = K_PASSES * PASS // 4
 CHUNK_WORDS = CHUNK // 4
 BANKS = 8
+RES_BEHIND = {0: [(0, 0)], 1: [(1, 0)], 2: [(0, 1)], 3: [(1, 1), (2, 0)], 4: [(2, 1)]}
 ALIGN = 64
 LIVE = 96
 DEPTH = 3
 MX_DEPTH = 4
-FUSED = 2
-WARM_PASSES = 7
 
 
 def tile_list_gmlpt_relu_resL_kernel(
@@ -158,22 +157,13 @@ def tile_list_gmlpt_relu_resL_kernel(
             wu_sorted[:].rearrange("p t k a (b e) -> p t (k a b) e", e=RUN // 2),
             wu_raw[:].rearrange("p k (g t e) -> p t (k g) e", t=PACK, e=RUN // 2),
         )
-        picked_b = held([P, 2 * CHUNK], U8, "picked_b")
+        picked_b = held([P, CHUNK], U8, "picked_b")
         staged_b = held([P, W_WORDS + CHUNK_WORDS], I32, "staged_b")
-        nc.vector.memset(picked_b[:, CHUNK:].bitcast(I32), 0)
-        gather_scales(1, picked_b[:, 0:CHUNK])
-        for w in range(WARM_PASSES):
-            nc.tensor.matmul_mx(
-                out=next_bank()[:],
-                lhsT=picked_b[:, 0 : 2 * P].bitcast(FP4X4),
-                lhsT_scale=picked_b[:, 0:P],
-                rhs=picked_b[:].bitcast(FP4X4),
-                rhs_scale=picked_b[:, 0:CHUNK],
-                start=True,
-                stop=True,
-            )
+        gather_scales(1, picked_b[:])
         stage_scales(1, picked_b, staged_b)
         move_scales(nc.scalar, staged_b, planes_b)
+        picked_c = held([P, 2 * CHUNK], U8, "picked_c")
+        gather_scales(2, picked_c[:], 2)
 
         wd_raw = held([P, HALVES, PACK, N], F32, "wd_raw", "picked_b")
         wd_rows = wd.rearrange("(a b t q) n -> a t b q n", a=HALVES, t=PACK, q=RUN)
@@ -197,11 +187,11 @@ def tile_list_gmlpt_relu_resL_kernel(
         part_words(1)
         load_res(0)
         gather_words(2, "picked_a")
-        picked_c = held([P, 2 * CHUNK], U8, "picked_c", "staged_a")
-        gather_scales(2, picked_c[:], 2)
         part_words(2)
         load_res(1)
         move_scales(nc.sync, picked_c[:].bitcast(I32), planes_c)
+        gather_words(LAST, "staged_b")
+        part_words(LAST)
 
         relu_g, up_copy, hid, hid_mx, res, y = {}, {}, {}, {}, {}, {}
 
@@ -250,25 +240,12 @@ def tile_list_gmlpt_relu_resL_kernel(
                 MULT,
             )
 
-        def up_quarter(n, s):
+        def up_narrow(n, s):
             bank = next_bank()
             places = bank[:].rearrange("p (t j) -> p t j", t=PACK)
             for t in range(PACK):
                 first_products(places[:, t, :], 1, n, t, SUB * s, SUB * (s + 1))
-            return places
-
-        def up_narrow(n, s):
-            product(n, SUB * s, SUB * (s + 1), up_quarter(n, s))
-
-        def up_pooled(n):
-            places = up_quarter(n, 0)
-            copied = held([P, SUB, PACK], F32, "up_quarter%d" % n)
-            nc.scalar.copy(copied[:], places.rearrange("p t j -> p j t"))
-            after = hid_tag(0, 1) if n == 1 else "y%d1" % (n // HALVES - 1)
-            hid[n, "pool"] = held([P, SUB, PACK], BF16, "hid_pool%d" % n, after)
-            nc.gpsimd.tensor_tensor(
-                hid[n, "pool"][:], copied[:], relu_g[n][:, :, 0:SUB].rearrange("p t j -> p j t"), MULT
-            )
+            product(n, SUB * s, SUB * (s + 1), places)
 
         wd_codes = held([P, HALVES, N], U32, "wd_codes")
         wd_scales = held([P, HALVES, N], U8, "wd_scales")
@@ -287,11 +264,10 @@ def tile_list_gmlpt_relu_resL_kernel(
                 hid_mx[n] = (codes, scales)
             codes, scales = hid_mx[n]
             h, at = lo // HALF, lo // HALF * HALF
-            values = hid[n, "pool"] if lo == 0 and (n, "pool") in hid else hid[n, h]
             nc.vector.quantize_mx(
                 out=codes[:, lo:hi].bitcast(FP8X4),
                 scales=scales[:, lo:hi],
-                in_=values[:, lo - at : hi - at, :].rearrange("p j t -> p (j t)"),
+                in_=hid[n, h][:, lo - at : hi - at, :].rearrange("p j t -> p (j t)"),
             )
 
         def down(c, m, lo, hi, acc):
@@ -312,13 +288,9 @@ def tile_list_gmlpt_relu_resL_kernel(
             nc.vector.tensor_copy(dst, res_win[m][:].indirect(entries(c)))
 
         def look_ahead(n):
-            if n == 1:
-                gather_words(LAST, hid_tag(n, 0))
-                part_words(LAST)
-                gather_res(FUSED, 0, held([P, CHUNK], F32, "res20", hid_tag(n, 1))[:])
-            if n == 3:
-                gather_res(FUSED, 1, held([P, CHUNK], F32, "res21", hid_tag(n, 0))[:])
-            if n == 5:
+            for h, (c, m) in enumerate(RES_BEHIND.get(n, [])):
+                gather_res(c, m, held([P, CHUNK], F32, "res%d%d" % (c, m), hid_tag(n, h))[:])
+            if n == STEPS - 3:
                 res[LAST] = held([P, OUT_TILES, CHUNK], F32, "res_last", hid_tag(n, 0))
                 for m in range(OUT_TILES):
                     gather_res(LAST, m, res[LAST][:, m, :])
@@ -331,12 +303,9 @@ def tile_list_gmlpt_relu_resL_kernel(
                 nc.scalar.copy(y[c, m][:], bank[:])
 
         def add_res(c, n):
-            total = held([P, OUT_TILES, CHUNK], F32, "total%d" % c, hid_tag(n, 0 if c < FUSED else 1))
+            total = held([P, OUT_TILES, CHUNK], F32, "total%d" % c, hid_tag(n, 1))
             for m in range(OUT_TILES):
-                if c < FUSED:
-                    nc.vector.tensor_tensor(total[:, m, :], res_win[m][:].indirect(entries(c)), y[c, m][:], ADD)
-                else:
-                    nc.gpsimd.tensor_tensor(total[:, m, :], y[c, m][:], res[c, m], ADD)
+                nc.gpsimd.tensor_tensor(total[:, m, :], y[c, m][:], res[c, m], ADD)
                 nc.sync.dma_start(out[m * P : (m + 1) * P, c * CHUNK : (c + 1) * CHUNK], total[:, m, :])
 
         def finish_last(lo, hi):
@@ -362,18 +331,18 @@ def tile_list_gmlpt_relu_resL_kernel(
                 product(n, lo, lo + HALF, up_copy[n][:, :, lo : lo + HALF])
             for lo in (0, HALF):
                 quantise_hid(n, lo, lo + HALF)
+            look_ahead(n)
             if c > 0:
                 add_res(c - 1, n)
 
         def narrow_step(n):
             gate(n)
-            up_pooled(n)
-            for s in range(1, PACK):
+            for s in range(PACK):
                 up_narrow(n, s)
             if n == 1:
                 cast_wd(1)
-            for lo, hi in ((SUB, HALF), (0, SUB), (HALF, CHUNK)):
-                quantise_hid(n, lo, hi)
+            for lo in (0, HALF):
+                quantise_hid(n, lo, lo + HALF)
             if n == 1:
                 nc.vector.quantize_mx(
                     out=wd_codes[:].rearrange("p a n -> p (a n)").bitcast(FP8X4),

@@ -35,7 +35,6 @@ PAIR = 2
 W_WORDS = K_PASSES * PASS // 4
 CHUNK_WORDS = CHUNK // 4
 BANKS = 8
-RES_BEHIND = {0: [(0, 0)], 1: [(1, 0)], 2: [(0, 1)], 3: [(1, 1), (2, 0)], 4: [(2, 1)]}
 ALIGN = 64
 LIVE = 96
 DEPTH = 3
@@ -49,7 +48,6 @@ def tile_list_gmlpt_relu_resL_kernel(
     with ExitStack() as ctx:
         lists = ctx.enter_context(tc.tile_pool(name="lists", bufs=1))
         keep = ctx.enter_context(tc.tile_pool(name="keep", bufs=1))
-        ring = ctx.enter_context(tc.tile_pool(name="ring", bufs=2))
         psum = ctx.enter_context(tc.psum_pool(name="psum", bufs=1))
 
         def held(shape, dtype, name, tag=None):
@@ -72,19 +70,36 @@ def tile_list_gmlpt_relu_resL_kernel(
         nc.sync.dma_start(scale_win[LIVE:P, :], tab_scales.rearrange("a s t -> s a t").bitcast(I32))
         w_scale_raw = held([P, K_PASSES, R // 4], I32, "w_scale_raw")
         for x, w_scales in enumerate((wg_scales, wu_scales)):
-            nc.sync.dma_start(w_scale_raw[LIVE + x : P : 2, :, :], w_scales.rearrange("k s c -> s k c").bitcast(I32))
+            nc.scalar.dma_start(w_scale_raw[LIVE + x : P : 2, :, :], w_scales.rearrange("k s c -> s k c").bitcast(I32))
         word_win = held([P, T], I32, "word_win")
         nc.sync.dma_start(word_win[:], tab_words[0].rearrange("p t b -> p (t b)").bitcast(I32))
         wg_first = [held([P, PASS], I32, "wg_first%d" % kp) for kp in range(K_PASSES)]
         for kp in range(K_PASSES):
             nc.sync.dma_start(wg_first[kp][:], wg_words[kp, :, 0:PASS, :].rearrange("p r i -> p (r i)").bitcast(I32))
 
+        def load_wu(a):
+            raw = held([P, K_PASSES, PASS // 2], I32, "wu_raw%d" % a)
+            columns = slice(2 * PASS * a, 2 * PASS * (a + 1))
+            nc.sync.dma_start(raw[:], wu_words[:, :, columns].rearrange("k p c -> p k c").bitcast(I32))
+            return raw
+
+        wu_raw = [load_wu(0)]
+        wg_second = held([P, K_PASSES, PASS], I32, "wg_second")
+        nc.sync.dma_start(wg_second[:], wg_words[:, :, PASS:, :].rearrange("k p r i -> p k (r i)").bitcast(I32))
+        wu_raw.append(load_wu(1))
+        wd_raw = [held([P, PACK, N], F32, "wd_raw%d" % a) for a in range(HALVES)]
+        wd_rows = wd.rearrange("(a b t q) n -> a t b q n", a=HALVES, t=PACK, q=RUN)
+        for a in range(HALVES):
+            for t in range(PACK):
+                nc.sync.dma_start(wd_raw[a][:, t, :], wd_rows[a, t])
+        res_win = [held([P, T], F32, "res_win%d" % m) for m in range(OUT_TILES)]
+        for m in range(OUT_TILES):
+            nc.sync.dma_start(res_win[m][:], rT[m * P : (m + 1) * P, :])
+
         nc.vector.memset(scale_win[0:LIVE, :], 0)
-        planes_a = held([P, 2, W_WORDS + CHUNK_WORDS], I32, "planes_a")
-        planes_b = held([P, 2, W_WORDS + CHUNK_WORDS], I32, "planes_b")
-        planes_c = held([P, 2, 2 * CHUNK_WORDS], I32, "planes_c")
-        for planes in (planes_a, planes_b, planes_c):
-            nc.vector.memset(planes[:], 0)
+        planes = [held([P, 2, W_WORDS + CHUNK_WORDS], I32, "planes%d" % a) for a in range(HALVES)]
+        for a in range(HALVES):
+            nc.vector.memset(planes[a][:], 0)
         warm = keep.tile([P, 2, 8], F32, name="warm")
         nc.gpsimd.memset(warm[:, 0, :], 0.0)
         nc.scalar.activation(warm[:, 1, :], warm[:, 0, :], RELU)
@@ -92,29 +107,39 @@ def tile_list_gmlpt_relu_resL_kernel(
         def gather_scales(c, dst, count=1):
             nc.vector.tensor_copy(dst, scale_win[:].bitcast(U8).indirect(entries(c, count)))
 
-        def stage_scales(a, picked, staged):
-            nc.vector.tensor_copy(
-                staged[LIVE:P, 0:W_WORDS].rearrange("p (k t b e) -> p k t b e", k=K_PASSES, t=PACK, e=RUN // 4),
-                w_scale_raw[LIVE:P, :, PASS // 4 * a : PASS // 4 * (a + 1)].rearrange(
-                    "p k (b t e) -> p k t b e", t=PACK, e=RUN // 4
-                ),
-            )
-            nc.vector.tensor_copy(staged[LIVE:P, W_WORDS:], picked[LIVE:P, 0:CHUNK].bitcast(I32))
-
         def move_scales(queue, src, dst):
             for quad in range(4):
                 queue.dma_start(dst[32 * quad : 32 * quad + 4, :, :], src[LIVE + 8 * quad : LIVE + 8 * quad + 8, :])
 
         def table_plane(c, kp, lo, hi):
-            if c < HALVES:
-                return (planes_a, planes_b)[c][:, kp, W_WORDS:].bitcast(U8)[:, lo:hi]
-            return planes_c[:, kp, :].bitcast(U8)[:, (c - HALVES) * CHUNK + lo : (c - HALVES) * CHUNK + hi]
+            return planes[c % 2][:, kp, W_WORDS:].bitcast(U8)[:, lo:hi]
 
         def weight_plane(x, kp, a, t):
             at = (kp * PACK + t) * (P // 4)
-            return (planes_a, planes_b)[a][:, x, at : at + P // 4].bitcast(U8)
+            return planes[a][:, x, at : at + P // 4].bitcast(U8)
 
-        both, table, wg_sorted = {}, {}, {}
+        staged = [held([P, W_WORDS + CHUNK_WORDS], I32, "staged%d" % a) for a in range(HALVES)]
+        for a in range(HALVES):
+            nc.vector.tensor_copy(
+                staged[a][LIVE:P, 0:W_WORDS].rearrange("p (k t b e) -> p k t b e", k=K_PASSES, t=PACK, e=RUN // 4),
+                w_scale_raw[LIVE:P, :, PASS // 4 * a : PASS // 4 * (a + 1)].rearrange(
+                    "p k (b t e) -> p k t b e", t=PACK, e=RUN // 4
+                ),
+            )
+        picked_first = held([P, CHUNK], U8, "picked_first", "picked")
+        gather_scales(0, picked_first[:])
+        nc.vector.tensor_copy(staged[0][LIVE:P, W_WORDS:], picked_first[LIVE:P, :].bitcast(I32))
+        move_scales(nc.scalar, staged[0], planes[0][:])
+        picked_rest = held([P, 2 * CHUNK], U8, "picked_rest", "picked")
+        gather_scales(1, picked_rest[:], 2)
+        picked = {2: picked_rest[:, CHUNK:]}
+        nc.vector.tensor_copy(staged[1][LIVE:P, W_WORDS:], picked_rest[LIVE:P, 0:CHUNK].bitcast(I32))
+        move_scales(nc.scalar, staged[1], planes[1][:])
+
+        def move_late(c):
+            move_scales(nc.sync, picked[c].bitcast(I32), planes[c % 2][:, :, W_WORDS:])
+
+        both, table, wg_sorted, wu_sorted = {}, {}, {}, {}
 
         def gather_words(c, tag):
             both[c] = held([P, CHUNK], U32, "both%d" % c, tag)
@@ -130,52 +155,27 @@ def tile_list_gmlpt_relu_resL_kernel(
                 table[c, kp] = parted[:, kp, :]
 
         def first_operands(kp):
+            parted = held([P, 2 * CHUNK], U8, "parted0%d" % kp)
+            nc.vector.tensor_copy(parted[:].bitcast(U16), by_pass(0)[:, kp, :])
+            table[0, kp] = parted[:]
             ordered = held([P, PACK, P], I32, "wg_sorted0%d" % kp)
             nc.vector.tensor_copy(
                 ordered[:].rearrange("p t (b e) -> p t b e", e=RUN),
                 wg_first[kp][:].rearrange("p (b t e) -> p t b e", t=PACK, e=RUN),
             )
             wg_sorted[0, kp] = ordered[:]
-            parted = held([P, 2 * CHUNK], U8, "parted0%d" % kp)
-            nc.vector.tensor_copy(parted[:].bitcast(U16), by_pass(0)[:, kp, :])
-            table[0, kp] = parted[:]
 
-        wu_sorted = held([P, PACK, K_PASSES, HALVES, P // 2], I32, "wu_sorted")
-        picked_a = held([P, CHUNK], U8, "picked_a")
-        staged_a = held([P, W_WORDS + CHUNK_WORDS], I32, "staged_a")
-        gather_scales(0, picked_a[:])
-        stage_scales(0, picked_a, staged_a)
-        move_scales(nc.scalar, staged_a, planes_a)
-        wu_raw = held([P, K_PASSES, R // 2], I32, "wu_raw", "picked_a")
-        nc.sync.dma_start(wu_raw[:], wu_words.rearrange("k p c -> p k c").bitcast(I32))
-        wg_second = held([P, K_PASSES, PASS], I32, "wg_second", "staged_a")
-        nc.sync.dma_start(wg_second[:], wg_words[:, :, PASS:, :].rearrange("k p r i -> p k (r i)").bitcast(I32))
+        def sort_wu(a):
+            wu_sorted[a] = held([P, PACK, K_PASSES, P // 2], I32, "wu_sorted%d" % a)
+            nc.vector.tensor_copy(
+                wu_sorted[a][:].rearrange("p t k (b e) -> p t (k b) e", e=RUN // 2),
+                wu_raw[a][:].rearrange("p k (b t e) -> p t (k b) e", t=PACK, e=RUN // 2),
+            )
+
         gather_words(0, "both0")
         for kp in range(K_PASSES):
             first_operands(kp)
-        nc.vector.tensor_copy(
-            wu_sorted[:].rearrange("p t k a (b e) -> p t (k a b) e", e=RUN // 2),
-            wu_raw[:].rearrange("p k (g t e) -> p t (k g) e", t=PACK, e=RUN // 2),
-        )
-        picked_b = held([P, CHUNK], U8, "picked_b")
-        staged_b = held([P, W_WORDS + CHUNK_WORDS], I32, "staged_b")
-        gather_scales(1, picked_b[:])
-        stage_scales(1, picked_b, staged_b)
-        move_scales(nc.scalar, staged_b, planes_b)
-        picked_c = held([P, 2 * CHUNK], U8, "picked_c")
-        gather_scales(2, picked_c[:], 2)
-
-        wd_raw = held([P, HALVES, PACK, N], F32, "wd_raw", "picked_b")
-        wd_rows = wd.rearrange("(a b t q) n -> a t b q n", a=HALVES, t=PACK, q=RUN)
-        for a in range(HALVES):
-            for t in range(PACK):
-                nc.sync.dma_start(wd_raw[:, a, t, :], wd_rows[a, t])
-        res_win = {}
-
-        def load_res(m):
-            res_win[m] = held([P, T], F32, "res_win%d" % m, "wg_first%d" % m)
-            nc.sync.dma_start(res_win[m][:], rT[m * P : (m + 1) * P, :])
-
+        sort_wu(0)
         gather_words(1, "wg_first1")
         ordered = held([P, PACK, K_PASSES, P], I32, "wg_sorted1")
         nc.vector.tensor_copy(
@@ -185,25 +185,19 @@ def tile_list_gmlpt_relu_resL_kernel(
         for kp in range(K_PASSES):
             wg_sorted[1, kp] = ordered[:, :, kp, :]
         part_words(1)
-        load_res(0)
-        gather_words(2, "picked_a")
-        part_words(2)
-        load_res(1)
-        move_scales(nc.sync, picked_c[:].bitcast(I32), planes_c)
-        gather_words(LAST, "staged_b")
-        part_words(LAST)
+        sort_wu(1)
 
-        relu_g, up_copy, hid, hid_mx, res, y = {}, {}, {}, {}, {}, {}
+        relu_g, pairs, hid, hid_mx, res, y, total = {}, {}, {}, {}, {}, {}, {}
 
-        def hid_tag(n, h):
-            return "hid%d%d" % (n, h)
+        def relu_tag(n, u):
+            return "relu%d%d" % (n if (n, u) in ((1, 0), (5, 0)) else (n + 1) % DEPTH + 6, u)
 
         def first_products(acc, x, n, t, lo, hi, passes=range(K_PASSES)):
             c, a = divmod(n, HALVES)
             for kp in passes:
                 nc.tensor.matmul_mx(
                     out=acc,
-                    lhsT=(wg_sorted[a, kp][:, t, :].bitcast(FP8X4), wu_sorted[:, t, kp, a, :].bitcast(FP4X4))[x],
+                    lhsT=(wg_sorted[a, kp][:, t, :].bitcast(FP8X4), wu_sorted[a][:, t, kp, :].bitcast(FP4X4))[x],
                     lhsT_scale=weight_plane(x, kp, a, t),
                     rhs=table[c, kp][:, 2 * lo : 2 * hi].bitcast(FP4X4),
                     rhs_scale=table_plane(c, kp, lo, hi),
@@ -216,28 +210,38 @@ def tile_list_gmlpt_relu_resL_kernel(
                 opened = [next_bank() for t in range(PACK)]
                 for t in range(PACK):
                     first_products(opened[t][:], 0, n, t, 0, CHUNK, [0])
-            relu_g[n] = ring.tile([P, PACK, CHUNK], F32, name="relu_g", bufs=DEPTH)
+            shape = [P, PACK, CHUNK] if n == STEPS - 1 else [P, PAIR, CHUNK]
             for t in range(PACK):
+                u, at = divmod(t, shape[1])
+                if at == 0:
+                    relu_g[n, u] = held(shape, F32, "relu_g%d%d" % (n, u), "relu_last" if n == STEPS - 1 else relu_tag(n, u))
                 bank = opened[t] if n == 0 else next_bank()
                 first_products(bank[:], 0, n, t, 0, CHUNK, [1] if n == 0 else range(K_PASSES))
-                nc.scalar.activation(relu_g[n][:, t, :], bank[:], RELU)
+                nc.scalar.activation(relu_g[n, u][:, at, :], bank[:], RELU)
 
-        def up_wide(n):
-            up_copy[n] = ring.tile([P, PACK, CHUNK], F32, name="up_copy", bufs=DEPTH)
-            for t in range(PACK):
-                bank = next_bank()
-                first_products(bank[:], 1, n, t, 0, CHUNK)
-                nc.scalar.copy(up_copy[n][:, t, :], bank[:])
+        behind = {1: relu_tag(0, 0), 3: "y1", 4: relu_tag(3, 0), 5: "y1"}
 
-        def product(n, lo, hi, up_values):
-            h, at = lo // HALF, lo // HALF * HALF
-            if (n, h) not in hid:
-                hid[n, h] = held([P, HALF, PACK], BF16, hid_tag(n, h))
+        def up_pair(n, h, u):
+            if u == 0:
+                tag = behind[n] if h == 0 and n in behind else "pairs%d%d" % (n % 2, h)
+                pairs[n, h] = held([P, PAIR, HALF, PAIR], BF16, "pairs%d%d" % (n, h), tag)
+            bank = next_bank()
+            places = bank[:].rearrange("p (t j) -> p t j", t=PAIR)
+            for t in range(PAIR):
+                first_products(places[:, t, :], 1, n, PAIR * u + t, HALF * h, HALF * (h + 1))
             nc.vector.tensor_tensor(
-                hid[n, h][:, lo - at : hi - at, :].rearrange("p (g i) t -> p g t i", i=PAIR),
-                up_values.rearrange("p t (g i) -> p g t i", i=PAIR),
-                relu_g[n][:, :, lo:hi].rearrange("p t (g i) -> p g t i", i=PAIR),
+                pairs[n, h][:, u],
+                places.rearrange("p t j -> p j t"),
+                relu_g[n, u][:, :, HALF * h : HALF * (h + 1)].rearrange("p t j -> p j t"),
                 MULT,
+            )
+
+        def merge(n, h):
+            tag = "wd_raw%d" % n if n < HALVES and h == 0 else "hid%d%d" % (n % 2, h)
+            hid[n, h] = held([P, HALF, PACK], BF16, "hid%d%d" % (n, h), tag)
+            nc.scalar.copy(
+                hid[n, h][:].rearrange("p j t -> p (j t)").bitcast(U32).rearrange("p (j u) -> p j u", u=PAIR),
+                pairs[n, h][:].rearrange("p u j t -> p u (j t)").bitcast(U32).rearrange("p u j -> p j u"),
             )
 
         def up_narrow(n, s):
@@ -245,7 +249,13 @@ def tile_list_gmlpt_relu_resL_kernel(
             places = bank[:].rearrange("p (t j) -> p t j", t=PACK)
             for t in range(PACK):
                 first_products(places[:, t, :], 1, n, t, SUB * s, SUB * (s + 1))
-            product(n, SUB * s, SUB * (s + 1), places)
+            hid[n, s] = held([P, SUB, PACK], BF16, "hid_last%d" % s)
+            nc.vector.tensor_tensor(
+                hid[n, s][:].rearrange("p (g i) t -> p g t i", i=PAIR),
+                places.rearrange("p t (g i) -> p g t i", i=PAIR),
+                relu_g[n, 0][:, :, SUB * s : SUB * (s + 1)].rearrange("p t (g i) -> p g t i", i=PAIR),
+                MULT,
+            )
 
         wd_codes = held([P, HALVES, N], U32, "wd_codes")
         wd_scales = held([P, HALVES, N], U8, "wd_scales")
@@ -254,20 +264,19 @@ def tile_list_gmlpt_relu_resL_kernel(
         def cast_wd(a):
             nc.scalar.copy(
                 wd_bf[:, a].rearrange("p (g i) t -> p g t i", i=LINE),
-                wd_raw[:, a].rearrange("p t (g i) -> p g t i", i=LINE),
+                wd_raw[a][:].rearrange("p t (g i) -> p g t i", i=LINE),
             )
 
-        def quantise_hid(n, lo, hi):
-            if n not in hid_mx:
-                codes = ring.tile([P, CHUNK], U32, name="hid_codes", align_bytes=ALIGN, bufs=MX_DEPTH)
-                scales = ring.tile([P, CHUNK], U8, name="hid_scales", align_bytes=ALIGN, bufs=MX_DEPTH)
+        def quantise(n, part, lo, hi):
+            if lo == 0:
+                codes = held([P, CHUNK], U32, "codes%d" % n, "codes%d" % (n % MX_DEPTH))
+                scales = held([P, CHUNK], U8, "scales%d" % n, "scales%d" % (n % MX_DEPTH))
                 hid_mx[n] = (codes, scales)
             codes, scales = hid_mx[n]
-            h, at = lo // HALF, lo // HALF * HALF
             nc.vector.quantize_mx(
                 out=codes[:, lo:hi].bitcast(FP8X4),
                 scales=scales[:, lo:hi],
-                in_=hid[n, h][:, lo - at : hi - at, :].rearrange("p j t -> p (j t)"),
+                in_=hid[n, part][:].rearrange("p j t -> p (j t)"),
             )
 
         def down(c, m, lo, hi, acc):
@@ -283,86 +292,75 @@ def tile_list_gmlpt_relu_resL_kernel(
                     stop=(a == HALVES - 1),
                 )
 
-        def gather_res(c, m, dst):
-            res[c, m] = dst
-            nc.vector.tensor_copy(dst, res_win[m][:].indirect(entries(c)))
+        def last_product(c, m):
+            bank = next_bank()
+            down(c, m, 0, CHUNK, bank[:])
+            y[c, m] = held([P, CHUNK], F32, "y%d%d" % (c, m), "y%d" % m)
+            nc.scalar.copy(y[c, m][:], bank[:])
 
-        def look_ahead(n):
-            for h, (c, m) in enumerate(RES_BEHIND.get(n, [])):
-                gather_res(c, m, held([P, CHUNK], F32, "res%d%d" % (c, m), hid_tag(n, h))[:])
-            if n == STEPS - 3:
-                res[LAST] = held([P, OUT_TILES, CHUNK], F32, "res_last", hid_tag(n, 0))
-                for m in range(OUT_TILES):
-                    gather_res(LAST, m, res[LAST][:, m, :])
-
-        def last_product(c):
-            for m in range(OUT_TILES):
-                bank = next_bank()
-                down(c, m, 0, CHUNK, bank[:])
-                y[c, m] = held([P, CHUNK], F32, "y%d%d" % (c, m))
-                nc.scalar.copy(y[c, m][:], bank[:])
-
-        def add_res(c, n):
-            total = held([P, OUT_TILES, CHUNK], F32, "total%d" % c, hid_tag(n, 1))
-            for m in range(OUT_TILES):
-                nc.gpsimd.tensor_tensor(total[:, m, :], y[c, m][:], res[c, m], ADD)
-                nc.sync.dma_start(out[m * P : (m + 1) * P, c * CHUNK : (c + 1) * CHUNK], total[:, m, :])
+        def add_res(c, m, tag):
+            if m == 0:
+                total[c] = held([P, OUT_TILES, CHUNK], F32, "total%d" % c, tag)
+            nc.vector.tensor_tensor(total[c][:, m, :], res_win[m][:].indirect(entries(c)), y[c, m][:], ADD)
+            if m == OUT_TILES - 1:
+                nc.sync.dma_start(out.rearrange("(m p) j -> p m j", p=P)[:, :, c * CHUNK : (c + 1) * CHUNK], total[c][:])
 
         def finish_last(lo, hi):
             bank = next_bank()
             acc = bank[:, 0 : OUT_TILES * (hi - lo)].rearrange("p (m j) -> p m j", m=OUT_TILES)
             for m in range(OUT_TILES):
                 down(LAST, m, lo, hi, acc[:, m, :])
-            total = held([P, OUT_TILES, hi - lo], F32, "total_last%d" % lo)
-            nc.vector.tensor_tensor(total[:], acc, res[LAST][:, :, lo:hi], ADD)
+            last = held([P, OUT_TILES, hi - lo], F32, "total_last%d" % lo)
+            nc.vector.tensor_tensor(last[:], acc, res[LAST][:, :, lo:hi], ADD)
             nc.sync.dma_start(
-                out.rearrange("(m p) j -> p m j", p=P)[:, :, LAST * CHUNK + lo : LAST * CHUNK + hi], total[:]
+                out.rearrange("(m p) j -> p m j", p=P)[:, :, LAST * CHUNK + lo : LAST * CHUNK + hi], last[:]
             )
 
-        def wide_step(n):
-            c = n // HALVES
-            gate(n)
-            up_wide(n)
-            if c == 0:
-                cast_wd(0)
-            else:
-                last_product(c - 1)
-            for lo in (0, HALF):
-                product(n, lo, lo + HALF, up_copy[n][:, :, lo : lo + HALF])
-            for lo in (0, HALF):
-                quantise_hid(n, lo, lo + HALF)
-            look_ahead(n)
-            if c > 0:
-                add_res(c - 1, n)
+        def look_up(n, i):
+            tag = relu_tag(n, 0)
+            if n in (0, 3):
+                if i == 0:
+                    gather_words(n // 3 + 2, tag)
+                else:
+                    part_words(n // 3 + 2)
+            elif n == 1:
+                if i == 0:
+                    last = held([P, CHUNK], U8, "picked_last", tag)
+                    picked[LAST] = last[:]
+                    gather_scales(LAST, last[:])
+            elif n % HALVES == 0:
+                add_res(n // HALVES - 1, i, tag)
+            elif n == 5:
+                if i == 0:
+                    res[LAST] = held([P, OUT_TILES, CHUNK], F32, "res_last", tag)
+                nc.vector.tensor_copy(res[LAST][:, i, :], res_win[i][:].indirect(entries(LAST)))
 
-        def narrow_step(n):
+        for n in range(STEPS - 1):
+            c, a = divmod(n, HALVES)
             gate(n)
-            for s in range(PACK):
-                up_narrow(n, s)
-            if n == 1:
-                cast_wd(1)
-            for lo in (0, HALF):
-                quantise_hid(n, lo, lo + HALF)
+            if c == 0:
+                cast_wd(a)
+            for h in range(2):
+                for u in range(PAIR):
+                    up_pair(n, h, u)
+                    if h == 1 and c > 0 and a == 0:
+                        last_product(c - 1, u)
+                merge(n, h)
+            for h in range(2):
+                look_up(n, h)
+                quantise(n, h, HALF * h, HALF * (h + 1))
             if n == 1:
                 nc.vector.quantize_mx(
                     out=wd_codes[:].rearrange("p a n -> p (a n)").bitcast(FP8X4),
                     scales=wd_scales[:].rearrange("p a n -> p (a n)"),
                     in_=wd_bf[:].rearrange("p a n t -> p (a n t)"),
                 )
-            look_ahead(n)
-
-        for c in range(LAST):
-            wide_step(HALVES * c)
-            narrow_step(HALVES * c + 1)
-        wide_step(STEPS - 2)
+            if n in (1, 3):
+                move_late(n // 2 + 2)
         n = STEPS - 1
         gate(n)
-        for s in range(PACK - 1):
+        for s in range(PACK):
             up_narrow(n, s)
-        quantise_hid(n, 0, HALF)
-        up_narrow(n, PACK - 1)
-        quantise_hid(n, HALF, HALF + SUB)
-        finish_last(0, HALF)
-        quantise_hid(n, HALF + SUB, CHUNK)
-        finish_last(HALF, HALF + SUB)
-        finish_last(HALF + SUB, CHUNK)
+        for s in range(PACK):
+            quantise(n, s, SUB * s, SUB * (s + 1))
+            finish_last(SUB * s, SUB * (s + 1))

@@ -39,6 +39,8 @@ ALIGN = 64
 LIVE = 96
 DEPTH = 3
 MX_DEPTH = 4
+SHARED_STEPS = ()
+AHEAD = {(3, 0): (3, 0), (3, 1): (3, 1)}
 
 
 def tile_list_gmlpt_relu_resL_kernel(
@@ -48,6 +50,7 @@ def tile_list_gmlpt_relu_resL_kernel(
     with ExitStack() as ctx:
         lists = ctx.enter_context(tc.tile_pool(name="lists", bufs=1))
         keep = ctx.enter_context(tc.tile_pool(name="keep", bufs=1))
+        shared = ctx.enter_context(tc.tile_pool(name="shared", bufs=1))
         psum = ctx.enter_context(tc.psum_pool(name="psum", bufs=1))
 
         def held(shape, dtype, name, tag=None):
@@ -83,23 +86,15 @@ def tile_list_gmlpt_relu_resL_kernel(
             nc.sync.dma_start(raw[:], wu_words[:, :, columns].rearrange("k p c -> p k c").bitcast(I32))
             return raw
 
-        wu_raw = [load_wu(0)]
         wg_second = held([P, K_PASSES, PASS], I32, "wg_second")
         nc.sync.dma_start(wg_second[:], wg_words[:, :, PASS:, :].rearrange("k p r i -> p k (r i)").bitcast(I32))
-        wu_raw.append(load_wu(1))
-        wd_raw = [held([P, PACK, N], F32, "wd_raw%d" % a) for a in range(HALVES)]
-        wd_rows = wd.rearrange("(a b t q) n -> a t b q n", a=HALVES, t=PACK, q=RUN)
-        for a in range(HALVES):
-            for t in range(PACK):
-                nc.sync.dma_start(wd_raw[a][:, t, :], wd_rows[a, t])
-        res_win = [held([P, T], F32, "res_win%d" % m) for m in range(OUT_TILES)]
-        for m in range(OUT_TILES):
-            nc.sync.dma_start(res_win[m][:], rT[m * P : (m + 1) * P, :])
 
         nc.vector.memset(scale_win[0:LIVE, :], 0)
-        planes = [held([P, 2, W_WORDS + CHUNK_WORDS], I32, "planes%d" % a) for a in range(HALVES)]
-        for a in range(HALVES):
-            nc.vector.memset(planes[a][:], 0)
+        planes = [held([P, 2, W_WORDS + CHUNK_WORDS * (1 - a)], I32, "planes%d" % a) for a in range(HALVES)]
+        middle_planes = held([P, 2, 2 * CHUNK_WORDS], I32, "middle_planes")
+        last_planes = held([P, 2, CHUNK_WORDS], I32, "last_planes")
+        for tile in planes + [middle_planes, last_planes]:
+            nc.vector.memset(tile[:], 0)
         warm = keep.tile([P, 2, 8], F32, name="warm")
         nc.gpsimd.memset(warm[:, 0, :], 0.0)
         nc.scalar.activation(warm[:, 1, :], warm[:, 0, :], RELU)
@@ -112,32 +107,45 @@ def tile_list_gmlpt_relu_resL_kernel(
                 queue.dma_start(dst[32 * quad : 32 * quad + 4, :, :], src[LIVE + 8 * quad : LIVE + 8 * quad + 8, :])
 
         def table_plane(c, kp, lo, hi):
-            return planes[c % 2][:, kp, W_WORDS:].bitcast(U8)[:, lo:hi]
+            if c == 0:
+                return planes[0][:, kp, W_WORDS:].bitcast(U8)[:, lo:hi]
+            if c == LAST:
+                return last_planes[:, kp, :].bitcast(U8)[:, lo:hi]
+            return middle_planes[:, kp, :].bitcast(U8)[:, (c - 1) * CHUNK + lo : (c - 1) * CHUNK + hi]
 
         def weight_plane(x, kp, a, t):
             at = (kp * PACK + t) * (P // 4)
             return planes[a][:, x, at : at + P // 4].bitcast(U8)
 
-        staged = [held([P, W_WORDS + CHUNK_WORDS], I32, "staged%d" % a) for a in range(HALVES)]
-        for a in range(HALVES):
+        def sort_weight_scales(a, staged):
             nc.vector.tensor_copy(
-                staged[a][LIVE:P, 0:W_WORDS].rearrange("p (k t b e) -> p k t b e", k=K_PASSES, t=PACK, e=RUN // 4),
+                staged[LIVE:P, 0:W_WORDS].rearrange("p (k t b e) -> p k t b e", k=K_PASSES, t=PACK, e=RUN // 4),
                 w_scale_raw[LIVE:P, :, PASS // 4 * a : PASS // 4 * (a + 1)].rearrange(
                     "p k (b t e) -> p k t b e", t=PACK, e=RUN // 4
                 ),
             )
-        picked_first = held([P, CHUNK], U8, "picked_first", "picked")
-        gather_scales(0, picked_first[:])
-        nc.vector.tensor_copy(staged[0][LIVE:P, W_WORDS:], picked_first[LIVE:P, :].bitcast(I32))
-        move_scales(nc.scalar, staged[0], planes[0][:])
-        picked_rest = held([P, 2 * CHUNK], U8, "picked_rest", "picked")
-        gather_scales(1, picked_rest[:], 2)
-        picked = {2: picked_rest[:, CHUNK:]}
-        nc.vector.tensor_copy(staged[1][LIVE:P, W_WORDS:], picked_rest[LIVE:P, 0:CHUNK].bitcast(I32))
-        move_scales(nc.scalar, staged[1], planes[1][:])
 
-        def move_late(c):
-            move_scales(nc.sync, picked[c].bitcast(I32), planes[c % 2][:, :, W_WORDS:])
+        staged_first = held([P, W_WORDS + CHUNK_WORDS], I32, "staged_first")
+        sort_weight_scales(0, staged_first)
+        picked_first = shared.tile([P, CHUNK], U8, name="picked_first", offset=4 * W_WORDS - HALF, align_bytes=ALIGN)
+        gather_scales(0, picked_first[:])
+        nc.vector.tensor_copy(staged_first[LIVE:P, W_WORDS:], picked_first[LIVE:P, :].bitcast(I32))
+        move_scales(nc.scalar, staged_first, planes[0][:])
+        staged_second = shared.tile([P, W_WORDS], I32, name="staged_second", offset=0, align_bytes=ALIGN)
+        sort_weight_scales(1, staged_second)
+        move_scales(nc.scalar, staged_second, planes[1][:])
+        picked_rest = shared.tile([P, 2 * CHUNK], U8, name="picked_rest", offset=4 * W_WORDS, align_bytes=ALIGN)
+        gather_scales(1, picked_rest[:], 2)
+        move_scales(nc.scalar, picked_rest[:].bitcast(I32), middle_planes[:])
+        wu_raw = [load_wu(a) for a in range(HALVES)]
+        res_win = [held([P, T], F32, "res_win%d" % m) for m in range(OUT_TILES)]
+        nc.sync.dma_start(res_win[0][:], rT[0:P, :])
+        wd_raw = [held([P, PACK, N], F32, "wd_raw%d" % a) for a in range(HALVES)]
+        wd_rows = wd.rearrange("(a b t q) n -> a t b q n", a=HALVES, t=PACK, q=RUN)
+        for a in range(HALVES):
+            for t in range(PACK):
+                nc.sync.dma_start(wd_raw[a][:, t, :], wd_rows[a, t])
+        nc.sync.dma_start(res_win[1][:], rT[P : 2 * P, :])
 
         both, table, wg_sorted, wu_sorted = {}, {}, {}, {}
 
@@ -175,8 +183,7 @@ def tile_list_gmlpt_relu_resL_kernel(
         gather_words(0, "both0")
         for kp in range(K_PASSES):
             first_operands(kp)
-        sort_wu(0)
-        gather_words(1, "wg_first1")
+        gather_words(1, "both0")
         ordered = held([P, PACK, K_PASSES, P], I32, "wg_sorted1")
         nc.vector.tensor_copy(
             ordered[:].rearrange("p t k (b e) -> p t (k b) e", e=RUN),
@@ -185,12 +192,18 @@ def tile_list_gmlpt_relu_resL_kernel(
         for kp in range(K_PASSES):
             wg_sorted[1, kp] = ordered[:, :, kp, :]
         part_words(1)
+        sort_wu(0)
+        gather_words(2, "wg_second")
+        picked_last = held([P, CHUNK], U8, "picked_last", "both0")
+        gather_scales(LAST, picked_last[:])
+        move_scales(nc.sync, picked_last[:].bitcast(I32), last_planes[:])
+        part_words(2)
         sort_wu(1)
 
         relu_g, pairs, hid, hid_mx, res, y, total = {}, {}, {}, {}, {}, {}, {}
 
         def relu_tag(n, u):
-            return "relu%d%d" % (n if (n, u) in ((1, 0), (5, 0)) else (n + 1) % DEPTH + 6, u)
+            return "relu%d%d" % (8 if u and n % 2 else n, u)
 
         def first_products(acc, x, n, t, lo, hi, passes=range(K_PASSES)):
             c, a = divmod(n, HALVES)
@@ -210,25 +223,41 @@ def tile_list_gmlpt_relu_resL_kernel(
                 opened = [next_bank() for t in range(PACK)]
                 for t in range(PACK):
                     first_products(opened[t][:], 0, n, t, 0, CHUNK, [0])
-            shape = [P, PACK, CHUNK] if n == STEPS - 1 else [P, PAIR, CHUNK]
+            if n == STEPS - 1:
+                relu_g[n] = held([P, PACK, CHUNK], F32, "relu_last")
             for t in range(PACK):
-                u, at = divmod(t, shape[1])
-                if at == 0:
-                    relu_g[n, u] = held(shape, F32, "relu_g%d%d" % (n, u), "relu_last" if n == STEPS - 1 else relu_tag(n, u))
+                u, at = divmod(t, PAIR)
+                if at == 0 and n == STEPS - 1:
+                    relu_g[n, u] = relu_g[n][:, PAIR * u : PAIR * (u + 1), :]
+                elif at == 0:
+                    relu_g[n, u] = held([P, PAIR, CHUNK], F32, "relu_g%d%d" % (n, u), relu_tag(n, u))
                 bank = opened[t] if n == 0 else next_bank()
                 first_products(bank[:], 0, n, t, 0, CHUNK, [1] if n == 0 else range(K_PASSES))
                 nc.scalar.activation(relu_g[n, u][:, at, :], bank[:], RELU)
 
-        behind = {1: relu_tag(0, 0), 3: "y1", 4: relu_tag(3, 0), 5: "y1"}
+        behind = {1: relu_tag(0, 0), 3: "y0", 5: "y0"}
 
         def up_pair(n, h, u):
+            shared = n in SHARED_STEPS and (h, u) == (1, 0)
             if u == 0:
                 tag = behind[n] if h == 0 and n in behind else "pairs%d%d" % (n % 2, h)
+                if shared:
+                    tag = "hid%d1" % ((n - 1) % 2)
                 pairs[n, h] = held([P, PAIR, HALF, PAIR], BF16, "pairs%d%d" % (n, h), tag)
             bank = next_bank()
             places = bank[:].rearrange("p (t j) -> p t j", t=PAIR)
             for t in range(PAIR):
                 first_products(places[:, t, :], 1, n, PAIR * u + t, HALF * h, HALF * (h + 1))
+            if shared:
+                copied = held([P, PAIR, HALF], F32, "up_copy%d" % n, "up_copy%d" % (n % 2))
+                nc.scalar.copy(copied[:], places)
+                nc.gpsimd.tensor_tensor(
+                    pairs[n, h][:, u].rearrange("p j t -> p t j"),
+                    copied[:],
+                    relu_g[n, u][:, :, HALF * h : HALF * (h + 1)],
+                    MULT,
+                )
+                return
             nc.vector.tensor_tensor(
                 pairs[n, h][:, u],
                 places.rearrange("p t j -> p j t"),
@@ -237,7 +266,7 @@ def tile_list_gmlpt_relu_resL_kernel(
             )
 
         def merge(n, h):
-            tag = "wd_raw%d" % n if n < HALVES and h == 0 else "hid%d%d" % (n % 2, h)
+            tag = "hid%d%d" % (n if h == 0 else n % 2, h)
             hid[n, h] = held([P, HALF, PACK], BF16, "hid%d%d" % (n, h), tag)
             nc.scalar.copy(
                 hid[n, h][:].rearrange("p j t -> p (j t)").bitcast(U32).rearrange("p (j u) -> p j u", u=PAIR),
@@ -253,7 +282,7 @@ def tile_list_gmlpt_relu_resL_kernel(
             nc.vector.tensor_tensor(
                 hid[n, s][:].rearrange("p (g i) t -> p g t i", i=PAIR),
                 places.rearrange("p t (g i) -> p g t i", i=PAIR),
-                relu_g[n, 0][:, :, SUB * s : SUB * (s + 1)].rearrange("p t (g i) -> p g t i", i=PAIR),
+                relu_g[n][:, :, SUB * s : SUB * (s + 1)].rearrange("p t (g i) -> p g t i", i=PAIR),
                 MULT,
             )
 
@@ -269,7 +298,8 @@ def tile_list_gmlpt_relu_resL_kernel(
 
         def quantise(n, part, lo, hi):
             if lo == 0:
-                codes = held([P, CHUNK], U32, "codes%d" % n, "codes%d" % (n % MX_DEPTH))
+                tag = {2: relu_tag(2, 1), 4: relu_tag(4, 1), 6: relu_tag(6, 1)}.get(n, "codes%d" % (n % MX_DEPTH))
+                codes = held([P, CHUNK], U32, "codes%d" % n, tag)
                 scales = held([P, CHUNK], U8, "scales%d" % n, "scales%d" % (n % MX_DEPTH))
                 hid_mx[n] = (codes, scales)
             codes, scales = hid_mx[n]
@@ -318,49 +348,76 @@ def tile_list_gmlpt_relu_resL_kernel(
 
         def look_up(n, i):
             tag = relu_tag(n, 0)
-            if n in (0, 3):
+            if n == 0:
                 if i == 0:
-                    gather_words(n // 3 + 2, tag)
+                    gather_words(LAST, tag)
                 else:
-                    part_words(n // 3 + 2)
-            elif n == 1:
-                if i == 0:
-                    last = held([P, CHUNK], U8, "picked_last", tag)
-                    picked[LAST] = last[:]
-                    gather_scales(LAST, last[:])
-            elif n % HALVES == 0:
+                    part_words(LAST)
+            elif n in (2, 4):
                 add_res(n // HALVES - 1, i, tag)
-            elif n == 5:
-                if i == 0:
-                    res[LAST] = held([P, OUT_TILES, CHUNK], F32, "res_last", tag)
-                nc.vector.tensor_copy(res[LAST][:, i, :], res_win[i][:].indirect(entries(LAST)))
+            elif n == STEPS - 2:
+                if (LAST - 1, i) not in AHEAD.values():
+                    whole = held([P, CHUNK], F32, "total%d%d" % (LAST - 1, i))
+                    nc.vector.tensor_tensor(whole[:], res_win[i][:].indirect(entries(LAST - 1)), y[LAST - 1, i][:], ADD)
+                    nc.sync.dma_start(out[i * P : (i + 1) * P, (LAST - 1) * CHUNK : LAST * CHUNK], whole[:])
+            elif (n, i) in AHEAD:
+                c, m = AHEAD[n, i]
+                if c == LAST:
+                    if LAST not in res:
+                        res[LAST] = held([P, OUT_TILES, CHUNK], F32, "res_last", tag if i == 0 else "hid%d0" % n)
+                    dst = res[LAST][:, m, :]
+                else:
+                    res[c, m] = held([P, CHUNK], F32, "res%d%d" % (c, m), tag if i == 0 else "hid%d0" % n if i == 1 else "hid%d1" % (n % 2))
+                    dst = res[c, m][:]
+                nc.vector.tensor_copy(dst, res_win[m][:].indirect(entries(c)))
 
+        def finish_gathered(c, m):
+            bank = next_bank()
+            down(c, m, 0, CHUNK, bank[:])
+            whole = held([P, CHUNK], F32, "total%d%d" % (c, m))
+            nc.vector.tensor_tensor(whole[:], bank[:], res[c, m][:], ADD)
+            nc.sync.dma_start(out[m * P : (m + 1) * P, c * CHUNK : (c + 1) * CHUNK], whole[:])
+
+        gate(0)
         for n in range(STEPS - 1):
             c, a = divmod(n, HALVES)
-            gate(n)
+            if n + 1 < STEPS - 1:
+                gate(n + 1)
             if c == 0:
                 cast_wd(a)
-            for h in range(2):
-                for u in range(PAIR):
-                    up_pair(n, h, u)
-                    if h == 1 and c > 0 and a == 0:
-                        last_product(c - 1, u)
-                merge(n, h)
+            order = [(1, 0), (0, 0), (0, 1), (1, 1)] if n in SHARED_STEPS else [(0, 0), (0, 1), (1, 0), (1, 1)]
+            for i, (h, u) in enumerate(order):
+                up_pair(n, h, u)
+                if u == 1:
+                    merge(n, h)
+                if i >= 2 and 0 < c < LAST and a == 0:
+                    last_product(c - 1, i - 2)
+            if n == STEPS - 2:
+                for m in range(OUT_TILES):
+                    if (c - 1, m) in AHEAD.values():
+                        finish_gathered(c - 1, m)
+                    else:
+                        last_product(c - 1, m)
+                gate(n + 1)
             for h in range(2):
                 look_up(n, h)
                 quantise(n, h, HALF * h, HALF * (h + 1))
+            if n % 2:
+                look_up(n, 2)
             if n == 1:
                 nc.vector.quantize_mx(
                     out=wd_codes[:].rearrange("p a n -> p (a n)").bitcast(FP8X4),
                     scales=wd_scales[:].rearrange("p a n -> p (a n)"),
                     in_=wd_bf[:].rearrange("p a n t -> p (a n t)"),
                 )
-            if n in (1, 3):
-                move_late(n // 2 + 2)
         n = STEPS - 1
-        gate(n)
-        for s in range(PACK):
+        for u in range(PAIR):
+            up_pair(n, 0, u)
+        merge(n, 0)
+        for s in range(PAIR, PACK):
             up_narrow(n, s)
-        for s in range(PACK):
+        quantise(n, 0, 0, HALF)
+        finish_last(0, HALF)
+        for s in range(PAIR, PACK):
             quantise(n, s, SUB * s, SUB * (s + 1))
             finish_last(SUB * s, SUB * (s + 1))

@@ -40,7 +40,7 @@ LIVE = 96
 DEPTH = 3
 MX_DEPTH = 4
 SHARED_STEPS = ()
-AHEAD = {(3, 0): (3, 0), (3, 1): (3, 1)}
+AHEAD = {(1, 0): (0, 0), (2, 0): (0, 1), (2, 1): (1, 0), (3, 0): (3, 0), (3, 1): (3, 1), (4, 0): (1, 1), (4, 1): (2, 0), (5, 0): (2, 1)}
 
 
 def tile_list_gmlpt_relu_resL_kernel(
@@ -235,7 +235,7 @@ def tile_list_gmlpt_relu_resL_kernel(
                 first_products(bank[:], 0, n, t, 0, CHUNK, [1] if n == 0 else range(K_PASSES))
                 nc.scalar.activation(relu_g[n, u][:, at, :], bank[:], RELU)
 
-        behind = {1: relu_tag(0, 0), 3: "y0", 5: "y0"}
+        behind = {1: relu_tag(0, 0)}
 
         def up_pair(n, h, u):
             shared = n in SHARED_STEPS and (h, u) == (1, 0)
@@ -266,7 +266,7 @@ def tile_list_gmlpt_relu_resL_kernel(
             )
 
         def merge(n, h):
-            tag = "hid%d%d" % (n if h == 0 else n % 2, h)
+            tag = "hid%d%d" % (n % 2, h)
             hid[n, h] = held([P, HALF, PACK], BF16, "hid%d%d" % (n, h), tag)
             nc.scalar.copy(
                 hid[n, h][:].rearrange("p j t -> p (j t)").bitcast(U32).rearrange("p (j u) -> p j u", u=PAIR),
@@ -298,7 +298,7 @@ def tile_list_gmlpt_relu_resL_kernel(
 
         def quantise(n, part, lo, hi):
             if lo == 0:
-                tag = {2: relu_tag(2, 1), 4: relu_tag(4, 1), 6: relu_tag(6, 1)}.get(n, "codes%d" % (n % MX_DEPTH))
+                tag = "codes%d" % (n % MX_DEPTH)
                 codes = held([P, CHUNK], U32, "codes%d" % n, tag)
                 scales = held([P, CHUNK], U8, "scales%d" % n, "scales%d" % (n % MX_DEPTH))
                 hid_mx[n] = (codes, scales)
@@ -325,15 +325,14 @@ def tile_list_gmlpt_relu_resL_kernel(
         def last_product(c, m):
             bank = next_bank()
             down(c, m, 0, CHUNK, bank[:])
-            y[c, m] = held([P, CHUNK], F32, "y%d%d" % (c, m), "y%d" % m)
+            y[c, m] = held([P, CHUNK], F32, "y%d%d" % (c, m))
             nc.scalar.copy(y[c, m][:], bank[:])
 
-        def add_res(c, m, tag):
-            if m == 0:
-                total[c] = held([P, OUT_TILES, CHUNK], F32, "total%d" % c, tag)
-            nc.vector.tensor_tensor(total[c][:, m, :], res_win[m][:].indirect(entries(c)), y[c, m][:], ADD)
-            if m == OUT_TILES - 1:
-                nc.sync.dma_start(out.rearrange("(m p) j -> p m j", p=P)[:, :, c * CHUNK : (c + 1) * CHUNK], total[c][:])
+        def add_res(c, tag):
+            whole = held([P, OUT_TILES, CHUNK], F32, "total%d" % c, tag)
+            for m in range(OUT_TILES):
+                nc.gpsimd.tensor_tensor(whole[:, m, :], y[c, m][:], res[c, m][:], ADD)
+                nc.sync.dma_start(out[m * P : (m + 1) * P, c * CHUNK : (c + 1) * CHUNK], whole[:, m, :])
 
         def finish_last(lo, hi):
             bank = next_bank()
@@ -353,25 +352,18 @@ def tile_list_gmlpt_relu_resL_kernel(
                     gather_words(LAST, tag)
                 else:
                     part_words(LAST)
-            elif n in (2, 4):
-                add_res(n // HALVES - 1, i, tag)
-            elif n == STEPS - 2:
-                if (LAST - 1, i) not in AHEAD.values():
-                    whole = held([P, CHUNK], F32, "total%d%d" % (LAST - 1, i))
-                    nc.vector.tensor_tensor(whole[:], res_win[i][:].indirect(entries(LAST - 1)), y[LAST - 1, i][:], ADD)
-                    nc.sync.dma_start(out[i * P : (i + 1) * P, (LAST - 1) * CHUNK : LAST * CHUNK], whole[:])
             elif (n, i) in AHEAD:
                 c, m = AHEAD[n, i]
                 if c == LAST:
                     if LAST not in res:
-                        res[LAST] = held([P, OUT_TILES, CHUNK], F32, "res_last", tag if i == 0 else "hid%d0" % n)
+                        res[LAST] = held([P, OUT_TILES, CHUNK], F32, "res_last", relu_tag(n, i))
                     dst = res[LAST][:, m, :]
                 else:
-                    res[c, m] = held([P, CHUNK], F32, "res%d%d" % (c, m), tag if i == 0 else "hid%d0" % n if i == 1 else "hid%d1" % (n % 2))
+                    res[c, m] = held([P, CHUNK], F32, "res%d%d" % (c, m), relu_tag(n, i))
                     dst = res[c, m][:]
                 nc.vector.tensor_copy(dst, res_win[m][:].indirect(entries(c)))
 
-        def finish_gathered(c, m):
+        def finish_from_bank(c, m):
             bank = next_bank()
             down(c, m, 0, CHUNK, bank[:])
             whole = held([P, CHUNK], F32, "total%d%d" % (c, m))
@@ -390,20 +382,16 @@ def tile_list_gmlpt_relu_resL_kernel(
                 up_pair(n, h, u)
                 if u == 1:
                     merge(n, h)
-                if i >= 2 and 0 < c < LAST and a == 0:
-                    last_product(c - 1, i - 2)
-            if n == STEPS - 2:
+            if 0 < c < LAST and a == 0:
                 for m in range(OUT_TILES):
-                    if (c - 1, m) in AHEAD.values():
-                        finish_gathered(c - 1, m)
-                    else:
-                        last_product(c - 1, m)
+                    last_product(c - 1, m)
+            if n == STEPS - 2:
                 gate(n + 1)
             for h in range(2):
                 look_up(n, h)
                 quantise(n, h, HALF * h, HALF * (h + 1))
-            if n % 2:
-                look_up(n, 2)
+            if 0 < c < LAST and a == 0:
+                add_res(c - 1, "hid%d1" % (n % 2))
             if n == 1:
                 nc.vector.quantize_mx(
                     out=wd_codes[:].rearrange("p a n -> p (a n)").bitcast(FP8X4),
@@ -411,13 +399,10 @@ def tile_list_gmlpt_relu_resL_kernel(
                     in_=wd_bf[:].rearrange("p a n t -> p (a n t)"),
                 )
         n = STEPS - 1
-        for u in range(PAIR):
-            up_pair(n, 0, u)
-        merge(n, 0)
-        for s in range(PAIR, PACK):
+        for m in range(OUT_TILES):
+            finish_from_bank(LAST - 1, m)
+        for s in range(PACK):
             up_narrow(n, s)
-        quantise(n, 0, 0, HALF)
-        finish_last(0, HALF)
-        for s in range(PAIR, PACK):
+        for s in range(PACK):
             quantise(n, s, SUB * s, SUB * (s + 1))
             finish_last(SUB * s, SUB * (s + 1))

@@ -39,8 +39,7 @@ ALIGN = 64
 LIVE = 96
 DEPTH = 3
 MX_DEPTH = 4
-SHARED_STEPS = ()
-AHEAD = {(1, 0): (0, 0), (2, 0): (0, 1), (2, 1): (1, 0), (3, 0): (3, 0), (3, 1): (3, 1), (4, 0): (1, 1), (4, 1): (2, 0), (5, 0): (2, 1)}
+BEHIND = {(1, 0): (0, 1, 2), (3, -1): (2, 0, 1), (3, 0): "last", (5, -1): (2, 1, 1)}
 
 
 def tile_list_gmlpt_relu_resL_kernel(
@@ -199,11 +198,9 @@ def tile_list_gmlpt_relu_resL_kernel(
         move_scales(nc.sync, picked_last[:].bitcast(I32), last_planes[:])
         part_words(2)
         sort_wu(1)
+        gather_words(LAST, "wu_raw0")
 
-        relu_g, pairs, hid, hid_mx, res, y, total = {}, {}, {}, {}, {}, {}, {}
-
-        def relu_tag(n, u):
-            return "relu%d%d" % (8 if u and n % 2 else n, u)
+        relu_g, up_copy, hid, hid_mx, res, y = {}, {}, {}, {}, {}, {}
 
         def first_products(acc, x, n, t, lo, hi, passes=range(K_PASSES)):
             c, a = divmod(n, HALVES)
@@ -218,73 +215,50 @@ def tile_list_gmlpt_relu_resL_kernel(
                     stop=(kp == K_PASSES - 1),
                 )
 
+        def relu_tag(n):
+            return {3: "word_win", 5: "wd_raw0"}.get(n, "relu%d" % (n % DEPTH))
+
         def gate(n):
             if n == 0:
                 opened = [next_bank() for t in range(PACK)]
                 for t in range(PACK):
                     first_products(opened[t][:], 0, n, t, 0, CHUNK, [0])
-            if n == STEPS - 1:
-                relu_g[n] = held([P, PACK, CHUNK], F32, "relu_last")
+            relu_g[n] = held([P, PACK, CHUNK], F32, "relu_g%d" % n, relu_tag(n))
             for t in range(PACK):
-                u, at = divmod(t, PAIR)
-                if at == 0 and n == STEPS - 1:
-                    relu_g[n, u] = relu_g[n][:, PAIR * u : PAIR * (u + 1), :]
-                elif at == 0:
-                    relu_g[n, u] = held([P, PAIR, CHUNK], F32, "relu_g%d%d" % (n, u), relu_tag(n, u))
                 bank = opened[t] if n == 0 else next_bank()
                 first_products(bank[:], 0, n, t, 0, CHUNK, [1] if n == 0 else range(K_PASSES))
-                nc.scalar.activation(relu_g[n, u][:, at, :], bank[:], RELU)
+                nc.scalar.activation(relu_g[n][:, t, :], bank[:], RELU)
 
-        behind = {1: relu_tag(0, 0)}
+        def hid_tag(n, h):
+            return "up_copy%d" % (n - 1) if n % HALVES and h == 0 else "hid%d%d" % (n, h)
 
-        def up_pair(n, h, u):
-            shared = n in SHARED_STEPS and (h, u) == (1, 0)
-            if u == 0:
-                tag = behind[n] if h == 0 and n in behind else "pairs%d%d" % (n % 2, h)
-                if shared:
-                    tag = "hid%d1" % ((n - 1) % 2)
-                pairs[n, h] = held([P, PAIR, HALF, PAIR], BF16, "pairs%d%d" % (n, h), tag)
-            bank = next_bank()
-            places = bank[:].rearrange("p (t j) -> p t j", t=PAIR)
-            for t in range(PAIR):
-                first_products(places[:, t, :], 1, n, PAIR * u + t, HALF * h, HALF * (h + 1))
-            if shared:
-                copied = held([P, PAIR, HALF], F32, "up_copy%d" % n, "up_copy%d" % (n % 2))
-                nc.scalar.copy(copied[:], places)
-                nc.gpsimd.tensor_tensor(
-                    pairs[n, h][:, u].rearrange("p j t -> p t j"),
-                    copied[:],
-                    relu_g[n, u][:, :, HALF * h : HALF * (h + 1)],
-                    MULT,
-                )
-                return
+        def width(n):
+            return CHUNK if (n, -1) in BEHIND else HALF
+
+        def product(n, lo, hi, up_values):
+            h, at = lo // width(n), lo // width(n) * width(n)
+            if (n, h) not in hid:
+                hid[n, h] = held([P, width(n), PACK], BF16, "hid%d%d" % (n, h), hid_tag(n, h))
             nc.vector.tensor_tensor(
-                pairs[n, h][:, u],
-                places.rearrange("p t j -> p j t"),
-                relu_g[n, u][:, :, HALF * h : HALF * (h + 1)].rearrange("p t j -> p j t"),
+                hid[n, h][:, lo - at : hi - at, :].rearrange("p (g i) t -> p g t i", i=PAIR),
+                up_values.rearrange("p t (g i) -> p g t i", i=PAIR),
+                relu_g[n][:, :, lo:hi].rearrange("p t (g i) -> p g t i", i=PAIR),
                 MULT,
             )
 
-        def merge(n, h):
-            tag = "hid%d%d" % (n % 2, h)
-            hid[n, h] = held([P, HALF, PACK], BF16, "hid%d%d" % (n, h), tag)
-            nc.scalar.copy(
-                hid[n, h][:].rearrange("p j t -> p (j t)").bitcast(U32).rearrange("p (j u) -> p j u", u=PAIR),
-                pairs[n, h][:].rearrange("p u j t -> p u (j t)").bitcast(U32).rearrange("p u j -> p j u"),
-            )
+        def up_wide(n):
+            up_copy[n] = held([P, PACK, CHUNK], F32, "up_copy%d" % n)
+            for t in range(PACK):
+                bank = next_bank()
+                first_products(bank[:], 1, n, t, 0, CHUNK)
+                nc.scalar.copy(up_copy[n][:, t, :], bank[:])
 
         def up_narrow(n, s):
             bank = next_bank()
             places = bank[:].rearrange("p (t j) -> p t j", t=PACK)
             for t in range(PACK):
                 first_products(places[:, t, :], 1, n, t, SUB * s, SUB * (s + 1))
-            hid[n, s] = held([P, SUB, PACK], BF16, "hid_last%d" % s)
-            nc.vector.tensor_tensor(
-                hid[n, s][:].rearrange("p (g i) t -> p g t i", i=PAIR),
-                places.rearrange("p t (g i) -> p g t i", i=PAIR),
-                relu_g[n][:, :, SUB * s : SUB * (s + 1)].rearrange("p t (g i) -> p g t i", i=PAIR),
-                MULT,
-            )
+            product(n, SUB * s, SUB * (s + 1), places)
 
         wd_codes = held([P, HALVES, N], U32, "wd_codes")
         wd_scales = held([P, HALVES, N], U8, "wd_scales")
@@ -296,17 +270,17 @@ def tile_list_gmlpt_relu_resL_kernel(
                 wd_raw[a][:].rearrange("p t (g i) -> p g t i", i=LINE),
             )
 
-        def quantise(n, part, lo, hi):
+        def quantise(n, lo, hi):
             if lo == 0:
-                tag = "codes%d" % (n % MX_DEPTH)
-                codes = held([P, CHUNK], U32, "codes%d" % n, tag)
+                codes = held([P, CHUNK], U32, "codes%d" % n, "codes%d" % (n % MX_DEPTH))
                 scales = held([P, CHUNK], U8, "scales%d" % n, "scales%d" % (n % MX_DEPTH))
                 hid_mx[n] = (codes, scales)
             codes, scales = hid_mx[n]
+            h, at = lo // width(n), lo // width(n) * width(n)
             nc.vector.quantize_mx(
                 out=codes[:, lo:hi].bitcast(FP8X4),
                 scales=scales[:, lo:hi],
-                in_=hid[n, part][:].rearrange("p j t -> p (j t)"),
+                in_=hid[n, h][:, lo - at : hi - at, :].rearrange("p j t -> p (j t)"),
             )
 
         def down(c, m, lo, hi, acc):
@@ -328,11 +302,11 @@ def tile_list_gmlpt_relu_resL_kernel(
             y[c, m] = held([P, CHUNK], F32, "y%d%d" % (c, m))
             nc.scalar.copy(y[c, m][:], bank[:])
 
-        def add_res(c, tag):
-            whole = held([P, OUT_TILES, CHUNK], F32, "total%d" % c, tag)
-            for m in range(OUT_TILES):
-                nc.gpsimd.tensor_tensor(whole[:, m, :], y[c, m][:], res[c, m][:], ADD)
-                nc.sync.dma_start(out[m * P : (m + 1) * P, c * CHUNK : (c + 1) * CHUNK], whole[:, m, :])
+        def add_res(c, tiles, tag):
+            whole = held([P, len(tiles), CHUNK], F32, "total%d" % c, tag)
+            for i, m in enumerate(tiles):
+                nc.gpsimd.tensor_tensor(whole[:, i, :], y[c, m][:], res[c, m], ADD)
+                nc.sync.dma_start(out[m * P : (m + 1) * P, c * CHUNK : (c + 1) * CHUNK], whole[:, i, :])
 
         def finish_last(lo, hi):
             bank = next_bank()
@@ -345,64 +319,71 @@ def tile_list_gmlpt_relu_resL_kernel(
                 out.rearrange("(m p) j -> p m j", p=P)[:, :, LAST * CHUNK + lo : LAST * CHUNK + hi], last[:]
             )
 
-        def look_up(n, i):
-            tag = relu_tag(n, 0)
-            if n == 0:
-                if i == 0:
-                    gather_words(LAST, tag)
-                else:
-                    part_words(LAST)
-            elif (n, i) in AHEAD:
-                c, m = AHEAD[n, i]
-                if c == LAST:
-                    if LAST not in res:
-                        res[LAST] = held([P, OUT_TILES, CHUNK], F32, "res_last", relu_tag(n, i))
-                    dst = res[LAST][:, m, :]
-                else:
-                    res[c, m] = held([P, CHUNK], F32, "res%d%d" % (c, m), relu_tag(n, i))
-                    dst = res[c, m][:]
-                nc.vector.tensor_copy(dst, res_win[m][:].indirect(entries(c)))
+        def look_up(n, h):
+            what = BEHIND.get((n, h))
+            tag = relu_tag(n) if h < 0 else hid_tag(n, h)
+            if what == "last":
+                res[LAST] = held([P, OUT_TILES, CHUNK], F32, "res_last", tag)
+                for m in range(OUT_TILES):
+                    nc.vector.tensor_copy(res[LAST][:, m, :], res_win[m][:].indirect(entries(LAST)))
+            elif what:
+                c, m, count = what
+                picked = held([P, count * CHUNK], F32, "res%d%d" % (c, m), tag)
+                nc.vector.tensor_copy(picked[:], res_win[m][:].indirect(entries(c, count)))
+                for i in range(count):
+                    res[c + i, m] = picked[:, i * CHUNK : (i + 1) * CHUNK]
 
         def finish_from_bank(c, m):
             bank = next_bank()
             down(c, m, 0, CHUNK, bank[:])
             whole = held([P, CHUNK], F32, "total%d%d" % (c, m))
-            nc.vector.tensor_tensor(whole[:], bank[:], res[c, m][:], ADD)
+            nc.vector.tensor_tensor(whole[:], bank[:], res[c, m], ADD)
             nc.sync.dma_start(out[m * P : (m + 1) * P, c * CHUNK : (c + 1) * CHUNK], whole[:])
 
+        early = held([P, 2 * CHUNK], F32, "res_early", "wg_second")
+        nc.vector.tensor_copy(early[:], res_win[0][:].indirect(entries(0, 2)))
+        for c in range(2):
+            res[c, 0] = early[:, c * CHUNK : (c + 1) * CHUNK]
+        part_words(LAST)
         gate(0)
         for n in range(STEPS - 1):
             c, a = divmod(n, HALVES)
             if n + 1 < STEPS - 1:
                 gate(n + 1)
+            if a == 0:
+                up_wide(n)
+            else:
+                for s in range(PACK):
+                    up_narrow(n, s)
             if c == 0:
                 cast_wd(a)
-            order = [(1, 0), (0, 0), (0, 1), (1, 1)] if n in SHARED_STEPS else [(0, 0), (0, 1), (1, 0), (1, 1)]
-            for i, (h, u) in enumerate(order):
-                up_pair(n, h, u)
-                if u == 1:
-                    merge(n, h)
             if 0 < c < LAST and a == 0:
                 for m in range(OUT_TILES):
                     last_product(c - 1, m)
             if n == STEPS - 2:
                 gate(n + 1)
-            for h in range(2):
-                look_up(n, h)
-                quantise(n, h, HALF * h, HALF * (h + 1))
-            if 0 < c < LAST and a == 0:
-                add_res(c - 1, "hid%d1" % (n % 2))
+            if a == 0:
+                for lo in (0, HALF):
+                    product(n, lo, lo + HALF, up_copy[n][:, :, lo : lo + HALF])
+            look_up(n, -1)
+            for lo in range(0, CHUNK, width(n)):
+                quantise(n, lo, lo + width(n))
             if n == 1:
                 nc.vector.quantize_mx(
                     out=wd_codes[:].rearrange("p a n -> p (a n)").bitcast(FP8X4),
                     scales=wd_scales[:].rearrange("p a n -> p (a n)"),
                     in_=wd_bf[:].rearrange("p a n t -> p (a n t)"),
                 )
+            for h in range(2):
+                look_up(n, h)
+            if 0 < c < LAST and a == 0:
+                add_res(c - 1, range(OUT_TILES), hid_tag(n, 1))
         n = STEPS - 1
-        for m in range(OUT_TILES):
-            finish_from_bank(LAST - 1, m)
+        finish_from_bank(LAST - 1, 0)
+        last_product(LAST - 1, 1)
+        add_res(LAST - 1, [1], hid_tag(n - 1, 1))
         for s in range(PACK):
             up_narrow(n, s)
         for s in range(PACK):
-            quantise(n, s, SUB * s, SUB * (s + 1))
+            quantise(n, SUB * s, SUB * (s + 1))
             finish_last(SUB * s, SUB * (s + 1))

@@ -39,7 +39,8 @@ ALIGN = 64
 LIVE = 96
 DEPTH = 3
 MX_DEPTH = 4
-BEHIND = {(1, 0): (0, 1, 2), (3, -1): (2, 0, 1), (3, 0): "last", (5, -1): (2, 1, 1)}
+PAIRED = (3, 5)
+BEHIND = {(1, 0): (0, 1, 2), (3, -1): "last", (3, 0): (2, 0, 1), (5, -1): (2, 1, 1)}
 
 
 def tile_list_gmlpt_relu_resL_kernel(
@@ -94,9 +95,6 @@ def tile_list_gmlpt_relu_resL_kernel(
         last_planes = held([P, 2, CHUNK_WORDS], I32, "last_planes")
         for tile in planes + [middle_planes, last_planes]:
             nc.vector.memset(tile[:], 0)
-        warm = keep.tile([P, 2, 8], F32, name="warm")
-        nc.gpsimd.memset(warm[:, 0, :], 0.0)
-        nc.scalar.activation(warm[:, 1, :], warm[:, 0, :], RELU)
 
         def gather_scales(c, dst, count=1):
             nc.vector.tensor_copy(dst, scale_win[:].bitcast(U8).indirect(entries(c, count)))
@@ -230,7 +228,7 @@ def tile_list_gmlpt_relu_resL_kernel(
                 nc.scalar.activation(relu_g[n][:, t, :], bank[:], RELU)
 
         def hid_tag(n, h):
-            return "up_copy%d" % (n - 1) if n % HALVES and h == 0 else "hid%d%d" % (n, h)
+            return "up_copy%d" % (n - 1) if n % HALVES and n not in PAIRED and h == 0 else "hid%d%d" % (n, h)
 
         def width(n):
             return CHUNK if (n, -1) in BEHIND else HALF
@@ -252,6 +250,29 @@ def tile_list_gmlpt_relu_resL_kernel(
                 bank = next_bank()
                 first_products(bank[:], 1, n, t, 0, CHUNK)
                 nc.scalar.copy(up_copy[n][:, t, :], bank[:])
+
+        def up_pairs(n, h):
+            lo, hi = HALF * h, HALF * (h + 1)
+            pairs = held([P, PAIR, HALF, PAIR], BF16, "pairs%d%d" % (n, h), "pairs1" if h else "up_copy%d" % (n - 1))
+            for u in range(PAIR):
+                bank = next_bank()
+                places = bank[:].rearrange("p (t j) -> p t j", t=PAIR)
+                for t in range(PAIR):
+                    first_products(places[:, t, :], 1, n, PAIR * u + t, lo, hi)
+                nc.vector.tensor_tensor(
+                    pairs[:, u].rearrange("p (g i) t -> p g t i", i=PAIR),
+                    places.rearrange("p t (g i) -> p g t i", i=PAIR),
+                    relu_g[n][:, PAIR * u : PAIR * (u + 1), lo:hi].rearrange("p t (g i) -> p g t i", i=PAIR),
+                    MULT,
+                )
+            part, at = lo // width(n), lo // width(n) * width(n)
+            if (n, part) not in hid:
+                hid[n, part] = held([P, width(n), PACK], BF16, "hid%d%d" % (n, part), hid_tag(n, part))
+            words = hid[n, part][:, lo - at : hi - at, :].rearrange("p j t -> p (j t)").bitcast(U32)
+            nc.scalar.copy(
+                words.rearrange("p (j u) -> p j u", u=PAIR),
+                pairs[:].rearrange("p u j t -> p u (j t)").bitcast(U32).rearrange("p u j -> p j u"),
+            )
 
         def up_narrow(n, s):
             bank = next_bank()
@@ -352,6 +373,9 @@ def tile_list_gmlpt_relu_resL_kernel(
                 gate(n + 1)
             if a == 0:
                 up_wide(n)
+            elif n in PAIRED:
+                for h in range(2):
+                    up_pairs(n, h)
             else:
                 for s in range(PACK):
                     up_narrow(n, s)
@@ -377,11 +401,11 @@ def tile_list_gmlpt_relu_resL_kernel(
             for h in range(2):
                 look_up(n, h)
             if 0 < c < LAST and a == 0:
-                add_res(c - 1, range(OUT_TILES), hid_tag(n, 1))
+                add_res(c - 1, range(OUT_TILES), hid_tag(n, 0))
         n = STEPS - 1
         finish_from_bank(LAST - 1, 0)
         last_product(LAST - 1, 1)
-        add_res(LAST - 1, [1], hid_tag(n - 1, 1))
+        add_res(LAST - 1, [1], hid_tag(n - 1, 0))
         for s in range(PACK):
             up_narrow(n, s)
         for s in range(PACK):

@@ -32,15 +32,13 @@ STEPS = CHUNKS * HALVES
 OUT_TILES = N // P
 LINE = 4
 PAIR = 2
-W_WORDS = K_PASSES * PASS // 4
-CHUNK_WORDS = CHUNK // 4
-BANKS = 8
+ROW = PASS // 4
+SET = 4
 ALIGN = 64
 LIVE = 96
-DEPTH = 3
-MX_DEPTH = 4
-PAIRED = (3, 5)
-BEHIND = {(1, 0): (0, 1, 2), (3, -1): "last", (3, 0): (2, 0, 1), (5, -1): (2, 1, 1)}
+HID_DEPTH = 3
+MX_DEPTH = 5
+GATE, UP = 0, 1
 
 
 def tile_list_gmlpt_relu_resL_kernel(
@@ -56,12 +54,12 @@ def tile_list_gmlpt_relu_resL_kernel(
         def held(shape, dtype, name, tag=None):
             return keep.tile(shape, dtype, name=name, tag=tag or name, align_bytes=ALIGN)
 
-        banks_taken = []
+        taken = {GATE: [], UP: []}
 
-        def next_bank():
-            banks_taken.append(True)
-            count = len(banks_taken)
-            return psum.tile([P, CHUNK], F32, name="bank%d" % count, tag="bank%d" % (count % BANKS))
+        def next_bank(kind):
+            taken[kind].append(True)
+            count = len(taken[kind])
+            return psum.tile([P, CHUNK], F32, name="bank%d_%d" % (kind, count), tag="bank%d_%d" % (kind, count % SET))
 
         offsets = lists.tile([P, J // 16], U16, name="offsets")
         nc.sync.dma_start(offsets[:], offs)
@@ -71,9 +69,9 @@ def tile_list_gmlpt_relu_resL_kernel(
 
         scale_win = held([P, T // 4], I32, "scale_win")
         nc.sync.dma_start(scale_win[LIVE:P, :], tab_scales.rearrange("a s t -> s a t").bitcast(I32))
-        w_scale_raw = held([P, K_PASSES, R // 4], I32, "w_scale_raw")
+        w_scale_raw = [held([P, R // 4], I32, "w_scale_raw%d" % x) for x in (GATE, UP)]
         for x, w_scales in enumerate((wg_scales, wu_scales)):
-            nc.scalar.dma_start(w_scale_raw[LIVE + x : P : 2, :, :], w_scales.rearrange("k s c -> s k c").bitcast(I32))
+            nc.scalar.dma_start(w_scale_raw[x][LIVE:P, :], w_scales.rearrange("k s c -> s k c").bitcast(I32))
         word_win = held([P, T], I32, "word_win")
         nc.sync.dma_start(word_win[:], tab_words[0].rearrange("p t b -> p (t b)").bitcast(I32))
         wg_first = [held([P, PASS], I32, "wg_first%d" % kp) for kp in range(K_PASSES)]
@@ -88,53 +86,50 @@ def tile_list_gmlpt_relu_resL_kernel(
 
         wg_second = held([P, K_PASSES, PASS], I32, "wg_second")
         nc.sync.dma_start(wg_second[:], wg_words[:, :, PASS:, :].rearrange("k p r i -> p k (r i)").bitcast(I32))
-
-        nc.vector.memset(scale_win[0:LIVE, :], 0)
-        planes = [held([P, 2, W_WORDS + CHUNK_WORDS * (1 - a)], I32, "planes%d" % a) for a in range(HALVES)]
-        middle_planes = held([P, 2, 2 * CHUNK_WORDS], I32, "middle_planes")
-        last_planes = held([P, 2, CHUNK_WORDS], I32, "last_planes")
-        for tile in planes + [middle_planes, last_planes]:
-            nc.vector.memset(tile[:], 0)
-
-        def gather_scales(c, dst, count=1):
-            nc.vector.tensor_copy(dst, scale_win[:].bitcast(U8).indirect(entries(c, count)))
-
-        def move_scales(queue, src, dst):
-            for quad in range(4):
-                queue.dma_start(dst[32 * quad : 32 * quad + 4, :, :], src[LIVE + 8 * quad : LIVE + 8 * quad + 8, :])
-
-        def table_plane(c, kp, lo, hi):
-            if c == 0:
-                return planes[0][:, kp, W_WORDS:].bitcast(U8)[:, lo:hi]
-            if c == LAST:
-                return last_planes[:, kp, :].bitcast(U8)[:, lo:hi]
-            return middle_planes[:, kp, :].bitcast(U8)[:, (c - 1) * CHUNK + lo : (c - 1) * CHUNK + hi]
-
-        def weight_plane(x, kp, a, t):
-            at = (kp * PACK + t) * (P // 4)
-            return planes[a][:, x, at : at + P // 4].bitcast(U8)
-
-        def sort_weight_scales(a, staged):
-            nc.vector.tensor_copy(
-                staged[LIVE:P, 0:W_WORDS].rearrange("p (k t b e) -> p k t b e", k=K_PASSES, t=PACK, e=RUN // 4),
-                w_scale_raw[LIVE:P, :, PASS // 4 * a : PASS // 4 * (a + 1)].rearrange(
-                    "p k (b t e) -> p k t b e", t=PACK, e=RUN // 4
-                ),
-            )
-
-        staged_first = held([P, W_WORDS + CHUNK_WORDS], I32, "staged_first")
-        sort_weight_scales(0, staged_first)
-        picked_first = shared.tile([P, CHUNK], U8, name="picked_first", offset=4 * W_WORDS - HALF, align_bytes=ALIGN)
-        gather_scales(0, picked_first[:])
-        nc.vector.tensor_copy(staged_first[LIVE:P, W_WORDS:], picked_first[LIVE:P, :].bitcast(I32))
-        move_scales(nc.scalar, staged_first, planes[0][:])
-        staged_second = shared.tile([P, W_WORDS], I32, name="staged_second", offset=0, align_bytes=ALIGN)
-        sort_weight_scales(1, staged_second)
-        move_scales(nc.scalar, staged_second, planes[1][:])
-        picked_rest = shared.tile([P, 2 * CHUNK], U8, name="picked_rest", offset=4 * W_WORDS, align_bytes=ALIGN)
-        gather_scales(1, picked_rest[:], 2)
-        move_scales(nc.scalar, picked_rest[:].bitcast(I32), middle_planes[:])
         wu_raw = [load_wu(a) for a in range(HALVES)]
+
+        groups = ([("w", GATE, 0), ("t", 0)], [("w", GATE, 1), ("w", UP, 0), ("w", UP, 1)], [("t", 1), ("t", 2)], [("t", LAST)])
+        nc.vector.memset(scale_win[0:LIVE, :], 0)
+        planes, place = [], {}
+        for g, members in enumerate(groups):
+            planes.append(held([P, K_PASSES, ROW * len(members)], I32, "planes%d" % g))
+            nc.vector.memset(planes[g][:], 0)
+            for i, member in enumerate(members):
+                place[member] = (g, ROW * i)
+
+        def plane(member, kp, lo, hi):
+            g, at = place[member]
+            return planes[g][:, kp, at : at + ROW].bitcast(U8)[:, lo:hi]
+
+        def gather_scales(picked, c, count):
+            nc.vector.tensor_copy(picked[:], scale_win[:].bitcast(U8).indirect(entries(c, count)))
+            return picked[:].bitcast(I32)
+
+        def move_scales(queue, src, g):
+            for quad in range(4):
+                queue.dma_start(planes[g][32 * quad : 32 * quad + 4, :, :], src[LIVE + 8 * quad : LIVE + 8 * quad + 8, :])
+
+        def sort_scales(staged, g):
+            for member in groups[g]:
+                if member[0] == "w":
+                    x, a = member[1:]
+                    at = place[member][1]
+                    nc.vector.tensor_copy(
+                        staged[LIVE:P, at : at + ROW].rearrange("p (t b e) -> p t b e", t=PACK, e=RUN // 4),
+                        w_scale_raw[x][LIVE:P, ROW * a : ROW * (a + 1)].rearrange("p (b t e) -> p t b e", t=PACK, e=RUN // 4),
+                    )
+            return staged
+
+        staged = sort_scales(held([P, ROW * len(groups[0])], I32, "staged_first"), 0)
+        next_bytes = 4 * ROW * len(groups[1])
+        picked = shared.tile([P, CHUNK], U8, name="picked_first", offset=next_bytes - HALF, align_bytes=ALIGN)
+        nc.vector.tensor_copy(staged[LIVE:P, ROW:], gather_scales(picked, 0, 1)[LIVE:P, :])
+        move_scales(nc.scalar, staged, 0)
+        staged = shared.tile([P, ROW * len(groups[1])], I32, name="staged_next", offset=0, align_bytes=ALIGN)
+        move_scales(nc.scalar, sort_scales(staged, 1), 1)
+        picked = shared.tile([P, 2 * CHUNK], U8, name="picked_next", offset=next_bytes, align_bytes=ALIGN)
+        move_scales(nc.scalar, gather_scales(picked, 1, 2), 2)
+
         res_win = [held([P, T], F32, "res_win%d" % m) for m in range(OUT_TILES)]
         nc.sync.dma_start(res_win[0][:], rT[0:P, :])
         wd_raw = [held([P, PACK, N], F32, "wd_raw%d" % a) for a in range(HALVES)]
@@ -153,8 +148,8 @@ def tile_list_gmlpt_relu_resL_kernel(
         def by_pass(c):
             return both[c][:].bitcast(U16).rearrange("p (j d) -> p d j", d=K_PASSES)
 
-        def part_words(c):
-            parted = held([P, K_PASSES, 2 * CHUNK], U8, "parted%d" % c)
+        def part_words(c, tag=None):
+            parted = held([P, K_PASSES, 2 * CHUNK], U8, "parted%d" % c, tag)
             nc.vector.tensor_copy(parted[:].bitcast(U16), by_pass(c))
             for kp in range(K_PASSES):
                 table[c, kp] = parted[:, kp, :]
@@ -170,6 +165,15 @@ def tile_list_gmlpt_relu_resL_kernel(
             )
             wg_sorted[0, kp] = ordered[:]
 
+        def sort_wg_second():
+            ordered = held([P, PACK, K_PASSES, P], I32, "wg_sorted1")
+            nc.vector.tensor_copy(
+                ordered[:].rearrange("p t k (b e) -> p t (k b) e", e=RUN),
+                wg_second[:].rearrange("p k (b t e) -> p t (k b) e", t=PACK, e=RUN),
+            )
+            for kp in range(K_PASSES):
+                wg_sorted[1, kp] = ordered[:, :, kp, :]
+
         def sort_wu(a):
             wu_sorted[a] = held([P, PACK, K_PASSES, P // 2], I32, "wu_sorted%d" % a)
             nc.vector.tensor_copy(
@@ -180,25 +184,16 @@ def tile_list_gmlpt_relu_resL_kernel(
         gather_words(0, "both0")
         for kp in range(K_PASSES):
             first_operands(kp)
-        gather_words(1, "both0")
-        ordered = held([P, PACK, K_PASSES, P], I32, "wg_sorted1")
-        nc.vector.tensor_copy(
-            ordered[:].rearrange("p t k (b e) -> p t (k b) e", e=RUN),
-            wg_second[:].rearrange("p k (b t e) -> p t (k b) e", t=PACK, e=RUN),
-        )
-        for kp in range(K_PASSES):
-            wg_sorted[1, kp] = ordered[:, :, kp, :]
-        part_words(1)
+        sort_wg_second()
         sort_wu(0)
-        gather_words(2, "wg_second")
-        picked_last = held([P, CHUNK], U8, "picked_last", "both0")
-        gather_scales(LAST, picked_last[:])
-        move_scales(nc.sync, picked_last[:].bitcast(I32), last_planes[:])
-        part_words(2)
+        gather_words(1, "wg_second")
         sort_wu(1)
-        gather_words(LAST, "wu_raw0")
+        part_words(1)
+        gather_words(2, "wu_raw1")
+        gather_words(LAST, "wg_second")
+        part_words(2)
 
-        relu_g, up_copy, hid, hid_mx, res, y = {}, {}, {}, {}, {}, {}
+        relu_g, hid, hid_mx, res, y = {}, {}, {}, {}, {}
 
         def first_products(acc, x, n, t, lo, hi, passes=range(K_PASSES)):
             c, a = divmod(n, HALVES)
@@ -206,80 +201,64 @@ def tile_list_gmlpt_relu_resL_kernel(
                 nc.tensor.matmul_mx(
                     out=acc,
                     lhsT=(wg_sorted[a, kp][:, t, :].bitcast(FP8X4), wu_sorted[a][:, t, kp, :].bitcast(FP4X4))[x],
-                    lhsT_scale=weight_plane(x, kp, a, t),
+                    lhsT_scale=plane(("w", x, a), kp, P * t, P * (t + 1)),
                     rhs=table[c, kp][:, 2 * lo : 2 * hi].bitcast(FP4X4),
-                    rhs_scale=table_plane(c, kp, lo, hi),
+                    rhs_scale=plane(("t", c), kp, lo, hi),
                     start=(kp == 0),
                     stop=(kp == K_PASSES - 1),
                 )
 
-        def relu_tag(n):
-            return {3: "word_win", 5: "wd_raw0"}.get(n, "relu%d" % (n % DEPTH))
+        def relu_tag(n, u):
+            return "relu%d%d" % (n, u)
 
         def gate(n):
             if n == 0:
-                opened = [next_bank() for t in range(PACK)]
+                opened = [next_bank(GATE) for t in range(PACK)]
                 for t in range(PACK):
-                    first_products(opened[t][:], 0, n, t, 0, CHUNK, [0])
-            relu_g[n] = held([P, PACK, CHUNK], F32, "relu_g%d" % n, relu_tag(n))
+                    first_products(opened[t][:], GATE, n, t, 0, CHUNK, [0])
+            shape = [P, PACK, CHUNK] if n == STEPS - 1 else [P, PAIR, CHUNK]
+            for u in range(PACK // shape[1]):
+                relu_g[n, u] = held(shape, F32, "relu_g%d%d" % (n, u), "word_win" if n == STEPS - 1 else relu_tag(n, u))
             for t in range(PACK):
-                bank = opened[t] if n == 0 else next_bank()
-                first_products(bank[:], 0, n, t, 0, CHUNK, [1] if n == 0 else range(K_PASSES))
-                nc.scalar.activation(relu_g[n][:, t, :], bank[:], RELU)
+                bank = opened[t] if n == 0 else next_bank(GATE)
+                first_products(bank[:], GATE, n, t, 0, CHUNK, [1] if n == 0 else range(K_PASSES))
+                nc.scalar.activation(relu_g[n, t // shape[1]][:, t % shape[1], :], bank[:], RELU)
 
-        def hid_tag(n, h):
-            return "up_copy%d" % (n - 1) if n % HALVES and n not in PAIRED and h == 0 else "hid%d%d" % (n, h)
-
-        def width(n):
-            return CHUNK if (n, -1) in BEHIND else HALF
-
-        def product(n, lo, hi, up_values):
-            h, at = lo // width(n), lo // width(n) * width(n)
-            if (n, h) not in hid:
-                hid[n, h] = held([P, width(n), PACK], BF16, "hid%d%d" % (n, h), hid_tag(n, h))
-            nc.vector.tensor_tensor(
-                hid[n, h][:, lo - at : hi - at, :].rearrange("p (g i) t -> p g t i", i=PAIR),
-                up_values.rearrange("p t (g i) -> p g t i", i=PAIR),
-                relu_g[n][:, :, lo:hi].rearrange("p t (g i) -> p g t i", i=PAIR),
-                MULT,
-            )
-
-        def up_wide(n):
-            up_copy[n] = held([P, PACK, CHUNK], F32, "up_copy%d" % n)
-            for t in range(PACK):
-                bank = next_bank()
-                first_products(bank[:], 1, n, t, 0, CHUNK)
-                nc.scalar.copy(up_copy[n][:, t, :], bank[:])
-
-        def up_pairs(n, h):
-            lo, hi = HALF * h, HALF * (h + 1)
-            pairs = held([P, PAIR, HALF, PAIR], BF16, "pairs%d%d" % (n, h), "pairs1" if h else "up_copy%d" % (n - 1))
-            for u in range(PAIR):
-                bank = next_bank()
-                places = bank[:].rearrange("p (t j) -> p t j", t=PAIR)
-                for t in range(PAIR):
-                    first_products(places[:, t, :], 1, n, PAIR * u + t, lo, hi)
-                nc.vector.tensor_tensor(
-                    pairs[:, u].rearrange("p (g i) t -> p g t i", i=PAIR),
-                    places.rearrange("p t (g i) -> p g t i", i=PAIR),
-                    relu_g[n][:, PAIR * u : PAIR * (u + 1), lo:hi].rearrange("p t (g i) -> p g t i", i=PAIR),
-                    MULT,
+        def up_pairs(n):
+            hid[n] = held([P, CHUNK, PACK], BF16, "hid%d" % n, "hid%d" % (n % HID_DEPTH))
+            for h in range(2):
+                lo, hi = HALF * h, HALF * (h + 1)
+                pairs = held([P, PAIR, HALF, PAIR], BF16, "pairs%d%d" % (n, h), "pairs%d%d" % (n % 2, h))
+                for u in range(PAIR):
+                    bank = next_bank(UP)
+                    places = bank[:].rearrange("p (t j) -> p t j", t=PAIR)
+                    for t in range(PAIR):
+                        first_products(places[:, t, :], UP, n, PAIR * u + t, lo, hi)
+                    nc.vector.tensor_tensor(
+                        pairs[:, u].rearrange("p (g i) t -> p g t i", i=PAIR),
+                        places.rearrange("p t (g i) -> p g t i", i=PAIR),
+                        relu_g[n, u][:, :, lo:hi].rearrange("p t (g i) -> p g t i", i=PAIR),
+                        MULT,
+                    )
+                words = hid[n][:, lo:hi, :].rearrange("p j t -> p (j t)").bitcast(U32)
+                nc.scalar.copy(
+                    words.rearrange("p (j u) -> p j u", u=PAIR),
+                    pairs[:].rearrange("p u j t -> p u (j t)").bitcast(U32).rearrange("p u j -> p j u"),
                 )
-            part, at = lo // width(n), lo // width(n) * width(n)
-            if (n, part) not in hid:
-                hid[n, part] = held([P, width(n), PACK], BF16, "hid%d%d" % (n, part), hid_tag(n, part))
-            words = hid[n, part][:, lo - at : hi - at, :].rearrange("p j t -> p (j t)").bitcast(U32)
-            nc.scalar.copy(
-                words.rearrange("p (j u) -> p j u", u=PAIR),
-                pairs[:].rearrange("p u j t -> p u (j t)").bitcast(U32).rearrange("p u j -> p j u"),
-            )
 
         def up_narrow(n, s):
-            bank = next_bank()
+            lo, hi = SUB * s, SUB * (s + 1)
+            bank = next_bank(UP)
             places = bank[:].rearrange("p (t j) -> p t j", t=PACK)
             for t in range(PACK):
-                first_products(places[:, t, :], 1, n, t, SUB * s, SUB * (s + 1))
-            product(n, SUB * s, SUB * (s + 1), places)
+                first_products(places[:, t, :], UP, n, t, lo, hi)
+            hid[n, s] = held([P, SUB, PACK], BF16, "hid%d%d" % (n, s))
+            nc.vector.tensor_tensor(
+                hid[n, s][:].rearrange("p (g i) t -> p g t i", i=PAIR),
+                places.rearrange("p t (g i) -> p g t i", i=PAIR),
+                relu_g[n, 0][:, :, lo:hi].rearrange("p t (g i) -> p g t i", i=PAIR),
+                MULT,
+            )
 
         wd_codes = held([P, HALVES, N], U32, "wd_codes")
         wd_scales = held([P, HALVES, N], U8, "wd_scales")
@@ -291,17 +270,14 @@ def tile_list_gmlpt_relu_resL_kernel(
                 wd_raw[a][:].rearrange("p t (g i) -> p g t i", i=LINE),
             )
 
-        def quantise(n, lo, hi):
+        def quantise(n, lo, hi, values):
             if lo == 0:
                 codes = held([P, CHUNK], U32, "codes%d" % n, "codes%d" % (n % MX_DEPTH))
                 scales = held([P, CHUNK], U8, "scales%d" % n, "scales%d" % (n % MX_DEPTH))
                 hid_mx[n] = (codes, scales)
             codes, scales = hid_mx[n]
-            h, at = lo // width(n), lo // width(n) * width(n)
             nc.vector.quantize_mx(
-                out=codes[:, lo:hi].bitcast(FP8X4),
-                scales=scales[:, lo:hi],
-                in_=hid[n, h][:, lo - at : hi - at, :].rearrange("p j t -> p (j t)"),
+                out=codes[:, lo:hi].bitcast(FP8X4), scales=scales[:, lo:hi], in_=values[:].rearrange("p j t -> p (j t)")
             )
 
         def down(c, m, lo, hi, acc):
@@ -317,20 +293,40 @@ def tile_list_gmlpt_relu_resL_kernel(
                     stop=(a == HALVES - 1),
                 )
 
-        def last_product(c, m):
-            bank = next_bank()
-            down(c, m, 0, CHUNK, bank[:])
-            y[c, m] = held([P, CHUNK], F32, "y%d%d" % (c, m))
-            nc.scalar.copy(y[c, m][:], bank[:])
+        def store(c, m, total):
+            nc.sync.dma_start(out[m * P : (m + 1) * P, c * CHUNK : (c + 1) * CHUNK], total[:])
 
-        def add_res(c, tiles, tag):
-            whole = held([P, len(tiles), CHUNK], F32, "total%d" % c, tag)
-            for i, m in enumerate(tiles):
-                nc.gpsimd.tensor_tensor(whole[:, i, :], y[c, m][:], res[c, m], ADD)
-                nc.sync.dma_start(out[m * P : (m + 1) * P, c * CHUNK : (c + 1) * CHUNK], whole[:, i, :])
+        def last_product(c):
+            for m in range(OUT_TILES):
+                bank = next_bank(GATE)
+                down(c, m, 0, CHUNK, bank[:])
+                y[c, m] = held([P, CHUNK], F32, "y%d%d" % (c, m))
+                nc.scalar.copy(y[c, m][:], bank[:])
+
+        def gather_and_add(c, m, tag=None):
+            total = held([P, CHUNK], F32, "total%d%d" % (c, m), tag)
+            nc.vector.tensor_tensor(total[:], res_win[m][:].indirect(entries(c)), y[c, m][:], ADD)
+            store(c, m, total)
+
+        def gather_res(c, m, tag):
+            if c < LAST:
+                res[c, m] = held([P, CHUNK], F32, "res%d%d" % (c, m), tag)[:]
+            else:
+                if m == 0:
+                    res[c] = held([P, OUT_TILES, CHUNK], F32, "res%d" % c, tag)
+                res[c, m] = res[c][:, m, :]
+            nc.vector.tensor_copy(res[c, m], res_win[m][:].indirect(entries(c)))
+
+        def finish_from_bank(c):
+            for m in range(OUT_TILES):
+                bank = next_bank(GATE)
+                down(c, m, 0, CHUNK, bank[:])
+                total = held([P, CHUNK], F32, "total%d%d" % (c, m))
+                nc.vector.tensor_tensor(total[:], bank[:], res[c, m], ADD)
+                store(c, m, total)
 
         def finish_last(lo, hi):
-            bank = next_bank()
+            bank = next_bank(GATE)
             acc = bank[:, 0 : OUT_TILES * (hi - lo)].rearrange("p (m j) -> p m j", m=OUT_TILES)
             for m in range(OUT_TILES):
                 down(LAST, m, lo, hi, acc[:, m, :])
@@ -340,74 +336,42 @@ def tile_list_gmlpt_relu_resL_kernel(
                 out.rearrange("(m p) j -> p m j", p=P)[:, :, LAST * CHUNK + lo : LAST * CHUNK + hi], last[:]
             )
 
-        def look_up(n, h):
-            what = BEHIND.get((n, h))
-            tag = relu_tag(n) if h < 0 else hid_tag(n, h)
-            if what == "last":
-                res[LAST] = held([P, OUT_TILES, CHUNK], F32, "res_last", tag)
-                for m in range(OUT_TILES):
-                    nc.vector.tensor_copy(res[LAST][:, m, :], res_win[m][:].indirect(entries(LAST)))
-            elif what:
-                c, m, count = what
-                picked = held([P, count * CHUNK], F32, "res%d%d" % (c, m), tag)
-                nc.vector.tensor_copy(picked[:], res_win[m][:].indirect(entries(c, count)))
-                for i in range(count):
-                    res[c + i, m] = picked[:, i * CHUNK : (i + 1) * CHUNK]
-
-        def finish_from_bank(c, m):
-            bank = next_bank()
-            down(c, m, 0, CHUNK, bank[:])
-            whole = held([P, CHUNK], F32, "total%d%d" % (c, m))
-            nc.vector.tensor_tensor(whole[:], bank[:], res[c, m], ADD)
-            nc.sync.dma_start(out[m * P : (m + 1) * P, c * CHUNK : (c + 1) * CHUNK], whole[:])
-
-        early = held([P, 2 * CHUNK], F32, "res_early", "wg_second")
-        nc.vector.tensor_copy(early[:], res_win[0][:].indirect(entries(0, 2)))
-        for c in range(2):
-            res[c, 0] = early[:, c * CHUNK : (c + 1) * CHUNK]
-        part_words(LAST)
         gate(0)
         for n in range(STEPS - 1):
-            c, a = divmod(n, HALVES)
-            if n + 1 < STEPS - 1:
-                gate(n + 1)
-            if a == 0:
-                up_wide(n)
-            elif n in PAIRED:
-                for h in range(2):
-                    up_pairs(n, h)
-            else:
-                for s in range(PACK):
-                    up_narrow(n, s)
-            if c == 0:
-                cast_wd(a)
-            if 0 < c < LAST and a == 0:
-                for m in range(OUT_TILES):
-                    last_product(c - 1, m)
+            gate(n + 1)
+            up_pairs(n)
             if n == STEPS - 2:
-                gate(n + 1)
-            if a == 0:
-                for lo in (0, HALF):
-                    product(n, lo, lo + HALF, up_copy[n][:, :, lo : lo + HALF])
-            look_up(n, -1)
-            for lo in range(0, CHUNK, width(n)):
-                quantise(n, lo, lo + width(n))
+                finish_from_bank(LAST - 1)
+            if n == 0:
+                gather_res(LAST - 1, 0, relu_tag(n, 0))
+                part_words(LAST, relu_tag(n, 1))
+            if n == 1:
+                picked = held([P, CHUNK], U8, "picked_last", relu_tag(n, 0))
+                move_scales(nc.sync, gather_scales(picked, LAST, 1), 3)
+            if n == 2:
+                for m in range(OUT_TILES):
+                    gather_res(LAST, m, relu_tag(n, 0))
+            if n == 4:
+                gather_and_add(0, 1, relu_tag(n, 0))
+            if n == 5:
+                gather_and_add(1, 1, relu_tag(n, 0))
+            quantise(n, 0, CHUNK, hid[n])
+            if n < HALVES:
+                cast_wd(n)
             if n == 1:
                 nc.vector.quantize_mx(
                     out=wd_codes[:].rearrange("p a n -> p (a n)").bitcast(FP8X4),
                     scales=wd_scales[:].rearrange("p a n -> p (a n)"),
                     in_=wd_bf[:].rearrange("p a n t -> p (a n t)"),
                 )
-            for h in range(2):
-                look_up(n, h)
-            if 0 < c < LAST and a == 0:
-                add_res(c - 1, range(OUT_TILES), hid_tag(n, 0))
+            if n == 3:
+                gather_res(LAST - 1, 1, relu_tag(n, 0))
+            if n in (3, 4):
+                last_product(n - 3)
+                gather_and_add(n - 3, 0)
         n = STEPS - 1
-        finish_from_bank(LAST - 1, 0)
-        last_product(LAST - 1, 1)
-        add_res(LAST - 1, [1], hid_tag(n - 1, 0))
         for s in range(PACK):
             up_narrow(n, s)
         for s in range(PACK):
-            quantise(n, SUB * s, SUB * (s + 1))
+            quantise(n, SUB * s, SUB * (s + 1), hid[n, s])
             finish_last(SUB * s, SUB * (s + 1))

@@ -184,20 +184,20 @@ def tile_list_gmlpt_relu_resL_kernel(
         gather_words(0, "both0")
         for kp in range(K_PASSES):
             first_operands(kp)
+        gather_words(1, "both0")
         sort_wg_second()
         sort_wu(0)
-        gather_words(1, "wg_second")
+        part_words(1, "wg_second")
+        gather_words(2, "wu_raw0")
         sort_wu(1)
-        part_words(1)
-        gather_words(2, "wu_raw1")
-        gather_words(LAST, "wg_second")
+        gather_words(LAST, "both0")
         part_words(2)
 
         relu_g, hid, hid_mx, res, y = {}, {}, {}, {}, {}
 
-        def first_products(acc, x, n, t, lo, hi, passes=range(K_PASSES)):
+        def first_products(acc, x, n, t, lo, hi):
             c, a = divmod(n, HALVES)
-            for kp in passes:
+            for kp in range(K_PASSES):
                 nc.tensor.matmul_mx(
                     out=acc,
                     lhsT=(wg_sorted[a, kp][:, t, :].bitcast(FP8X4), wu_sorted[a][:, t, kp, :].bitcast(FP4X4))[x],
@@ -212,16 +212,12 @@ def tile_list_gmlpt_relu_resL_kernel(
             return "relu%d%d" % (n, u)
 
         def gate(n):
-            if n == 0:
-                opened = [next_bank(GATE) for t in range(PACK)]
-                for t in range(PACK):
-                    first_products(opened[t][:], GATE, n, t, 0, CHUNK, [0])
             shape = [P, PACK, CHUNK] if n == STEPS - 1 else [P, PAIR, CHUNK]
             for u in range(PACK // shape[1]):
                 relu_g[n, u] = held(shape, F32, "relu_g%d%d" % (n, u), "word_win" if n == STEPS - 1 else relu_tag(n, u))
             for t in range(PACK):
-                bank = opened[t] if n == 0 else next_bank(GATE)
-                first_products(bank[:], GATE, n, t, 0, CHUNK, [1] if n == 0 else range(K_PASSES))
+                bank = next_bank(GATE if n else UP)
+                first_products(bank[:], GATE, n, t, 0, CHUNK)
                 nc.scalar.activation(relu_g[n, t // shape[1]][:, t % shape[1], :], bank[:], RELU)
 
         def up_pairs(n):
@@ -296,8 +292,8 @@ def tile_list_gmlpt_relu_resL_kernel(
         def store(c, m, total):
             nc.sync.dma_start(out[m * P : (m + 1) * P, c * CHUNK : (c + 1) * CHUNK], total[:])
 
-        def last_product(c):
-            for m in range(OUT_TILES):
+        def last_product(c, tiles):
+            for m in tiles:
                 bank = next_bank(GATE)
                 down(c, m, 0, CHUNK, bank[:])
                 y[c, m] = held([P, CHUNK], F32, "y%d%d" % (c, m))
@@ -317,13 +313,17 @@ def tile_list_gmlpt_relu_resL_kernel(
                 res[c, m] = res[c][:, m, :]
             nc.vector.tensor_copy(res[c, m], res_win[m][:].indirect(entries(c)))
 
-        def finish_from_bank(c):
-            for m in range(OUT_TILES):
-                bank = next_bank(GATE)
-                down(c, m, 0, CHUNK, bank[:])
-                total = held([P, CHUNK], F32, "total%d%d" % (c, m))
-                nc.vector.tensor_tensor(total[:], bank[:], res[c, m], ADD)
-                store(c, m, total)
+        def add_res(c, m):
+            total = held([P, CHUNK], F32, "total%d%d" % (c, m))
+            nc.gpsimd.tensor_tensor(total[:], y[c, m][:], res[c, m], ADD)
+            store(c, m, total)
+
+        def finish_from_bank(c, m):
+            bank = next_bank(GATE)
+            down(c, m, 0, CHUNK, bank[:])
+            total = held([P, CHUNK], F32, "total%d%d" % (c, m))
+            nc.vector.tensor_tensor(total[:], bank[:], res[c, m], ADD)
+            store(c, m, total)
 
         def finish_last(lo, hi):
             bank = next_bank(GATE)
@@ -341,14 +341,17 @@ def tile_list_gmlpt_relu_resL_kernel(
             gate(n + 1)
             up_pairs(n)
             if n == STEPS - 2:
-                finish_from_bank(LAST - 1)
+                for s in range(PAIR):
+                    up_narrow(n + 1, s)
             if n == 0:
-                gather_res(LAST - 1, 0, relu_tag(n, 0))
-                part_words(LAST, relu_tag(n, 1))
-            if n == 1:
                 picked = held([P, CHUNK], U8, "picked_last", relu_tag(n, 0))
                 move_scales(nc.sync, gather_scales(picked, LAST, 1), 3)
+            if n == 1:
+                gather_res(LAST - 1, 0, relu_tag(n, 0))
+                part_words(LAST, relu_tag(n, 1))
             if n == 2:
+                gather_res(LAST - 1, 1, relu_tag(n, 0))
+            if n == 3:
                 for m in range(OUT_TILES):
                     gather_res(LAST, m, relu_tag(n, 0))
             if n == 4:
@@ -364,14 +367,18 @@ def tile_list_gmlpt_relu_resL_kernel(
                     scales=wd_scales[:].rearrange("p a n -> p (a n)"),
                     in_=wd_bf[:].rearrange("p a n t -> p (a n t)"),
                 )
-            if n == 3:
-                gather_res(LAST - 1, 1, relu_tag(n, 0))
             if n in (3, 4):
-                last_product(n - 3)
+                last_product(n - 3, range(OUT_TILES))
                 gather_and_add(n - 3, 0)
         n = STEPS - 1
-        for s in range(PACK):
-            up_narrow(n, s)
-        for s in range(PACK):
+        finish_from_bank(LAST - 1, 0)
+        last_product(LAST - 1, [1])
+        add_res(LAST - 1, 1)
+        for s in range(PAIR):
             quantise(n, SUB * s, SUB * (s + 1), hid[n, s])
+        for s in range(PAIR, PACK):
+            up_narrow(n, s)
+        for s in range(PAIR, PACK):
+            quantise(n, SUB * s, SUB * (s + 1), hid[n, s])
+        for s in range(PACK):
             finish_last(SUB * s, SUB * (s + 1))

@@ -39,6 +39,7 @@ LIVE = 96
 HID_DEPTH = 3
 MX_DEPTH = 5
 GATE, UP = 0, 1
+WARM_UP = 4
 
 
 def tile_list_gmlpt_relu_resL_kernel(
@@ -181,6 +182,17 @@ def tile_list_gmlpt_relu_resL_kernel(
                 wu_raw[a][:].rearrange("p k (b t e) -> p t (k b) e", t=PACK, e=RUN // 2),
             )
 
+        idle = next_bank(GATE)
+        for i in range(WARM_UP):
+            nc.tensor.matmul_mx(
+                out=idle[:],
+                lhsT=word_win[:].bitcast(U8)[:, 0 : 2 * P].bitcast(FP4X4),
+                lhsT_scale=scale_win[:].bitcast(U8)[:, 0:P],
+                rhs=word_win[:].bitcast(U8)[:, 0 : 2 * CHUNK].bitcast(FP4X4),
+                rhs_scale=scale_win[:].bitcast(U8)[:, 0:CHUNK],
+                start=True,
+                stop=True,
+            )
         gather_words(0, "both0")
         for kp in range(K_PASSES):
             first_operands(kp)

@@ -129,7 +129,7 @@ def tile_list_gmlpt_relu_resL_kernel(
         staged = shared.tile([P, ROW * len(groups[1])], I32, name="staged_next", offset=0, align_bytes=ALIGN)
         move_scales(nc.scalar, sort_scales(staged, 1), 1)
         picked = shared.tile([P, 2 * CHUNK], U8, name="picked_next", offset=next_bytes, align_bytes=ALIGN)
-        move_scales(nc.scalar, gather_scales(picked, 1, 2), 2)
+        move_scales(nc.sync, gather_scales(picked, 1, 2), 2)
 
         res_win = [held([P, T], F32, "res_win%d" % m) for m in range(OUT_TILES)]
         nc.sync.dma_start(res_win[0][:], rT[0:P, :])
@@ -362,10 +362,10 @@ def tile_list_gmlpt_relu_resL_kernel(
                 gather_res(LAST - 1, 0, relu_tag(n, 0))
                 part_words(LAST, relu_tag(n, 1))
             if n == 2:
-                gather_res(LAST - 1, 1, relu_tag(n, 0))
+                gather_res(LAST, 0, relu_tag(n, 0))
             if n == 3:
-                for m in range(OUT_TILES):
-                    gather_res(LAST, m, relu_tag(n, 0))
+                gather_res(LAST, 1, None)
+                gather_res(LAST - 1, 1, relu_tag(n, 0))
             if n == 4:
                 gather_and_add(0, 1, relu_tag(n, 0))
             if n == 5:

@@ -39,7 +39,6 @@ LIVE = 96
 HID_DEPTH = 3
 MX_DEPTH = 5
 GATE, UP = 0, 1
-WARM_UP = 4
 
 
 def tile_list_gmlpt_relu_resL_kernel(
@@ -182,17 +181,6 @@ def tile_list_gmlpt_relu_resL_kernel(
                 wu_raw[a][:].rearrange("p k (b t e) -> p t (k b) e", t=PACK, e=RUN // 2),
             )
 
-        idle = next_bank(GATE)
-        for i in range(WARM_UP):
-            nc.tensor.matmul_mx(
-                out=idle[:],
-                lhsT=word_win[:].bitcast(U8)[:, 0 : 2 * P].bitcast(FP4X4),
-                lhsT_scale=scale_win[:].bitcast(U8)[:, 0:P],
-                rhs=word_win[:].bitcast(U8)[:, 0 : 2 * CHUNK].bitcast(FP4X4),
-                rhs_scale=scale_win[:].bitcast(U8)[:, 0:CHUNK],
-                start=True,
-                stop=True,
-            )
         gather_words(0, "both0")
         for kp in range(K_PASSES):
             first_operands(kp)

@@ -28,7 +28,6 @@ CHUNKS = J // CHUNK
 LAST = CHUNKS - 1
 HALF = CHUNK // 2
 SUB = CHUNK // PACK
-STEPS = CHUNKS * HALVES
 OUT_TILES = N // P
 LINE = 4
 PAIR = 2
@@ -39,6 +38,7 @@ LIVE = 96
 HID_DEPTH = 3
 MX_DEPTH = 5
 GATE, UP = 0, 1
+STEPS = CHUNKS * HALVES
 
 
 def tile_list_gmlpt_relu_resL_kernel(
@@ -48,7 +48,6 @@ def tile_list_gmlpt_relu_resL_kernel(
     with ExitStack() as ctx:
         lists = ctx.enter_context(tc.tile_pool(name="lists", bufs=1))
         keep = ctx.enter_context(tc.tile_pool(name="keep", bufs=1))
-        shared = ctx.enter_context(tc.tile_pool(name="shared", bufs=1))
         psum = ctx.enter_context(tc.psum_pool(name="psum", bufs=1))
 
         def held(shape, dtype, name, tag=None):
@@ -74,9 +73,12 @@ def tile_list_gmlpt_relu_resL_kernel(
             nc.scalar.dma_start(w_scale_raw[x][LIVE:P, :], w_scales.rearrange("k s c -> s k c").bitcast(I32))
         word_win = held([P, T], I32, "word_win")
         nc.sync.dma_start(word_win[:], tab_words[0].rearrange("p t b -> p (t b)").bitcast(I32))
-        wg_first = [held([P, PASS], I32, "wg_first%d" % kp) for kp in range(K_PASSES)]
-        for kp in range(K_PASSES):
-            nc.sync.dma_start(wg_first[kp][:], wg_words[kp, :, 0:PASS, :].rearrange("p r i -> p (r i)").bitcast(I32))
+
+        def load_wg(a):
+            raw = held([P, K_PASSES, PASS], I32, "wg_raw%d" % a)
+            columns = slice(PASS * a, PASS * (a + 1))
+            nc.sync.dma_start(raw[:], wg_words[:, :, columns, :].rearrange("k p r i -> p k (r i)").bitcast(I32))
+            return raw
 
         def load_wu(a):
             raw = held([P, K_PASSES, PASS // 2], I32, "wu_raw%d" % a)
@@ -84,16 +86,22 @@ def tile_list_gmlpt_relu_resL_kernel(
             nc.sync.dma_start(raw[:], wu_words[:, :, columns].rearrange("k p c -> p k c").bitcast(I32))
             return raw
 
-        wg_second = held([P, K_PASSES, PASS], I32, "wg_second")
-        nc.sync.dma_start(wg_second[:], wg_words[:, :, PASS:, :].rearrange("k p r i -> p k (r i)").bitcast(I32))
-        wu_raw = [load_wu(a) for a in range(HALVES)]
+        wg_raw, wu_raw = [], []
+        for a in range(HALVES):
+            wg_raw.append(load_wg(a))
+            wu_raw.append(load_wu(a))
 
-        groups = ([("w", GATE, 0), ("t", 0)], [("w", GATE, 1), ("w", UP, 0), ("w", UP, 1)], [("t", 1), ("t", 2)], [("t", LAST)])
+        groups = (
+            [("w", GATE, 0), ("w", UP, 0), ("t", 0)],
+            [("w", GATE, 1), ("w", UP, 1)],
+            [("t", 1), ("t", 2)],
+            [("t", LAST)],
+        )
         nc.vector.memset(scale_win[0:LIVE, :], 0)
         planes, place = [], {}
         for g, members in enumerate(groups):
             planes.append(held([P, K_PASSES, ROW * len(members)], I32, "planes%d" % g))
-            nc.vector.memset(planes[g][:], 0)
+            (nc.gpsimd if g else nc.vector).memset(planes[g][:], 0)
             for i, member in enumerate(members):
                 place[member] = (g, ROW * i)
 
@@ -102,96 +110,96 @@ def tile_list_gmlpt_relu_resL_kernel(
             return planes[g][:, kp, at : at + ROW].bitcast(U8)[:, lo:hi]
 
         def gather_scales(picked, c, count):
-            nc.vector.tensor_copy(picked[:], scale_win[:].bitcast(U8).indirect(entries(c, count)))
-            return picked[:].bitcast(I32)
+            nc.vector.tensor_copy(picked, scale_win[:].bitcast(U8).indirect(entries(c, count)))
 
         def move_scales(queue, src, g):
-            for quad in range(4):
+            for quad in (0, 2, 1, 3):
                 queue.dma_start(planes[g][32 * quad : 32 * quad + 4, :, :], src[LIVE + 8 * quad : LIVE + 8 * quad + 8, :])
 
-        def sort_scales(staged, g):
+        def sort_scales(g):
+            staged = held([P, ROW * len(groups[g])], I32, "staged%d" % g)
             for member in groups[g]:
                 if member[0] == "w":
                     x, a = member[1:]
                     at = place[member][1]
-                    nc.vector.tensor_copy(
-                        staged[LIVE:P, at : at + ROW].rearrange("p (t b e) -> p t b e", t=PACK, e=RUN // 4),
-                        w_scale_raw[x][LIVE:P, ROW * a : ROW * (a + 1)].rearrange("p (b t e) -> p t b e", t=PACK, e=RUN // 4),
+                    nc.scalar.copy(
+                        staged[LIVE:P, at : at + ROW].bitcast(U32).rearrange("p (t b e) -> p t b e", t=PACK, e=RUN // 4),
+                        w_scale_raw[x][LIVE:P, ROW * a : ROW * (a + 1)]
+                        .bitcast(U32)
+                        .rearrange("p (b t e) -> p t b e", t=PACK, e=RUN // 4),
                     )
             return staged
 
-        staged = sort_scales(held([P, ROW * len(groups[0])], I32, "staged_first"), 0)
-        next_bytes = 4 * ROW * len(groups[1])
-        picked = shared.tile([P, CHUNK], U8, name="picked_first", offset=next_bytes - HALF, align_bytes=ALIGN)
-        nc.vector.tensor_copy(staged[LIVE:P, ROW:], gather_scales(picked, 0, 1)[LIVE:P, :])
+        staged = sort_scales(0)
+        picked_first = held([P, CHUNK], U8, "picked_first")
+        gather_scales(picked_first[:], 0, 1)
+        nc.vector.tensor_copy(staged[LIVE:P, place["t", 0][1] :], picked_first[:].bitcast(I32)[LIVE:P, :])
         move_scales(nc.scalar, staged, 0)
-        staged = shared.tile([P, ROW * len(groups[1])], I32, name="staged_next", offset=0, align_bytes=ALIGN)
-        move_scales(nc.scalar, sort_scales(staged, 1), 1)
-        picked = shared.tile([P, 2 * CHUNK], U8, name="picked_next", offset=next_bytes, align_bytes=ALIGN)
-        move_scales(nc.sync, gather_scales(picked, 1, 2), 2)
+        move_scales(nc.sync, sort_scales(1), 1)
+        picked_next = held([P, 2 * CHUNK], U8, "picked_next", "picked_first")
+        gather_scales(picked_next[:], 1, 2)
 
         res_win = [held([P, T], F32, "res_win%d" % m) for m in range(OUT_TILES)]
+        move_scales(nc.sync, picked_next[:].bitcast(I32), 2)
         nc.sync.dma_start(res_win[0][:], rT[0:P, :])
         wd_raw = [held([P, PACK, N], F32, "wd_raw%d" % a) for a in range(HALVES)]
         wd_rows = wd.rearrange("(a b t q) n -> a t b q n", a=HALVES, t=PACK, q=RUN)
         for a in range(HALVES):
             for t in range(PACK):
                 nc.sync.dma_start(wd_raw[a][:, t, :], wd_rows[a, t])
+
         nc.sync.dma_start(res_win[1][:], rT[P : 2 * P, :])
 
         both, table, wg_sorted, wu_sorted = {}, {}, {}, {}
 
-        def gather_words(c, tag):
-            both[c] = held([P, CHUNK], U32, "both%d" % c, tag)
-            nc.vector.tensor_copy(both[c][:], word_win[:].bitcast(U32).indirect(entries(c)))
+        def gather_words(c, count, tag):
+            both[c] = held([P, count * CHUNK], U32, "both%d" % c, tag)
+            nc.vector.tensor_copy(both[c][:], word_win[:].bitcast(U32).indirect(entries(c, count)))
 
         def by_pass(c):
             return both[c][:].bitcast(U16).rearrange("p (j d) -> p d j", d=K_PASSES)
 
-        def part_words(c, tag=None):
-            parted = held([P, K_PASSES, 2 * CHUNK], U8, "parted%d" % c, tag)
+        def part_words(c, count, tag):
+            parted = held([P, K_PASSES, 2 * count * CHUNK], U8, "parted%d" % c, tag)
             nc.vector.tensor_copy(parted[:].bitcast(U16), by_pass(c))
-            for kp in range(K_PASSES):
-                table[c, kp] = parted[:, kp, :]
+            for i in range(count):
+                for kp in range(K_PASSES):
+                    table[c + i, kp] = parted[:, kp, 2 * i * CHUNK : 2 * (i + 1) * CHUNK]
 
-        def first_operands(kp):
+        def part_first(kp):
             parted = held([P, 2 * CHUNK], U8, "parted0%d" % kp)
             nc.vector.tensor_copy(parted[:].bitcast(U16), by_pass(0)[:, kp, :])
             table[0, kp] = parted[:]
-            ordered = held([P, PACK, P], I32, "wg_sorted0%d" % kp)
-            nc.vector.tensor_copy(
-                ordered[:].rearrange("p t (b e) -> p t b e", e=RUN),
-                wg_first[kp][:].rearrange("p (b t e) -> p t b e", t=PACK, e=RUN),
-            )
-            wg_sorted[0, kp] = ordered[:]
 
-        def sort_wg_second():
-            ordered = held([P, PACK, K_PASSES, P], I32, "wg_sorted1")
-            nc.vector.tensor_copy(
+        def sort_wg(a, first, count):
+            ordered = held([P, count, K_PASSES, P], U32, "wg_sorted%d%d" % (a, first))
+            nc.scalar.copy(
                 ordered[:].rearrange("p t k (b e) -> p t (k b) e", e=RUN),
-                wg_second[:].rearrange("p k (b t e) -> p t (k b) e", t=PACK, e=RUN),
+                wg_raw[a][:].bitcast(U32).rearrange("p k (b t e) -> p t (k b) e", t=PACK, e=RUN)[:, first : first + count],
             )
-            for kp in range(K_PASSES):
-                wg_sorted[1, kp] = ordered[:, :, kp, :]
+            for t in range(count):
+                for kp in range(K_PASSES):
+                    wg_sorted[a, kp, first + t] = ordered[:, t, kp, :]
 
         def sort_wu(a):
-            wu_sorted[a] = held([P, PACK, K_PASSES, P // 2], I32, "wu_sorted%d" % a)
-            nc.vector.tensor_copy(
+            wu_sorted[a] = held([P, PACK, K_PASSES, P // 2], U32, "wu_sorted%d" % a)
+            nc.scalar.copy(
                 wu_sorted[a][:].rearrange("p t k (b e) -> p t (k b) e", e=RUN // 2),
-                wu_raw[a][:].rearrange("p k (b t e) -> p t (k b) e", t=PACK, e=RUN // 2),
+                wu_raw[a][:].bitcast(U32).rearrange("p k (b t e) -> p t (k b) e", t=PACK, e=RUN // 2),
             )
 
-        gather_words(0, "both0")
+        gather_words(0, 1, None)
         for kp in range(K_PASSES):
-            first_operands(kp)
-        gather_words(1, "both0")
-        sort_wg_second()
+            part_first(kp)
+        sort_wg(0, 0, 1)
+        sort_wg(0, 1, 1)
+        sort_wg(0, PAIR, PAIR)
+        gather_words(1, 2, "both0")
+        gather_words(LAST, 1, "wg_raw0")
         sort_wu(0)
-        part_words(1, "wg_second")
-        gather_words(2, "wu_raw0")
-        sort_wu(1)
-        gather_words(LAST, "both0")
-        part_words(2)
+        part_words(1, 2, "wu_raw0")
+        for u in range(PAIR):
+            sort_wg(1, PAIR * u, PAIR)
 
         relu_g, hid, hid_mx, res, y = {}, {}, {}, {}, {}
 
@@ -200,7 +208,7 @@ def tile_list_gmlpt_relu_resL_kernel(
             for kp in range(K_PASSES):
                 nc.tensor.matmul_mx(
                     out=acc,
-                    lhsT=(wg_sorted[a, kp][:, t, :].bitcast(FP8X4), wu_sorted[a][:, t, kp, :].bitcast(FP4X4))[x],
+                    lhsT=wg_sorted[a, kp, t].bitcast(FP8X4) if x == GATE else wu_sorted[a][:, t, kp, :].bitcast(FP4X4),
                     lhsT_scale=plane(("w", x, a), kp, P * t, P * (t + 1)),
                     rhs=table[c, kp][:, 2 * lo : 2 * hi].bitcast(FP4X4),
                     rhs_scale=plane(("t", c), kp, lo, hi),
@@ -211,14 +219,17 @@ def tile_list_gmlpt_relu_resL_kernel(
         def relu_tag(n, u):
             return "relu%d%d" % (n, u)
 
-        def gate(n):
-            shape = [P, PACK, CHUNK] if n == STEPS - 1 else [P, PAIR, CHUNK]
-            for u in range(PACK // shape[1]):
-                relu_g[n, u] = held(shape, F32, "relu_g%d%d" % (n, u), "word_win" if n == STEPS - 1 else relu_tag(n, u))
-            for t in range(PACK):
-                bank = next_bank(GATE if n else UP)
-                first_products(bank[:], GATE, n, t, 0, CHUNK)
-                nc.scalar.activation(relu_g[n, t // shape[1]][:, t % shape[1], :], bank[:], RELU)
+        def gate(n, u):
+            if n < STEPS - 1:
+                relu_g[n, u] = held([P, PAIR, CHUNK], F32, "relu_g%d%d" % (n, u), relu_tag(n, u))[:]
+            else:
+                if u == 0:
+                    relu_g[n] = held([P, PACK, CHUNK], F32, "relu_g%d" % n, "word_win")
+                relu_g[n, u] = relu_g[n][:, PAIR * u : PAIR * (u + 1), :]
+            for t in range(PAIR):
+                bank = next_bank(GATE)
+                first_products(bank[:], GATE, n, PAIR * u + t, 0, CHUNK)
+                nc.scalar.activation(relu_g[n, u][:, t, :], bank[:], RELU)
 
         def up_pairs(n):
             hid[n] = held([P, CHUNK, PACK], BF16, "hid%d" % n, "hid%d" % (n % HID_DEPTH))
@@ -252,18 +263,26 @@ def tile_list_gmlpt_relu_resL_kernel(
             nc.vector.tensor_tensor(
                 hid[n, s][:].rearrange("p (g i) t -> p g t i", i=PAIR),
                 places.rearrange("p t (g i) -> p g t i", i=PAIR),
-                relu_g[n, 0][:, :, lo:hi].rearrange("p t (g i) -> p g t i", i=PAIR),
+                relu_g[n][:, :, lo:hi].rearrange("p t (g i) -> p g t i", i=PAIR),
                 MULT,
             )
 
         wd_codes = held([P, HALVES, N], U32, "wd_codes")
         wd_scales = held([P, HALVES, N], U8, "wd_scales")
+
         wd_bf = held([P, HALVES, N, PACK], BF16, "wd_bf")
 
         def cast_wd(a):
             nc.scalar.copy(
                 wd_bf[:, a].rearrange("p (g i) t -> p g t i", i=LINE),
                 wd_raw[a][:].rearrange("p t (g i) -> p g t i", i=LINE),
+            )
+
+        def quantise_wd():
+            nc.vector.quantize_mx(
+                out=wd_codes[:].rearrange("p a n -> p (a n)").bitcast(FP8X4),
+                scales=wd_scales[:].rearrange("p a n -> p (a n)"),
+                in_=wd_bf[:].rearrange("p a n t -> p (a n t)"),
             )
 
         def quantise(n, lo, hi, values):
@@ -318,8 +337,8 @@ def tile_list_gmlpt_relu_resL_kernel(
             nc.gpsimd.tensor_tensor(total[:], y[c, m][:], res[c, m], ADD)
             store(c, m, total)
 
-        def finish_from_bank(c, m):
-            bank = next_bank(GATE)
+        def finish_from_bank(c, m, kind):
+            bank = next_bank(kind)
             down(c, m, 0, CHUNK, bank[:])
             total = held([P, CHUNK], F32, "total%d%d" % (c, m))
             nc.vector.tensor_tensor(total[:], bank[:], res[c, m], ADD)
@@ -336,42 +355,46 @@ def tile_list_gmlpt_relu_resL_kernel(
                 out.rearrange("(m p) j -> p m j", p=P)[:, :, LAST * CHUNK + lo : LAST * CHUNK + hi], last[:]
             )
 
-        gate(0)
+        gated = []
         for n in range(STEPS - 1):
-            gate(n + 1)
+            while len(gated) < PAIR * (n + 1) + min(n, PAIR):
+                gate(*divmod(len(gated), PAIR))
+                gated.append(True)
+            if n == 1:
+                sort_wu(1)
             up_pairs(n)
             if n == STEPS - 2:
                 for s in range(PAIR):
                     up_narrow(n + 1, s)
             if n == 0:
-                picked = held([P, CHUNK], U8, "picked_last", relu_tag(n, 0))
-                move_scales(nc.sync, gather_scales(picked, LAST, 1), 3)
+                picked_last = held([P, CHUNK], U8, "picked_last", relu_tag(n, 0))
+                gather_scales(picked_last[:], LAST, 1)
+                move_scales(nc.sync, picked_last[:].bitcast(I32), 3)
+                part_words(LAST, 1, relu_tag(n, 1))
             if n == 1:
                 gather_res(LAST - 1, 0, relu_tag(n, 0))
-                part_words(LAST, relu_tag(n, 1))
+                gather_res(LAST, 0, relu_tag(n, 1))
             if n == 2:
-                gather_res(LAST, 0, relu_tag(n, 0))
+                gather_res(1, 0, relu_tag(n, 0))
             if n == 3:
                 gather_res(LAST, 1, None)
                 gather_res(LAST - 1, 1, relu_tag(n, 0))
             if n == 4:
-                gather_and_add(0, 1, relu_tag(n, 0))
+                finish_from_bank(1, 0, UP)
+                last_product(1, [1])
+                for m in range(OUT_TILES):
+                    gather_and_add(0, m, relu_tag(n, m))
             if n == 5:
                 gather_and_add(1, 1, relu_tag(n, 0))
             quantise(n, 0, CHUNK, hid[n])
-            if n < HALVES:
-                cast_wd(n)
-            if n == 1:
-                nc.vector.quantize_mx(
-                    out=wd_codes[:].rearrange("p a n -> p (a n)").bitcast(FP8X4),
-                    scales=wd_scales[:].rearrange("p a n -> p (a n)"),
-                    in_=wd_bf[:].rearrange("p a n t -> p (a n t)"),
-                )
-            if n in (3, 4):
-                last_product(n - 3, range(OUT_TILES))
-                gather_and_add(n - 3, 0)
+            if n in (1, 2):
+                cast_wd(n - 1)
+            if n == 2:
+                quantise_wd()
+            if n == 3:
+                last_product(0, range(OUT_TILES))
         n = STEPS - 1
-        finish_from_bank(LAST - 1, 0)
+        finish_from_bank(LAST - 1, 0, GATE)
         last_product(LAST - 1, [1])
         add_res(LAST - 1, 1)
         for s in range(PAIR):

@@ -37,6 +37,7 @@ ALIGN = 64
 LIVE = 96
 HID_DEPTH = 3
 MX_DEPTH = 5
+TABLE_LOADS = 4
 GATE, UP = 0, 1
 STEPS = CHUNKS * HALVES
 
@@ -72,7 +73,9 @@ def tile_list_gmlpt_relu_resL_kernel(
         for x, w_scales in enumerate((wg_scales, wu_scales)):
             nc.scalar.dma_start(w_scale_raw[x][LIVE:P, :], w_scales.rearrange("k s c -> s k c").bitcast(I32))
         word_win = held([P, T], I32, "word_win")
-        nc.sync.dma_start(word_win[:], tab_words[0].rearrange("p t b -> p (t b)").bitcast(I32))
+        table_rows = tab_words[0].rearrange("p t b -> p (t b)").bitcast(I32)
+        for lo in range(0, T, T // TABLE_LOADS):
+            nc.sync.dma_start(word_win[:, lo : lo + T // TABLE_LOADS], table_rows[:, lo : lo + T // TABLE_LOADS])
 
         def load_wg(a):
             raw = held([P, K_PASSES, PASS], I32, "wg_raw%d" % a)
@@ -101,7 +104,7 @@ def tile_list_gmlpt_relu_resL_kernel(
         planes, place = [], {}
         for g, members in enumerate(groups):
             planes.append(held([P, K_PASSES, ROW * len(members)], I32, "planes%d" % g))
-            (nc.gpsimd if g else nc.vector).memset(planes[g][:], 0)
+            nc.vector.memset(planes[g][:], 0)
             for i, member in enumerate(members):
                 place[member] = (g, ROW * i)
 

@@ -37,7 +37,6 @@ ALIGN = 64
 LIVE = 96
 HID_DEPTH = 3
 MX_DEPTH = 5
-TABLE_LOADS = 4
 GATE, UP = 0, 1
 STEPS = CHUNKS * HALVES
 
@@ -73,9 +72,7 @@ def tile_list_gmlpt_relu_resL_kernel(
         for x, w_scales in enumerate((wg_scales, wu_scales)):
             nc.scalar.dma_start(w_scale_raw[x][LIVE:P, :], w_scales.rearrange("k s c -> s k c").bitcast(I32))
         word_win = held([P, T], I32, "word_win")
-        table_rows = tab_words[0].rearrange("p t b -> p (t b)").bitcast(I32)
-        for lo in range(0, T, T // TABLE_LOADS):
-            nc.sync.dma_start(word_win[:, lo : lo + T // TABLE_LOADS], table_rows[:, lo : lo + T // TABLE_LOADS])
+        nc.sync.dma_start(word_win[:], tab_words[0].rearrange("p t b -> p (t b)").bitcast(I32))
 
         def load_wg(a):
             raw = held([P, K_PASSES, PASS], I32, "wg_raw%d" % a)
@@ -186,7 +183,7 @@ def tile_list_gmlpt_relu_resL_kernel(
 
         def sort_wu(a):
             wu_sorted[a] = held([P, PACK, K_PASSES, P // 2], U32, "wu_sorted%d" % a)
-            nc.scalar.copy(
+            nc.vector.tensor_copy(
                 wu_sorted[a][:].rearrange("p t k (b e) -> p t (k b) e", e=RUN // 2),
                 wu_raw[a][:].bitcast(U32).rearrange("p k (b t e) -> p t (k b) e", t=PACK, e=RUN // 2),
             )
@@ -197,10 +194,10 @@ def tile_list_gmlpt_relu_resL_kernel(
         sort_wg(0, 0, 1)
         sort_wg(0, 1, 1)
         sort_wg(0, PAIR, PAIR)
-        gather_words(1, 2, "both0")
-        gather_words(LAST, 1, "wg_raw0")
         sort_wu(0)
-        part_words(1, 2, "wu_raw0")
+        gather_words(1, 2, "both0")
+        gather_words(LAST, 1, "wu_raw0")
+        part_words(1, 2, "wg_raw0")
         for u in range(PAIR):
             sort_wg(1, PAIR * u, PAIR)
 

@@ -48,6 +48,7 @@ def tile_list_gmlpt_relu_resL_kernel(
     with ExitStack() as ctx:
         lists = ctx.enter_context(tc.tile_pool(name="lists", bufs=1))
         keep = ctx.enter_context(tc.tile_pool(name="keep", bufs=1))
+        shared = ctx.enter_context(tc.tile_pool(name="shared", bufs=1))
         psum = ctx.enter_context(tc.psum_pool(name="psum", bufs=1))
 
         def held(shape, dtype, name, tag=None):
@@ -74,26 +75,16 @@ def tile_list_gmlpt_relu_resL_kernel(
         word_win = held([P, T], I32, "word_win")
         nc.sync.dma_start(word_win[:], tab_words[0].rearrange("p t b -> p (t b)").bitcast(I32))
 
-        def load_wg(a):
-            raw = held([P, K_PASSES, PASS], I32, "wg_raw%d" % a)
-            columns = slice(PASS * a, PASS * (a + 1))
-            nc.sync.dma_start(raw[:], wg_words[:, :, columns, :].rearrange("k p r i -> p k (r i)").bitcast(I32))
+        def load_wg_first(kp):
+            raw = held([P, PASS], I32, "wg_first%d" % kp)
+            nc.sync.dma_start(raw[:], wg_words[kp, :, 0:PASS, :].rearrange("p r i -> p (r i)").bitcast(I32))
             return raw
 
-        def load_wu(a):
-            raw = held([P, K_PASSES, PASS // 2], I32, "wu_raw%d" % a)
-            columns = slice(2 * PASS * a, 2 * PASS * (a + 1))
-            nc.sync.dma_start(raw[:], wu_words[:, :, columns].rearrange("k p c -> p k c").bitcast(I32))
-            return raw
-
-        wg_raw, wu_raw = [], []
-        for a in range(HALVES):
-            wg_raw.append(load_wg(a))
-            wu_raw.append(load_wu(a))
+        wg_first = [load_wg_first(0)]
 
         groups = (
-            [("w", GATE, 0), ("w", UP, 0), ("t", 0)],
-            [("w", GATE, 1), ("w", UP, 1)],
+            [("w", GATE, 0), ("t", 0)],
+            [("w", UP, 0), ("w", GATE, 1), ("w", UP, 1)],
             [("t", 1), ("t", 2)],
             [("t", LAST)],
         )
@@ -112,9 +103,9 @@ def tile_list_gmlpt_relu_resL_kernel(
         def gather_scales(picked, c, count):
             nc.vector.tensor_copy(picked, scale_win[:].bitcast(U8).indirect(entries(c, count)))
 
-        def move_scales(queue, src, g):
+        def move_scales(src, g):
             for quad in (0, 2, 1, 3):
-                queue.dma_start(planes[g][32 * quad : 32 * quad + 4, :, :], src[LIVE + 8 * quad : LIVE + 8 * quad + 8, :])
+                nc.sync.dma_start(planes[g][32 * quad : 32 * quad + 4, :, :], src[LIVE + 8 * quad : LIVE + 8 * quad + 8, :])
 
         def sort_scales(g):
             staged = held([P, ROW * len(groups[g])], I32, "staged%d" % g)
@@ -134,13 +125,18 @@ def tile_list_gmlpt_relu_resL_kernel(
         picked_first = held([P, CHUNK], U8, "picked_first")
         gather_scales(picked_first[:], 0, 1)
         nc.vector.tensor_copy(staged[LIVE:P, place["t", 0][1] :], picked_first[:].bitcast(I32)[LIVE:P, :])
-        move_scales(nc.scalar, staged, 0)
-        move_scales(nc.sync, sort_scales(1), 1)
+        move_scales(staged, 0)
+        wg_first.append(load_wg_first(1))
+        wu_raw = held([P, K_PASSES, R // 2], I32, "wu_raw")
+        nc.sync.dma_start(wu_raw[:], wu_words.rearrange("k p c -> p k c").bitcast(I32))
+        move_scales(sort_scales(1), 1)
+        wg_second = held([P, K_PASSES, PASS], I32, "wg_second")
+        nc.sync.dma_start(wg_second[:], wg_words[:, :, PASS:, :].rearrange("k p r i -> p k (r i)").bitcast(I32))
         picked_next = held([P, 2 * CHUNK], U8, "picked_next", "picked_first")
         gather_scales(picked_next[:], 1, 2)
 
         res_win = [held([P, T], F32, "res_win%d" % m) for m in range(OUT_TILES)]
-        move_scales(nc.sync, picked_next[:].bitcast(I32), 2)
+        move_scales(picked_next[:].bitcast(I32), 2)
         nc.sync.dma_start(res_win[0][:], rT[0:P, :])
         wd_raw = [held([P, PACK, N], F32, "wd_raw%d" % a) for a in range(HALVES)]
         wd_rows = wd.rearrange("(a b t q) n -> a t b q n", a=HALVES, t=PACK, q=RUN)
@@ -152,54 +148,62 @@ def tile_list_gmlpt_relu_resL_kernel(
 
         both, table, wg_sorted, wu_sorted = {}, {}, {}, {}
 
-        def gather_words(c, count, tag):
-            both[c] = held([P, count * CHUNK], U32, "both%d" % c, tag)
+        def gather_words(c, count, offset):
+            both[c] = shared.tile([P, count * CHUNK], U32, name="both%d" % c, offset=offset, align_bytes=ALIGN)
             nc.vector.tensor_copy(both[c][:], word_win[:].bitcast(U32).indirect(entries(c, count)))
 
         def by_pass(c):
             return both[c][:].bitcast(U16).rearrange("p (j d) -> p d j", d=K_PASSES)
 
-        def part_words(c, count, tag):
-            parted = held([P, K_PASSES, 2 * count * CHUNK], U8, "parted%d" % c, tag)
+        def part_words(c, count):
+            parted = held([P, K_PASSES, 2 * count * CHUNK], U8, "parted%d" % c)
             nc.vector.tensor_copy(parted[:].bitcast(U16), by_pass(c))
             for i in range(count):
                 for kp in range(K_PASSES):
                     table[c + i, kp] = parted[:, kp, 2 * i * CHUNK : 2 * (i + 1) * CHUNK]
 
-        def part_first(kp):
+        def first_operands(kp):
             parted = held([P, 2 * CHUNK], U8, "parted0%d" % kp)
             nc.vector.tensor_copy(parted[:].bitcast(U16), by_pass(0)[:, kp, :])
             table[0, kp] = parted[:]
+            ordered = held([P, PACK, P], U32, "wg_sorted0%d" % kp)
+            nc.scalar.copy(
+                ordered[:].rearrange("p t (b e) -> p t b e", e=RUN),
+                wg_first[kp][:].bitcast(U32).rearrange("p (b t e) -> p t b e", t=PACK, e=RUN),
+            )
+            for t in range(PACK):
+                wg_sorted[0, kp, t] = ordered[:, t, :]
 
-        def sort_wg(a, first, count):
-            ordered = held([P, count, K_PASSES, P], U32, "wg_sorted%d%d" % (a, first))
+        def sort_wg_second(u):
+            ordered = held([P, PAIR, K_PASSES, P], U32, "wg_sorted1%d" % u)
             nc.scalar.copy(
                 ordered[:].rearrange("p t k (b e) -> p t (k b) e", e=RUN),
-                wg_raw[a][:].bitcast(U32).rearrange("p k (b t e) -> p t (k b) e", t=PACK, e=RUN)[:, first : first + count],
+                wg_second[:].bitcast(U32).rearrange("p k (b t e) -> p t (k b) e", t=PACK, e=RUN)[:, PAIR * u : PAIR * (u + 1)],
             )
-            for t in range(count):
+            for t in range(PAIR):
                 for kp in range(K_PASSES):
-                    wg_sorted[a, kp, first + t] = ordered[:, t, kp, :]
+                    wg_sorted[1, kp, PAIR * u + t] = ordered[:, t, kp, :]
 
         def sort_wu(a):
             wu_sorted[a] = held([P, PACK, K_PASSES, P // 2], U32, "wu_sorted%d" % a)
-            nc.vector.tensor_copy(
-                wu_sorted[a][:].rearrange("p t k (b e) -> p t (k b) e", e=RUN // 2),
-                wu_raw[a][:].bitcast(U32).rearrange("p k (b t e) -> p t (k b) e", t=PACK, e=RUN // 2),
+            nc.scalar.copy(
+                wu_sorted[a][:].rearrange("p t k (b e) -> p t k b e", e=RUN // 2),
+                wu_raw[:, :, a * PASS // 2 : (a + 1) * PASS // 2]
+                .bitcast(U32)
+                .rearrange("p k (b t e) -> p t k b e", t=PACK, e=RUN // 2),
             )
 
-        gather_words(0, 1, None)
+        gather_words(0, 1, 7 * CHUNK)
         for kp in range(K_PASSES):
-            part_first(kp)
-        sort_wg(0, 0, 1)
-        sort_wg(0, 1, 1)
-        sort_wg(0, PAIR, PAIR)
-        sort_wu(0)
-        gather_words(1, 2, "both0")
-        gather_words(LAST, 1, "wu_raw0")
-        part_words(1, 2, "wg_raw0")
+            first_operands(kp)
+        for a in range(HALVES):
+            sort_wu(a)
+        gather_words(1, 2, 0)
+        gather_words(LAST, 1, 8 * CHUNK)
+        part_words(1, 2)
+        part_words(LAST, 1)
         for u in range(PAIR):
-            sort_wg(1, PAIR * u, PAIR)
+            sort_wg_second(u)
 
         relu_g, hid, hid_mx, res, y = {}, {}, {}, {}, {}
 
@@ -217,7 +221,7 @@ def tile_list_gmlpt_relu_resL_kernel(
                 )
 
         def relu_tag(n, u):
-            return "relu%d%d" % (n, u)
+            return ("wu_raw", "wg_second")[u] if n == 0 else "relu%d%d" % (n, u)
 
         def gate(n, u):
             if n < STEPS - 1:
@@ -360,17 +364,14 @@ def tile_list_gmlpt_relu_resL_kernel(
             while len(gated) < PAIR * (n + 1) + min(n, PAIR):
                 gate(*divmod(len(gated), PAIR))
                 gated.append(True)
-            if n == 1:
-                sort_wu(1)
             up_pairs(n)
             if n == STEPS - 2:
                 for s in range(PAIR):
                     up_narrow(n + 1, s)
             if n == 0:
-                picked_last = held([P, CHUNK], U8, "picked_last", relu_tag(n, 0))
+                picked_last = held([P, CHUNK], U8, "picked_last", relu_tag(n, 1))
                 gather_scales(picked_last[:], LAST, 1)
-                move_scales(nc.sync, picked_last[:].bitcast(I32), 3)
-                part_words(LAST, 1, relu_tag(n, 1))
+                move_scales(picked_last[:].bitcast(I32), 3)
             if n == 1:
                 gather_res(LAST - 1, 0, relu_tag(n, 0))
                 gather_res(LAST, 0, relu_tag(n, 1))

@@ -37,6 +37,7 @@ ALIGN = 64
 LIVE = 96
 HID_DEPTH = 3
 MX_DEPTH = 5
+WARM_UPS = 6
 GATE, UP = 0, 1
 STEPS = CHUNKS * HALVES
 
@@ -49,6 +50,7 @@ def tile_list_gmlpt_relu_resL_kernel(
         lists = ctx.enter_context(tc.tile_pool(name="lists", bufs=1))
         keep = ctx.enter_context(tc.tile_pool(name="keep", bufs=1))
         shared = ctx.enter_context(tc.tile_pool(name="shared", bufs=1))
+        early = ctx.enter_context(tc.tile_pool(name="early", bufs=1))
         psum = ctx.enter_context(tc.psum_pool(name="psum", bufs=1))
 
         def held(shape, dtype, name, tag=None):
@@ -84,7 +86,7 @@ def tile_list_gmlpt_relu_resL_kernel(
 
         groups = (
             [("w", GATE, 0), ("t", 0)],
-            [("w", UP, 0), ("w", GATE, 1), ("w", UP, 1)],
+            [("w", UP, 0), ("w", UP, 1), ("w", GATE, 1)],
             [("t", 1), ("t", 2)],
             [("t", LAST)],
         )
@@ -107,32 +109,48 @@ def tile_list_gmlpt_relu_resL_kernel(
             for quad in (0, 2, 1, 3):
                 nc.sync.dma_start(planes[g][32 * quad : 32 * quad + 4, :, :], src[LIVE + 8 * quad : LIVE + 8 * quad + 8, :])
 
-        def sort_scales(g):
-            staged = held([P, ROW * len(groups[g])], I32, "staged%d" % g)
+        def sort_scales(staged, g):
             for member in groups[g]:
                 if member[0] == "w":
                     x, a = member[1:]
                     at = place[member][1]
+                    first = 0 if x == UP else LIVE
                     nc.scalar.copy(
-                        staged[LIVE:P, at : at + ROW].bitcast(U32).rearrange("p (t b e) -> p t b e", t=PACK, e=RUN // 4),
-                        w_scale_raw[x][LIVE:P, ROW * a : ROW * (a + 1)]
+                        staged[first:P, at : at + ROW].bitcast(U32).rearrange("p (t b e) -> p t b e", t=PACK, e=RUN // 4),
+                        w_scale_raw[x][first:P, ROW * a : ROW * (a + 1)]
                         .bitcast(U32)
                         .rearrange("p (b t e) -> p t b e", t=PACK, e=RUN // 4),
                     )
             return staged
 
-        staged = sort_scales(0)
-        picked_first = held([P, CHUNK], U8, "picked_first")
+        nc.vector.memset(w_scale_raw[UP][0:LIVE, :], 0)
+        staged = sort_scales(held([P, ROW * len(groups[0])], I32, "staged_first"), 0)
+        next_bytes = 4 * ROW * len(groups[1])
+        picked_first = early.tile([P, CHUNK], U8, name="picked_first", offset=next_bytes - HALF, align_bytes=ALIGN)
         gather_scales(picked_first[:], 0, 1)
         nc.vector.tensor_copy(staged[LIVE:P, place["t", 0][1] :], picked_first[:].bitcast(I32)[LIVE:P, :])
         move_scales(staged, 0)
         wg_first.append(load_wg_first(1))
         wu_raw = held([P, K_PASSES, R // 2], I32, "wu_raw")
         nc.sync.dma_start(wu_raw[:], wu_words.rearrange("k p c -> p k c").bitcast(I32))
-        move_scales(sort_scales(1), 1)
+        staged = sort_scales(early.tile([P, ROW * len(groups[1])], I32, name="staged_next", offset=0, align_bytes=ALIGN), 1)
+        move_scales(staged, 1)
+
+        idle_bank = next_bank(UP)
+        for i in range(WARM_UPS):
+            nc.tensor.matmul_mx(
+                out=idle_bank[:],
+                lhsT=staged[:, 0 : P // 2].bitcast(FP4X4),
+                lhsT_scale=staged[:].bitcast(U8)[:, 0:P],
+                rhs=staged[:, 0 : CHUNK // 2].bitcast(FP4X4),
+                rhs_scale=staged[:].bitcast(U8)[:, 0:CHUNK],
+                start=(i == 0),
+                stop=(i == WARM_UPS - 1),
+            )
+
         wg_second = held([P, K_PASSES, PASS], I32, "wg_second")
         nc.sync.dma_start(wg_second[:], wg_words[:, :, PASS:, :].rearrange("k p r i -> p k (r i)").bitcast(I32))
-        picked_next = held([P, 2 * CHUNK], U8, "picked_next", "picked_first")
+        picked_next = early.tile([P, 2 * CHUNK], U8, name="picked_next", offset=next_bytes, align_bytes=ALIGN)
         gather_scales(picked_next[:], 1, 2)
 
         res_win = [held([P, T], F32, "res_win%d" % m) for m in range(OUT_TILES)]
@@ -155,8 +173,8 @@ def tile_list_gmlpt_relu_resL_kernel(
         def by_pass(c):
             return both[c][:].bitcast(U16).rearrange("p (j d) -> p d j", d=K_PASSES)
 
-        def part_words(c, count):
-            parted = held([P, K_PASSES, 2 * count * CHUNK], U8, "parted%d" % c)
+        def part_words(c, count, tag=None):
+            parted = held([P, K_PASSES, 2 * count * CHUNK], U8, "parted%d" % c, tag)
             nc.vector.tensor_copy(parted[:].bitcast(U16), by_pass(c))
             for i in range(count):
                 for kp in range(K_PASSES):
@@ -201,7 +219,6 @@ def tile_list_gmlpt_relu_resL_kernel(
         gather_words(1, 2, 0)
         gather_words(LAST, 1, 8 * CHUNK)
         part_words(1, 2)
-        part_words(LAST, 1)
         for u in range(PAIR):
             sort_wg_second(u)
 
@@ -369,6 +386,7 @@ def tile_list_gmlpt_relu_resL_kernel(
                 for s in range(PAIR):
                     up_narrow(n + 1, s)
             if n == 0:
+                part_words(LAST, 1, relu_tag(n, 0))
                 picked_last = held([P, CHUNK], U8, "picked_last", relu_tag(n, 1))
                 gather_scales(picked_last[:], LAST, 1)
                 move_scales(picked_last[:].bitcast(I32), 3)

@@ -37,7 +37,7 @@ ALIGN = 64
 LIVE = 96
 HID_DEPTH = 3
 MX_DEPTH = 5
-WARM_UPS = 6
+WARM_UPS = 5
 GATE, UP = 0, 1
 STEPS = CHUNKS * HALVES
 
@@ -50,7 +50,6 @@ def tile_list_gmlpt_relu_resL_kernel(
         lists = ctx.enter_context(tc.tile_pool(name="lists", bufs=1))
         keep = ctx.enter_context(tc.tile_pool(name="keep", bufs=1))
         shared = ctx.enter_context(tc.tile_pool(name="shared", bufs=1))
-        early = ctx.enter_context(tc.tile_pool(name="early", bufs=1))
         psum = ctx.enter_context(tc.psum_pool(name="psum", bufs=1))
 
         def held(shape, dtype, name, tag=None):
@@ -125,15 +124,14 @@ def tile_list_gmlpt_relu_resL_kernel(
 
         nc.vector.memset(w_scale_raw[UP][0:LIVE, :], 0)
         staged = sort_scales(held([P, ROW * len(groups[0])], I32, "staged_first"), 0)
-        next_bytes = 4 * ROW * len(groups[1])
-        picked_first = early.tile([P, CHUNK], U8, name="picked_first", offset=next_bytes - HALF, align_bytes=ALIGN)
+        picked_first = held([P, CHUNK], U8, "picked_first")
         gather_scales(picked_first[:], 0, 1)
         nc.vector.tensor_copy(staged[LIVE:P, place["t", 0][1] :], picked_first[:].bitcast(I32)[LIVE:P, :])
         move_scales(staged, 0)
         wg_first.append(load_wg_first(1))
         wu_raw = held([P, K_PASSES, R // 2], I32, "wu_raw")
         nc.sync.dma_start(wu_raw[:], wu_words.rearrange("k p c -> p k c").bitcast(I32))
-        staged = sort_scales(early.tile([P, ROW * len(groups[1])], I32, name="staged_next", offset=0, align_bytes=ALIGN), 1)
+        staged = sort_scales(held([P, ROW * len(groups[1])], I32, "staged_next", "picked_first"), 1)
         move_scales(staged, 1)
 
         idle_bank = next_bank(UP)
@@ -150,8 +148,9 @@ def tile_list_gmlpt_relu_resL_kernel(
 
         wg_second = held([P, K_PASSES, PASS], I32, "wg_second")
         nc.sync.dma_start(wg_second[:], wg_words[:, :, PASS:, :].rearrange("k p r i -> p k (r i)").bitcast(I32))
-        picked_next = early.tile([P, 2 * CHUNK], U8, name="picked_next", offset=next_bytes, align_bytes=ALIGN)
-        gather_scales(picked_next[:], 1, 2)
+        picked_next = held([P, 2 * CHUNK], U8, "picked_next")
+        for c in (1, 2):
+            gather_scales(picked_next[:, (c - 1) * CHUNK : c * CHUNK], c, 1)
 
         res_win = [held([P, T], F32, "res_win%d" % m) for m in range(OUT_TILES)]
         move_scales(picked_next[:].bitcast(I32), 2)
@@ -173,17 +172,14 @@ def tile_list_gmlpt_relu_resL_kernel(
         def by_pass(c):
             return both[c][:].bitcast(U16).rearrange("p (j d) -> p d j", d=K_PASSES)
 
-        def part_words(c, count, tag=None):
-            parted = held([P, K_PASSES, 2 * count * CHUNK], U8, "parted%d" % c, tag)
+        def part_words(c, count):
+            parted = held([P, K_PASSES, 2 * count * CHUNK], U8, "parted%d" % c)
             nc.vector.tensor_copy(parted[:].bitcast(U16), by_pass(c))
             for i in range(count):
                 for kp in range(K_PASSES):
                     table[c + i, kp] = parted[:, kp, 2 * i * CHUNK : 2 * (i + 1) * CHUNK]
 
-        def first_operands(kp):
-            parted = held([P, 2 * CHUNK], U8, "parted0%d" % kp)
-            nc.vector.tensor_copy(parted[:].bitcast(U16), by_pass(0)[:, kp, :])
-            table[0, kp] = parted[:]
+        def sort_wg_first(kp):
             ordered = held([P, PACK, P], U32, "wg_sorted0%d" % kp)
             nc.scalar.copy(
                 ordered[:].rearrange("p t (b e) -> p t b e", e=RUN),
@@ -211,14 +207,25 @@ def tile_list_gmlpt_relu_resL_kernel(
                 .rearrange("p k (b t e) -> p t k b e", t=PACK, e=RUN // 2),
             )
 
-        gather_words(0, 1, 7 * CHUNK)
+        halves = [shared.tile([P, HALF], U32, name="both0%d" % h, offset=(7, 12)[h] * CHUNK, align_bytes=ALIGN) for h in range(PAIR)]
+        for h in range(PAIR):
+            half_entries = offsets[:, h * HALF // 16 : (h + 1) * HALF // 16]
+            nc.vector.tensor_copy(halves[h][:], word_win[:].bitcast(U32).indirect(half_entries))
+        parted_first = held([P, K_PASSES, 2 * CHUNK], U8, "parted0")
+        for h in range(PAIR):
+            nc.vector.tensor_copy(
+                parted_first[:].bitcast(U16)[:, :, h * HALF : (h + 1) * HALF],
+                halves[h][:].bitcast(U16).rearrange("p (j d) -> p d j", d=K_PASSES),
+            )
         for kp in range(K_PASSES):
-            first_operands(kp)
+            table[0, kp] = parted_first[:, kp, :]
+            sort_wg_first(kp)
         for a in range(HALVES):
             sort_wu(a)
         gather_words(1, 2, 0)
         gather_words(LAST, 1, 8 * CHUNK)
         part_words(1, 2)
+        part_words(LAST, 1)
         for u in range(PAIR):
             sort_wg_second(u)
 
@@ -386,7 +393,6 @@ def tile_list_gmlpt_relu_resL_kernel(
                 for s in range(PAIR):
                     up_narrow(n + 1, s)
             if n == 0:
-                part_words(LAST, 1, relu_tag(n, 0))
                 picked_last = held([P, CHUNK], U8, "picked_last", relu_tag(n, 1))
                 gather_scales(picked_last[:], LAST, 1)
                 move_scales(picked_last[:].bitcast(I32), 3)

@@ -37,7 +37,7 @@ ALIGN = 64
 LIVE = 96
 HID_DEPTH = 3
 MX_DEPTH = 5
-WARM_UPS = 5
+WARM_UPS = 4
 GATE, UP = 0, 1
 STEPS = CHUNKS * HALVES
 
@@ -259,9 +259,9 @@ def tile_list_gmlpt_relu_resL_kernel(
                 first_products(bank[:], GATE, n, PAIR * u + t, 0, CHUNK)
                 nc.scalar.activation(relu_g[n, u][:, t, :], bank[:], RELU)
 
-        def up_pairs(n):
-            hid[n] = held([P, CHUNK, PACK], BF16, "hid%d" % n, "hid%d" % (n % HID_DEPTH))
-            for h in range(2):
+        def up_pairs(n, halves):
+            hid[n] = held([P, halves * HALF, PACK], BF16, "hid%d" % n, "hid%d" % (n % HID_DEPTH))
+            for h in range(halves):
                 lo, hi = HALF * h, HALF * (h + 1)
                 pairs = held([P, PAIR, HALF, PAIR], BF16, "pairs%d%d" % (n, h), "pairs%d%d" % (n % 2, h))
                 for u in range(PAIR):
@@ -388,10 +388,9 @@ def tile_list_gmlpt_relu_resL_kernel(
             while len(gated) < PAIR * (n + 1) + min(n, PAIR):
                 gate(*divmod(len(gated), PAIR))
                 gated.append(True)
-            up_pairs(n)
+            up_pairs(n, 2)
             if n == STEPS - 2:
-                for s in range(PAIR):
-                    up_narrow(n + 1, s)
+                up_pairs(n + 1, 1)
             if n == 0:
                 picked_last = held([P, CHUNK], U8, "picked_last", relu_tag(n, 1))
                 gather_scales(picked_last[:], LAST, 1)
@@ -422,8 +421,7 @@ def tile_list_gmlpt_relu_resL_kernel(
         finish_from_bank(LAST - 1, 0, GATE)
         last_product(LAST - 1, [1])
         add_res(LAST - 1, 1)
-        for s in range(PAIR):
-            quantise(n, SUB * s, SUB * (s + 1), hid[n, s])
+        quantise(n, 0, HALF, hid[n])
         for s in range(PAIR, PACK):
             up_narrow(n, s)
         for s in range(PAIR, PACK):

@@ -339,9 +339,9 @@ def tile_list_gmlpt_relu_resL_kernel(
         def store(c, m, total):
             nc.sync.dma_start(out[m * P : (m + 1) * P, c * CHUNK : (c + 1) * CHUNK], total[:])
 
-        def last_product(c, tiles):
+        def last_product(c, tiles, kind=GATE):
             for m in tiles:
-                bank = next_bank(GATE)
+                bank = next_bank(kind)
                 down(c, m, 0, CHUNK, bank[:])
                 y[c, m] = held([P, CHUNK], F32, "y%d%d" % (c, m))
                 nc.scalar.copy(y[c, m][:], bank[:])
@@ -360,13 +360,13 @@ def tile_list_gmlpt_relu_resL_kernel(
                 res[c, m] = res[c][:, m, :]
             nc.vector.tensor_copy(res[c, m], res_win[m][:].indirect(entries(c)))
 
-        def add_res(c, m):
-            total = held([P, CHUNK], F32, "total%d%d" % (c, m))
+        def add_res(c, m, tag=None):
+            total = held([P, CHUNK], F32, "total%d%d" % (c, m), tag)
             nc.gpsimd.tensor_tensor(total[:], y[c, m][:], res[c, m], ADD)
             store(c, m, total)
 
-        def finish_from_bank(c, m, kind):
-            bank = next_bank(kind)
+        def finish_from_bank(c, m):
+            bank = next_bank(GATE)
             down(c, m, 0, CHUNK, bank[:])
             total = held([P, CHUNK], F32, "total%d%d" % (c, m))
             nc.vector.tensor_tensor(total[:], bank[:], res[c, m], ADD)
@@ -404,13 +404,15 @@ def tile_list_gmlpt_relu_resL_kernel(
                 gather_res(LAST, 1, None)
                 gather_res(LAST - 1, 1, relu_tag(n, 0))
             if n == 4:
-                finish_from_bank(1, 0, UP)
                 last_product(1, [1])
+                last_product(1, [0], UP)
                 for m in range(OUT_TILES):
                     gather_and_add(0, m, relu_tag(n, m))
             if n == 5:
                 gather_and_add(1, 1, relu_tag(n, 0))
             quantise(n, 0, CHUNK, hid[n])
+            if n == 4:
+                add_res(1, 0, "hid%d" % (n % HID_DEPTH))
             if n in (1, 2):
                 cast_wd(n - 1)
             if n == 2:
@@ -418,7 +420,7 @@ def tile_list_gmlpt_relu_resL_kernel(
             if n == 3:
                 last_product(0, range(OUT_TILES))
         n = STEPS - 1
-        finish_from_bank(LAST - 1, 0, GATE)
+        finish_from_bank(LAST - 1, 0)
         last_product(LAST - 1, [1])
         add_res(LAST - 1, 1)
         quantise(n, 0, HALF, hid[n])

from contextlib import ExitStack

import concourse.mybir as mybir

K, R, N, T, J = 1024, 1024, 256, 4096, 2048
FLOPS = 2 * J * (2 * K * R + R * N)

F32 = mybir.dt.float32
BF16 = mybir.dt.bfloat16
I32 = mybir.dt.int32
U32 = mybir.dt.uint32
U16 = mybir.dt.uint16
U8 = mybir.dt.uint8
FP8X4 = mybir.dt.float8_e4m3fn_x4
FP4X4 = mybir.dt.float4_e2m1fn_x4
MULT = mybir.AluOpType.mult
ADD = mybir.AluOpType.add
RELU = mybir.ActivationFunctionType.Relu

P = 128
PACK = 4
PASS = P * PACK
K_PASSES = K // PASS
HALVES = R // PASS
RUN = 8
CHUNK = 512
CHUNKS = J // CHUNK
LAST = CHUNKS - 1
HALF = CHUNK // 2
SUB = CHUNK // PACK
OUT_TILES = N // P
LINE = 4
PAIR = 2
ROW = PASS // 4
SET = 4
ALIGN = 64
LIVE = 96
HID_DEPTH = 3
MX_DEPTH = 5
WARM_UPS = 4
GATE, UP = 0, 1
STEPS = CHUNKS * HALVES


def tile_list_gmlpt_relu_resL_kernel(
    tc, tab_words, tab_scales, wg_words, wg_scales, wu_words, wu_scales, wd, rT, offs, out
):
    nc = tc.nc
    with ExitStack() as ctx:
        lists = ctx.enter_context(tc.tile_pool(name="lists", bufs=1))
        keep = ctx.enter_context(tc.tile_pool(name="keep", bufs=1))
        shared = ctx.enter_context(tc.tile_pool(name="shared", bufs=1))
        psum = ctx.enter_context(tc.psum_pool(name="psum", bufs=1))

        def held(shape, dtype, name, tag=None):
            return keep.tile(shape, dtype, name=name, tag=tag or name, align_bytes=ALIGN)

        taken = {GATE: [], UP: []}

        def next_bank(kind):
            taken[kind].append(True)
            count = len(taken[kind])
            return psum.tile([P, CHUNK], F32, name="bank%d_%d" % (kind, count), tag="bank%d_%d" % (kind, count % SET))

        offsets = lists.tile([P, J // 16], U16, name="offsets")
        nc.sync.dma_start(offsets[:], offs)

        def entries(c, count=1):
            return offsets[:, c * CHUNK // 16 : (c + count) * CHUNK // 16]

        scale_win = held([P, T // 4], I32, "scale_win")
        nc.sync.dma_start(scale_win[LIVE:P, :], tab_scales.rearrange("a s t -> s a t").bitcast(I32))
        w_scale_raw = [held([P, R // 4], I32, "w_scale_raw%d" % x) for x in (GATE, UP)]
        for x, w_scales in enumerate((wg_scales, wu_scales)):
            nc.scalar.dma_start(w_scale_raw[x][LIVE:P, :], w_scales.rearrange("k s c -> s k c").bitcast(I32))
        word_win = held([P, T], I32, "word_win")
        nc.sync.dma_start(word_win[:], tab_words[0].rearrange("p t b -> p (t b)").bitcast(I32))

        def load_wg_first(kp):
            raw = held([P, PASS], I32, "wg_first%d" % kp)
            nc.sync.dma_start(raw[:], wg_words[kp, :, 0:PASS, :].rearrange("p r i -> p (r i)").bitcast(I32))
            return raw

        wg_first = [load_wg_first(0)]

        groups = (
            [("w", GATE, 0), ("t", 0)],
            [("w", UP, 0), ("w", UP, 1), ("w", GATE, 1)],
            [("t", 1), ("t", 2)],
            [("t", LAST)],
        )
        nc.vector.memset(scale_win[0:LIVE, :], 0)
        planes, place = [], {}
        for g, members in enumerate(groups):
            planes.append(held([P, K_PASSES, ROW * len(members)], I32, "planes%d" % g))
            nc.vector.memset(planes[g][:], 0)
            for i, member in enumerate(members):
                place[member] = (g, ROW * i)

        def plane(member, kp, lo, hi):
            g, at = place[member]
            return planes[g][:, kp, at : at + ROW].bitcast(U8)[:, lo:hi]

        def gather_scales(picked, c, count):
            nc.vector.tensor_copy(picked, scale_win[:].bitcast(U8).indirect(entries(c, count)))

        def move_scales(src, g):
            for quad in (0, 2, 1, 3):
                nc.sync.dma_start(planes[g][32 * quad : 32 * quad + 4, :, :], src[LIVE + 8 * quad : LIVE + 8 * quad + 8, :])

        def sort_scales(staged, g):
            for member in groups[g]:
                if member[0] == "w":
                    x, a = member[1:]
                    at = place[member][1]
                    first = 0 if x == UP else LIVE
                    nc.scalar.copy(
                        staged[first:P, at : at + ROW].bitcast(U32).rearrange("p (t b e) -> p t b e", t=PACK, e=RUN // 4),
                        w_scale_raw[x][first:P, ROW * a : ROW * (a + 1)]
                        .bitcast(U32)
                        .rearrange("p (b t e) -> p t b e", t=PACK, e=RUN // 4),
                    )
            return staged

        nc.vector.memset(w_scale_raw[UP][0:LIVE, :], 0)
        staged = sort_scales(held([P, ROW * len(groups[0])], I32, "staged_first"), 0)
        picked_first = held([P, CHUNK], U8, "picked_first")
        gather_scales(picked_first[:], 0, 1)
        nc.vector.tensor_copy(staged[LIVE:P, place["t", 0][1] :], picked_first[:].bitcast(I32)[LIVE:P, :])
        move_scales(staged, 0)
        wg_first.append(load_wg_first(1))
        wu_raw = held([P, K_PASSES, R // 2], I32, "wu_raw")
        nc.sync.dma_start(wu_raw[:], wu_words.rearrange("k p c -> p k c").bitcast(I32))
        staged = sort_scales(held([P, ROW * len(groups[1])], I32, "staged_next", "picked_first"), 1)
        move_scales(staged, 1)

        idle_bank = next_bank(UP)
        for i in range(WARM_UPS):
            nc.tensor.matmul_mx(
                out=idle_bank[:],
                lhsT=staged[:, 0 : P // 2].bitcast(FP4X4),
                lhsT_scale=staged[:].bitcast(U8)[:, 0:P],
                rhs=staged[:, 0 : CHUNK // 2].bitcast(FP4X4),
                rhs_scale=staged[:].bitcast(U8)[:, 0:CHUNK],
                start=(i == 0),
                stop=(i == WARM_UPS - 1),
            )

        wg_second = held([P, K_PASSES, PASS], I32, "wg_second")
        nc.sync.dma_start(wg_second[:], wg_words[:, :, PASS:, :].rearrange("k p r i -> p k (r i)").bitcast(I32))
        picked_next = held([P, 2 * CHUNK], U8, "picked_next")
        for c in (1, 2):
            gather_scales(picked_next[:, (c - 1) * CHUNK : c * CHUNK], c, 1)

        res_win = [held([P, T], F32, "res_win%d" % m) for m in range(OUT_TILES)]
        move_scales(picked_next[:].bitcast(I32), 2)
        nc.sync.dma_start(res_win[0][:], rT[0:P, :])
        wd_raw = [held([P, PACK, N], F32, "wd_raw%d" % a) for a in range(HALVES)]
        wd_rows = wd.rearrange("(a b t q) n -> a t b q n", a=HALVES, t=PACK, q=RUN)
        for a in range(HALVES):
            for t in range(PACK):
                nc.sync.dma_start(wd_raw[a][:, t, :], wd_rows[a, t])

        nc.sync.dma_start(res_win[1][:], rT[P : 2 * P, :])

        both, table, wg_sorted, wu_sorted = {}, {}, {}, {}

        def gather_words(c, count, offset):
            both[c] = shared.tile([P, count * CHUNK], U32, name="both%d" % c, offset=offset, align_bytes=ALIGN)
            nc.vector.tensor_copy(both[c][:], word_win[:].bitcast(U32).indirect(entries(c, count)))

        def by_pass(c):
            return both[c][:].bitcast(U16).rearrange("p (j d) -> p d j", d=K_PASSES)

        def part_words(c, count):
            parted = held([P, K_PASSES, 2 * count * CHUNK], U8, "parted%d" % c)
            nc.vector.tensor_copy(parted[:].bitcast(U16), by_pass(c))
            for i in range(count):
                for kp in range(K_PASSES):
                    table[c + i, kp] = parted[:, kp, 2 * i * CHUNK : 2 * (i + 1) * CHUNK]

        def sort_wg_first(kp):
            ordered = held([P, PACK, P], U32, "wg_sorted0%d" % kp)
            nc.scalar.copy(
                ordered[:].rearrange("p t (b e) -> p t b e", e=RUN),
                wg_first[kp][:].bitcast(U32).rearrange("p (b t e) -> p t b e", t=PACK, e=RUN),
            )
            for t in range(PACK):
                wg_sorted[0, kp, t] = ordered[:, t, :]

        def sort_wg_second(u):
            ordered = held([P, PAIR, K_PASSES, P], U32, "wg_sorted1%d" % u)
            nc.scalar.copy(
                ordered[:].rearrange("p t k (b e) -> p t (k b) e", e=RUN),
                wg_second[:].bitcast(U32).rearrange("p k (b t e) -> p t (k b) e", t=PACK, e=RUN)[:, PAIR * u : PAIR * (u + 1)],
            )
            for t in range(PAIR):
                for kp in range(K_PASSES):
                    wg_sorted[1, kp, PAIR * u + t] = ordered[:, t, kp, :]

        def sort_wu(a):
            wu_sorted[a] = held([P, PACK, K_PASSES, P // 2], U32, "wu_sorted%d" % a)
            nc.scalar.copy(
                wu_sorted[a][:].rearrange("p t k (b e) -> p t k b e", e=RUN // 2),
                wu_raw[:, :, a * PASS // 2 : (a + 1) * PASS // 2]
                .bitcast(U32)
                .rearrange("p k (b t e) -> p t k b e", t=PACK, e=RUN // 2),
            )

        halves = [shared.tile([P, HALF], U32, name="both0%d" % h, offset=(7, 12)[h] * CHUNK, align_bytes=ALIGN) for h in range(PAIR)]
        for h in range(PAIR):
            half_entries = offsets[:, h * HALF // 16 : (h + 1) * HALF // 16]
            nc.vector.tensor_copy(halves[h][:], word_win[:].bitcast(U32).indirect(half_entries))
        parted_first = held([P, K_PASSES, 2 * CHUNK], U8, "parted0")
        for h in range(PAIR):
            nc.vector.tensor_copy(
                parted_first[:].bitcast(U16)[:, :, h * HALF : (h + 1) * HALF],
                halves[h][:].bitcast(U16).rearrange("p (j d) -> p d j", d=K_PASSES),
            )
        for kp in range(K_PASSES):
            table[0, kp] = parted_first[:, kp, :]
            sort_wg_first(kp)
        for a in range(HALVES):
            sort_wu(a)
        gather_words(1, 2, 0)
        gather_words(LAST, 1, 8 * CHUNK)
        part_words(1, 2)
        part_words(LAST, 1)
        for u in range(PAIR):
            sort_wg_second(u)

        relu_g, hid, hid_mx, res, y = {}, {}, {}, {}, {}

        def first_products(acc, x, n, t, lo, hi):
            c, a = divmod(n, HALVES)
            for kp in range(K_PASSES):
                nc.tensor.matmul_mx(
                    out=acc,
                    lhsT=wg_sorted[a, kp, t].bitcast(FP8X4) if x == GATE else wu_sorted[a][:, t, kp, :].bitcast(FP4X4),
                    lhsT_scale=plane(("w", x, a), kp, P * t, P * (t + 1)),
                    rhs=table[c, kp][:, 2 * lo : 2 * hi].bitcast(FP4X4),
                    rhs_scale=plane(("t", c), kp, lo, hi),
                    start=(kp == 0),
                    stop=(kp == K_PASSES - 1),
                )

        def relu_tag(n, u):
            return ("wu_raw", "wg_second")[u] if n == 0 else "relu%d%d" % (n, u)

        def gate(n, u):
            if n < STEPS - 1:
                relu_g[n, u] = held([P, PAIR, CHUNK], F32, "relu_g%d%d" % (n, u), relu_tag(n, u))[:]
            else:
                if u == 0:
                    relu_g[n] = held([P, PACK, CHUNK], F32, "relu_g%d" % n, "word_win")
                relu_g[n, u] = relu_g[n][:, PAIR * u : PAIR * (u + 1), :]
            for t in range(PAIR):
                bank = next_bank(GATE)
                first_products(bank[:], GATE, n, PAIR * u + t, 0, CHUNK)
                nc.scalar.activation(relu_g[n, u][:, t, :], bank[:], RELU)

        def up_pairs(n, halves):
            hid[n] = held([P, halves * HALF, PACK], BF16, "hid%d" % n, "hid%d" % (n % HID_DEPTH))
            for h in range(halves):
                lo, hi = HALF * h, HALF * (h + 1)
                pairs = held([P, PAIR, HALF, PAIR], BF16, "pairs%d%d" % (n, h), "pairs%d%d" % (n % 2, h))
                for u in range(PAIR):
                    bank = next_bank(UP)
                    places = bank[:].rearrange("p (t j) -> p t j", t=PAIR)
                    for t in range(PAIR):
                        first_products(places[:, t, :], UP, n, PAIR * u + t, lo, hi)
                    nc.vector.tensor_tensor(
                        pairs[:, u].rearrange("p (g i) t -> p g t i", i=PAIR),
                        places.rearrange("p t (g i) -> p g t i", i=PAIR),
                        relu_g[n, u][:, :, lo:hi].rearrange("p t (g i) -> p g t i", i=PAIR),
                        MULT,
                    )
                words = hid[n][:, lo:hi, :].rearrange("p j t -> p (j t)").bitcast(U32)
                nc.scalar.copy(
                    words.rearrange("p (j u) -> p j u", u=PAIR),
                    pairs[:].rearrange("p u j t -> p u (j t)").bitcast(U32).rearrange("p u j -> p j u"),
                )

        def up_narrow(n, s):
            lo, hi = SUB * s, SUB * (s + 1)
            bank = next_bank(UP)
            places = bank[:].rearrange("p (t j) -> p t j", t=PACK)
            for t in range(PACK):
                first_products(places[:, t, :], UP, n, t, lo, hi)
            hid[n, s] = held([P, SUB, PACK], BF16, "hid%d%d" % (n, s))
            nc.vector.tensor_tensor(
                hid[n, s][:].rearrange("p (g i) t -> p g t i", i=PAIR),
                places.rearrange("p t (g i) -> p g t i", i=PAIR),
                relu_g[n][:, :, lo:hi].rearrange("p t (g i) -> p g t i", i=PAIR),
                MULT,
            )

        wd_codes = held([P, HALVES, N], U32, "wd_codes")
        wd_scales = held([P, HALVES, N], U8, "wd_scales")

        wd_bf = held([P, HALVES, N, PACK], BF16, "wd_bf")

        def cast_wd(a):
            nc.scalar.copy(
                wd_bf[:, a].rearrange("p (g i) t -> p g t i", i=LINE),
                wd_raw[a][:].rearrange("p t (g i) -> p g t i", i=LINE),
            )

        def quantise_wd():
            nc.vector.quantize_mx(
                out=wd_codes[:].rearrange("p a n -> p (a n)").bitcast(FP8X4),
                scales=wd_scales[:].rearrange("p a n -> p (a n)"),
                in_=wd_bf[:].rearrange("p a n t -> p (a n t)"),
            )

        def quantise(n, lo, hi, values):
            if lo == 0:
                codes = held([P, CHUNK], U32, "codes%d" % n, "codes%d" % (n % MX_DEPTH))
                scales = held([P, CHUNK], U8, "scales%d" % n, "scales%d" % (n % MX_DEPTH))
                hid_mx[n] = (codes, scales)
            codes, scales = hid_mx[n]
            nc.vector.quantize_mx(
                out=codes[:, lo:hi].bitcast(FP8X4), scales=scales[:, lo:hi], in_=values[:].rearrange("p j t -> p (j t)")
            )

        def down(c, m, lo, hi, acc):
            for a in range(HALVES):
                codes, scales = hid_mx[HALVES * c + a]
                nc.tensor.matmul_mx(
                    out=acc,
                    lhsT=wd_codes[:, a, m * P : (m + 1) * P].bitcast(FP8X4),
                    lhsT_scale=wd_scales[:, a, m * P : (m + 1) * P],
                    rhs=codes[:, lo:hi].bitcast(FP8X4),
                    rhs_scale=scales[:, lo:hi],
                    start=(a == 0),
                    stop=(a == HALVES - 1),
                )

        def store(c, m, total):
            nc.sync.dma_start(out[m * P : (m + 1) * P, c * CHUNK : (c + 1) * CHUNK], total[:])

        def last_product(c, tiles, kind=GATE):
            for m in tiles:
                bank = next_bank(kind)
                down(c, m, 0, CHUNK, bank[:])
                y[c, m] = held([P, CHUNK], F32, "y%d%d" % (c, m))
                nc.scalar.copy(y[c, m][:], bank[:])

        def gather_and_add(c, m, tag=None):
            total = held([P, CHUNK], F32, "total%d%d" % (c, m), tag)
            nc.vector.tensor_tensor(total[:], res_win[m][:].indirect(entries(c)), y[c, m][:], ADD)
            store(c, m, total)

        def gather_res(c, m, tag):
            if c < LAST:
                res[c, m] = held([P, CHUNK], F32, "res%d%d" % (c, m), tag)[:]
            else:
                if m == 0:
                    res[c] = held([P, OUT_TILES, CHUNK], F32, "res%d" % c, tag)
                res[c, m] = res[c][:, m, :]
            nc.vector.tensor_copy(res[c, m], res_win[m][:].indirect(entries(c)))

        def add_res(c, m, tag=None):
            total = held([P, CHUNK], F32, "total%d%d" % (c, m), tag)
            nc.gpsimd.tensor_tensor(total[:], y[c, m][:], res[c, m], ADD)
            store(c, m, total)

        def finish_from_bank(c, m):
            bank = next_bank(GATE)
            down(c, m, 0, CHUNK, bank[:])
            total = held([P, CHUNK], F32, "total%d%d" % (c, m))
            nc.vector.tensor_tensor(total[:], bank[:], res[c, m], ADD)
            store(c, m, total)

        def finish_last(lo, hi):
            bank = next_bank(GATE)
            acc = bank[:, 0 : OUT_TILES * (hi - lo)].rearrange("p (m j) -> p m j", m=OUT_TILES)
            for m in range(OUT_TILES):
                down(LAST, m, lo, hi, acc[:, m, :])
            last = held([P, OUT_TILES, hi - lo], F32, "total_last%d" % lo)
            nc.vector.tensor_tensor(last[:], acc, res[LAST][:, :, lo:hi], ADD)
            nc.sync.dma_start(
                out.rearrange("(m p) j -> p m j", p=P)[:, :, LAST * CHUNK + lo : LAST * CHUNK + hi], last[:]
            )

        gated = []
        for n in range(STEPS - 1):
            while len(gated) < PAIR * (n + 1) + min(n, PAIR):
                gate(*divmod(len(gated), PAIR))
                gated.append(True)
            up_pairs(n, 2)
            if n == STEPS - 2:
                up_pairs(n + 1, 1)
            if n == 0:
                picked_last = held([P, CHUNK], U8, "picked_last", relu_tag(n, 1))
                gather_scales(picked_last[:], LAST, 1)
                move_scales(picked_last[:].bitcast(I32), 3)
            if n == 1:
                gather_res(LAST - 1, 0, relu_tag(n, 0))
                gather_res(LAST, 0, relu_tag(n, 1))
            if n == 2:
                gather_res(1, 0, relu_tag(n, 0))
            if n == 3:
                gather_res(LAST, 1, None)
                gather_res(LAST - 1, 1, relu_tag(n, 0))
            if n == 4:
                last_product(1, [1])
                last_product(1, [0], UP)
                for m in range(OUT_TILES):
                    gather_and_add(0, m, relu_tag(n, m))
            if n == 5:
                gather_and_add(1, 1, relu_tag(n, 0))
            quantise(n, 0, CHUNK, hid[n])
            if n == 4:
                add_res(1, 0, "hid%d" % (n % HID_DEPTH))
            if n in (1, 2):
                cast_wd(n - 1)
            if n == 2:
                quantise_wd()
            if n == 3:
                last_product(0, range(OUT_TILES))
        n = STEPS - 1
        finish_from_bank(LAST - 1, 0)
        last_product(LAST - 1, [1])
        add_res(LAST - 1, 1)
        quantise(n, 0, HALF, hid[n])
        for s in range(PAIR, PACK):
            up_narrow(n, s)
        for s in range(PAIR, PACK):
            quantise(n, SUB * s, SUB * (s + 1), hid[n, s])
        for s in range(PACK):
            finish_last(SUB * s, SUB * (s + 1))
